import numpy as np
import ml_dtypes


def mxq(x, axis, fmt="e4m3"):
    dtype, down = {"e4m3": (ml_dtypes.float8_e4m3fn, 7), "e5m2": (ml_dtypes.float8_e5m2, 14)}[fmt]
    v = np.moveaxis(np.asarray(x, np.float32).astype(ml_dtypes.bfloat16).astype(np.float64), axis, -1)
    blocks = v.reshape(v.shape[:-1] + (-1, 32))
    amax = np.abs(blocks).max(-1, keepdims=True)
    byte = np.maximum(np.where(amax > 0, np.frexp(amax)[1] - 1 + 127, 0) - down, 1)
    scale = np.exp2(byte - 127.0)
    codes = (blocks / scale).astype(np.float32).astype(dtype).astype(np.float64)
    return np.moveaxis((codes * scale).reshape(v.shape), -1, axis)


WIDE = False


def mx_kscale(k):
    if not WIDE:
        return np.ones(k)
    levels = np.array([24, -24, 12, -12, 0])
    if k % 512:
        return np.exp2(np.random.permutation(np.resize(levels, k // 32))).repeat(32)
    a = np.empty((k // 512, 16))
    for p in range(k // 512):
        a[p, :8] = np.random.permutation(np.resize(levels, 8))
        for g in range(8):
            far = levels[np.abs(levels - a[p, g]) >= 10]
            a[p, g + 8] = far[np.random.randint(len(far))]
    return np.exp2(a.ravel()).repeat(32)


def f64(x):
    return np.asarray(x).astype(np.float64)


def striped(idx):
    return np.tile(idx.reshape(-1, 16).T, (8, 1)).astype(np.uint16)


def unstriped(offs):
    return offs[:16].T.reshape(-1).astype(np.int64)


E2M1 = np.array([0.0, 0.5, 1.0, 1.5, 2.0, 3.0, 4.0, 6.0, -0.0, -0.5, -1.0, -1.5, -2.0, -3.0, -4.0, -6.0])


def pack_weight(w, fmt):
    k, n = w.shape
    w = f64(np.asarray(w, np.float32).astype(ml_dtypes.bfloat16)).reshape(k // 32, 32, n)
    amax = np.abs(w).max(1)
    if fmt == "e4m3":
        byte = np.frexp(amax)[1] - 1 + 127 - 7
    else:
        mant, ex = np.frexp(amax / 6.0)
        byte = np.where(mant > 0.5, ex, ex - 1) + 127
    byte = np.clip(np.where(amax > 0, byte, 1), 1, 254)
    scaled = (w * np.exp2(127.0 - byte)[:, None, :]).reshape(k, n).astype(np.float32)
    by_word = np.ascontiguousarray(scaled.reshape(k // 512, 128, 4, n).transpose(0, 1, 3, 2))
    if fmt == "e4m3":
        words = by_word.astype(ml_dtypes.float8_e4m3fn).view(np.uint8)
    else:
        c = by_word.astype(ml_dtypes.float4_e2m1fn).view(np.uint8) & 0xF
        words = (c[..., 0::2] | (c[..., 1::2] << 4)).reshape(k // 512, 128, 2 * n)
    return np.ascontiguousarray(words), np.ascontiguousarray(byte.astype(np.uint8).reshape(k // 512, 16, n))


def unpack_weight(words, scales, fmt):
    g, _, n = scales.shape
    words = np.ascontiguousarray(words).reshape(g, 128, n, -1)
    if fmt == "e4m3":
        vals = words.view(ml_dtypes.float8_e4m3fn).astype(np.float64)
    else:
        nib = np.empty((g, 128, n, 4), np.uint8)
        nib[..., 0::2] = words & 0xF
        nib[..., 1::2] = words >> 4
        vals = E2M1[nib]
    vals = vals * np.repeat(np.exp2(scales.astype(np.float64) - 127.0), 8, axis=1)[..., None]
    return vals.transpose(0, 1, 3, 2).reshape(g * 512, n)


def pack_table4(v):
    words, scales = pack_weight(v, "e2m1")
    g, t = words.shape[0] // 2, v.shape[1]
    return np.ascontiguousarray(words.reshape(g, 2, 128, t, 2).transpose(0, 2, 3, 1, 4).reshape(g, 128, t, 4)), scales


def unpack_table4(words, scales):
    g, _, t, _ = words.shape
    return unpack_weight(words.reshape(g, 128, t, 2, 2).transpose(0, 3, 1, 2, 4).reshape(2 * g, 128, 2 * t), scales, "e2m1")


K, R, N, T, J = 1024, 512, 512, 2048, 1024


def setup_inputs():
    n = np.random.standard_normal
    s = mx_kscale(K)[:, None]
    u = mx_kscale(R)[:, None]
    p_tab = pack_table4(n((K, T)) * s)
    p_ws = pack_weight(n((K, R)) / np.sqrt(2 * K) / s, "e2m1")
    p_wt = pack_weight(n((K, R)) / np.sqrt(2 * K) / s, "e4m3")
    p_wd = pack_weight(n((R, N)) / np.sqrt(R) / u, "e2m1")
    return {
        "tab_words": p_tab[0],
        "tab_scales": p_tab[1],
        "ws_words": p_ws[0],
        "ws_scales": p_ws[1],
        "wt_words": p_wt[0],
        "wt_scales": p_wt[1],
        "sm": (np.random.uniform(0.5, 2.0, R) * u[:, 0]).astype(np.float32),
        "wd_words": p_wd[0],
        "wd_scales": p_wd[1],
        "gT": (n((N, T))).astype(np.float32),
        "wgo": np.tile(np.random.uniform(0.5, 2.0, J), (128, 1)).astype(np.float32),
        "offs": striped(np.random.permutation(T)[:J]),
        "offs2": striped(np.random.permutation(T)[:J]),
    }


def reference(tab_words, tab_scales, ws_words, ws_scales, wt_words, wt_scales, sm, wd_words, wd_scales, gT, wgo, offs, offs2):
    idx = unstriped(offs)
    idx2 = unstriped(offs2)
    tab_ = unpack_table4(tab_words, tab_scales)[:, idx]
    tabb_ = unpack_table4(tab_words, tab_scales)[:, idx2]
    ws_ = unpack_weight(ws_words, ws_scales, "e2m1")
    wt_ = unpack_weight(wt_words, wt_scales, "e4m3")
    a = ws_.T @ tab_ + wt_.T @ tabb_
    h = f64(sm)[:, None] * np.tanh(a)
    h_ = mxq(h, 0, "e4m3")
    wd_ = unpack_weight(wd_words, wd_scales, "e2m1")
    y = wd_.T @ h_
    out = np.zeros((N, T))
    out[:, idx2] = f64(wgo)[0] * (y * f64(gT)[:, idx])
    return out

@@ -1,0 +1,230 @@
+from contextlib import ExitStack
+
+import concourse.mybir as mybir
+from concourse.masks import make_identity
+
+K, R, N, T, J = 1024, 512, 512, 2048, 1024
+FLOPS = 2 * J * (2 * K * R + R * N)
+
+F32 = mybir.dt.float32
+BF16 = mybir.dt.bfloat16
+I32 = mybir.dt.int32
+U32 = mybir.dt.uint32
+U16 = mybir.dt.uint16
+U8 = mybir.dt.uint8
+FP8X4 = mybir.dt.float8_e4m3fn_x4
+FP4X4 = mybir.dt.float4_e2m1fn_x4
+ACT = mybir.ActivationFunctionType
+MULT = mybir.AluOpType.mult
+
+P = 128
+CH = 256
+NCH = J // CH
+HALF = J // 2
+
+
+def tile_list_msg_tanh_gate_kernel(
+    tc, tab_words, tab_scales, ws_words, ws_scales, wt_words, wt_scales, sm, wd_words, wd_scales, gT, wgo, offs, offs2, out
+):
+    nc = tc.nc
+    with ExitStack() as ctx:
+        keep = ctx.enter_context(tc.tile_pool(name="keep", bufs=1))
+        ring = ctx.enter_context(tc.tile_pool(name="ring", bufs=2))
+        psum = ctx.enter_context(tc.psum_pool(name="psum", bufs=2))
+
+        src_list = keep.tile([P, J // 16], U16, name="src_list")
+        dst_list = keep.tile([P, J // 16], U16, name="dst_list")
+        lists = (src_list, dst_list)
+        tabw = keep.tile([P, T], I32, name="tabw", align_bytes=64)
+        tabs = keep.tile([P, T], U8, name="tabs", tag="late_b", align_bytes=64)
+        wsw = keep.tile([P, 2, 2 * R], U8, name="wsw", align_bytes=64)
+        wdw = keep.tile([P, 2 * N], U8, name="wdw", align_bytes=64)
+        wss = keep.tile([P, 2, R], U8, name="wss", align_bytes=64)
+        wts = keep.tile([P, 2, R], U8, name="wts", align_bytes=64)
+        wds = keep.tile([P, N], U8, name="wds", align_bytes=64)
+        sm_t = keep.tile([P, 4], F32, name="sm_t")
+        wrow = keep.tile([P, P], F32, name="wrow")
+        wcol = keep.tile([P, J // P], F32, name="wcol")
+        ident = keep.tile([P, P], F32, name="ident")
+        gs0 = [keep.tile([P, 2, HALF], U8, name=f"gs0_{h}", align_bytes=64) for h in range(2)]
+        gs1 = [keep.tile([P, 2, HALF], U8, name=f"gs1_{h}", align_bytes=64) for h in range(2)]
+        gw = [keep.tile([P, 2, CH], I32, name=f"gw{c}", tag=("late_a" if c == 0 else f"gw{c}"), align_bytes=64) for c in range(NCH)]
+        vw = [keep.tile([P, 2, 2 * 2 * CH], U8, name=f"vw{c}", align_bytes=64) for c in range(NCH)]
+        gg = [keep.tile([P, J], F32, name=f"gg{n}") for n in range(4)]
+        win = [keep.tile([P, T], F32, name=f"win{n}") for n in range(4)]
+        ysb = keep.tile([P, 4, J], F32, name="ysb")
+
+        nc.gpsimd.memset(tabs[:].bitcast(I32), 0)
+        nc.gpsimd.memset(wts[:].rearrange("p a n -> p (a n)").bitcast(I32), 0)
+        make_identity(nc, ident[:])
+        nc.vector.memset(wss[:].rearrange("p a n -> p (a n)").bitcast(I32), 0)
+        nc.vector.memset(wds[:].bitcast(I32), 0)
+        nc.vector.memset(wrow[:], 0.0)
+        for h in range(2):
+            nc.vector.memset(gs1[h][:].rearrange("p a n -> p (a n)").bitcast(I32), 0)
+        warm = keep.tile([P, 1], F32, name="warm", tag="wt_slot", align_bytes=64)
+        nc.scalar.activation(warm[:], ident[:, 0:1], ACT.Tanh)
+
+        nc.sync.dma_start(src_list[:], offs)
+        nc.sync.dma_start(dst_list[:], offs2)
+        nc.sync.dma_start(out=tabw[:], in_=tab_words[0].rearrange("p t b -> p (t b)").bitcast(I32))
+        for q in range(4):
+            nc.sync.dma_start(out=tabs[32 * q : 32 * q + 8, :].bitcast(I32), in_=tab_scales[:, 4 * q : 4 * q + 4, :].bitcast(I32))
+        nc.sync.dma_start(out=wsw[:].bitcast(I32), in_=ws_words.rearrange("a p n -> p a n").bitcast(I32))
+        wtw = keep.tile([P, 2, R], I32, name="wtw", tag="wt_slot", align_bytes=64)
+        nc.sync.dma_start(out=wtw[:], in_=wt_words.rearrange("a p n b -> p a (n b)").bitcast(I32))
+        for plane, rows, queue in ((wss, ws_scales, nc.sync), (wts, wt_scales, nc.gpsimd)):
+            for q in range(4):
+                queue.dma_start(
+                    out=plane[32 * q : 32 * q + 4, :, :].bitcast(I32),
+                    in_=rows[:, 4 * q : 4 * q + 4, :].rearrange("a r n -> r a n").bitcast(I32),
+                )
+        nc.gpsimd.dma_start(out=sm_t[:], in_=sm.rearrange("(p t) -> p t", t=4))
+        nc.gpsimd.dma_start(out=wrow[0 : J // P, :], in_=wgo[0].rearrange("(c p) -> c p", p=P))
+        nc.gpsimd.dma_start(out=wdw[:].bitcast(I32), in_=wd_words[0].bitcast(I32))
+        for q in range(4):
+            nc.gpsimd.dma_start(out=wds[32 * q : 32 * q + 4, :].bitcast(I32), in_=wd_scales[0, 4 * q : 4 * q + 4, :].bitcast(I32))
+        for n in range(4):
+            (nc.vector if n < 2 else nc.gpsimd).memset(win[n][:], 0.0)
+
+        def entries(lst, j0, count):
+            return lst[:, j0 // 16 : (j0 + count) // 16]
+
+        def gather_scales(h):
+            for l in range(2):
+                nc.vector.tensor_copy(gs0[h][:, l, :], tabs[:].indirect(entries(lists[l], h * HALF, HALF)))
+            nc.sync.dma_start(
+                out=gs1[h][0:112, :, :].rearrange("p a n -> p (a n)").bitcast(I32),
+                in_=gs0[h][4:116, :, :].rearrange("p a n -> p (a n)").bitcast(I32),
+            )
+
+        def gather_words(c):
+            for l in range(2):
+                nc.vector.tensor_copy(gw[c][:, l, :].bitcast(U32), tabw[:].bitcast(U32).indirect(entries(lists[l], c * CH, CH)))
+
+        def part_words(c):
+            nc.vector.tensor_copy(
+                vw[c][:].bitcast(U16),
+                gw[c][:].rearrange("p l j -> p (l j)").bitcast(U16).rearrange("p (j a) -> p a j", a=2),
+            )
+
+        def load_gates(pair, tag):
+            gates = keep.tile([P, 2, T], F32, name=f"gates{pair}", tag=tag, align_bytes=64)
+            for nn in range(2):
+                n = 2 * pair + nn
+                nc.sync.dma_start(out=gates[:, nn, :], in_=gT[n * P : (n + 1) * P, :])
+            return gates
+
+        def gather_gates(gates, n):
+            nc.vector.tensor_copy(gg[n][:], gates[:, n % 2, :].indirect(src_list[:]))
+
+        def stage1(c):
+            h, base = divmod(c * CH, HALF)
+            th = ring.tile([P, CH // P, 4, P], F32, name="th")
+            for u in range(CH // P):
+                acc = psum.tile([P, R], F32, name="acc")
+                for a in range(2):
+                    plane = (gs0, gs1)[a][h]
+                    for l in range(2):
+                        j0 = l * CH + u * P
+                        if l == 0:
+                            w = wsw[:, a, :].bitcast(FP4X4)
+                        else:
+                            w = wtw[:, a, :].bitcast(FP8X4)
+                        nc.tensor.matmul_mx(
+                            out=acc[:],
+                            lhsT=vw[c][:, a, 2 * j0 : 2 * (j0 + P)].bitcast(FP4X4),
+                            lhsT_scale=plane[:, l, base + u * P : base + (u + 1) * P],
+                            rhs=w,
+                            rhs_scale=(wss, wts)[l][:, a, :],
+                            start=(a == 0 and l == 0),
+                            stop=(a == 1 and l == 1),
+                        )
+                nc.scalar.activation(th[:, u, :, :], acc[:].rearrange("p (m t) -> p t m", t=4), ACT.Tanh)
+            hb = ring.tile([P, 4, CH], BF16, name="hb")
+            for pair in range(2):
+                ht = psum.tile([P, 2, CH], F32, name="ht")
+                for tt in range(2):
+                    for u in range(CH // P):
+                        nc.tensor.transpose(ht[:, tt, u * P : (u + 1) * P], th[:, u, 2 * pair + tt, :], ident[:])
+                for tt in range(2):
+                    t = 2 * pair + tt
+                    nc.scalar.activation(hb[:, t, :], ht[:, tt, :], ACT.Copy, scale=sm_t[:, t : t + 1])
+            hi = ring.tile([P, CH, 4], BF16, name="hi", align_bytes=64)
+            nc.scalar.copy(hi[:].rearrange("p (c i) t -> p c t i", i=4), hb[:].rearrange("p t (c i) -> p c t i", i=4))
+            return hi
+
+        def quantise(hi):
+            hq = ring.tile([P, CH], U32, name="hq", align_bytes=64)
+            hs = ring.tile([P, CH], U8, name="hs", align_bytes=64)
+            nc.vector.quantize_mx(out=hq[:].bitcast(FP8X4), scales=hs[:], in_=hi[:].rearrange("p j t -> p (j t)"))
+            return hq, hs
+
+        def stage2(c, hq, hs):
+            yw = ring.tile([P, CH // P, N], F32, name="yw")
+            for u in range(CH // P):
+                yt = psum.tile([P, N], F32, name="yt")
+                nc.tensor.matmul_mx(
+                    out=yt[:],
+                    lhsT=hq[:, u * P : (u + 1) * P].bitcast(FP8X4),
+                    lhsT_scale=hs[:, u * P : (u + 1) * P],
+                    rhs=wdw[:].bitcast(FP4X4),
+                    rhs_scale=wds[:],
+                    start=True,
+                    stop=True,
+                )
+                col = c * (CH // P) + u
+                nc.scalar.activation(yw[:, u, :], yt[:], ACT.Copy, scale=wcol[:, col : col + 1])
+            for pair in range(2):
+                yb = psum.tile([P, 2, CH], F32, name="yb")
+                for nn in range(2):
+                    n = 2 * pair + nn
+                    for u in range(CH // P):
+                        nc.tensor.transpose(yb[:, nn, u * P : (u + 1) * P], yw[:, u, n * P : (n + 1) * P], ident[:])
+                nc.scalar.copy(ysb[:, 2 * pair : 2 * pair + 2, c * CH : (c + 1) * CH], yb[:])
+
+        def scatter(n, j0, count):
+            nc.vector.tensor_tensor(
+                win[n][:].indirect(entries(dst_list, j0, count)), ysb[:, n, j0 : j0 + count], gg[n][:, j0 : j0 + count], MULT
+            )
+
+        wps = psum.tile([P, 2, CH], F32, name="yb")
+        nc.tensor.transpose(wps[:, 0, 0:P], wrow[:], ident[:])
+        nc.scalar.copy(wcol[:], wps[:, 0, 0 : J // P])
+
+        gather_scales(0)
+        gather_words(0)
+        part_words(0)
+        gates_a = load_gates(0, "late_a")
+        gather_words(1)
+        part_words(1)
+        hi0 = stage1(0)
+        gather_scales(1)
+        gates_b = load_gates(1, "late_b")
+        gather_words(2)
+        part_words(2)
+        q0 = quantise(hi0)
+        hi1 = stage1(1)
+        stage2(0, *q0)
+        gather_words(3)
+        part_words(3)
+        gather_gates(gates_a, 0)
+        gather_gates(gates_a, 1)
+        q1 = quantise(hi1)
+        hi2 = stage1(2)
+        stage2(1, *q1)
+        gather_gates(gates_b, 2)
+        gather_gates(gates_b, 3)
+        q2 = quantise(hi2)
+        hi3 = stage1(3)
+        stage2(2, *q2)
+        for n in range(4):
+            scatter(n, 0, CH)
+        q3 = quantise(hi3)
+        stage2(3, *q3)
+        for n in range(4):
+            scatter(n, CH, CH)
+        for c, n in ((2, 0), (2, 1), (3, 0), (2, 2), (3, 1), (3, 2), (2, 3), (3, 3)):
+            scatter(n, c * CH, CH)
+            if c == 3:
+                nc.sync.dma_start(out=out[n * P : (n + 1) * P, :], in_=win[n][:])

@@ -36,67 +36,61 @@ def tile_list_msg_tanh_gate_kernel(
         dst_list = keep.tile([P, J // 16], U16, name="dst_list")
         lists = (src_list, dst_list)
         tabw = keep.tile([P, T], I32, name="tabw", align_bytes=64)
+        wsw = keep.tile([P, 4 * R], U8, name="wsw", align_bytes=64)
+        wtw = keep.tile([P, 8 * R], U8, name="wtw", align_bytes=64)
         tabs = keep.tile([P, T], U8, name="tabs", tag="late_b", align_bytes=64)
-        wsw = keep.tile([P, 2, 2 * R], U8, name="wsw", align_bytes=64)
-        wdw = keep.tile([P, 2 * N], U8, name="wdw", align_bytes=64)
         wss = keep.tile([P, 2, R], U8, name="wss", align_bytes=64)
         wts = keep.tile([P, 2, R], U8, name="wts", align_bytes=64)
-        wds = keep.tile([P, N], U8, name="wds", align_bytes=64)
         sm_t = keep.tile([P, 4], F32, name="sm_t")
-        wrow = keep.tile([P, P], F32, name="wrow")
-        wcol = keep.tile([P, J // P], F32, name="wcol")
         ident = keep.tile([P, P], F32, name="ident")
-        gs0 = [keep.tile([P, 2, HALF], U8, name=f"gs0_{h}", align_bytes=64) for h in range(2)]
-        gs1 = [keep.tile([P, 2, HALF], U8, name=f"gs1_{h}", align_bytes=64) for h in range(2)]
-        gw = [keep.tile([P, 2, CH], I32, name=f"gw{c}", tag=("late_a" if c == 0 else f"gw{c}"), align_bytes=64) for c in range(NCH)]
+        vs = [keep.tile([P, 2, 2, HALF], U8, name=f"vs{h}", align_bytes=64) for h in range(2)]
+        gw = [keep.tile([P, 2, CH], I32, name=f"gw{c}", tag=f"gw{c}", align_bytes=64) for c in range(NCH)]
         vw = [keep.tile([P, 2, 2 * 2 * CH], U8, name=f"vw{c}", align_bytes=64) for c in range(NCH)]
-        gg = [keep.tile([P, J], F32, name=f"gg{n}") for n in range(4)]
+        gg = {}
         win = [keep.tile([P, T], F32, name=f"win{n}") for n in range(4)]
         ysb = keep.tile([P, 4, J], F32, name="ysb")
 
-        nc.gpsimd.memset(tabs[:].bitcast(I32), 0)
         nc.gpsimd.memset(wts[:].rearrange("p a n -> p (a n)").bitcast(I32), 0)
-        make_identity(nc, ident[:])
-        nc.vector.memset(wss[:].rearrange("p a n -> p (a n)").bitcast(I32), 0)
-        nc.vector.memset(wds[:].bitcast(I32), 0)
-        nc.vector.memset(wrow[:], 0.0)
+        nc.gpsimd.memset(wss[:].rearrange("p a n -> p (a n)").bitcast(I32), 0)
+        for q in range(4):
+            nc.vector.memset(tabs[32 * q : 32 * q + 24, :].bitcast(I32), 0)
         for h in range(2):
-            nc.vector.memset(gs1[h][:].rearrange("p a n -> p (a n)").bitcast(I32), 0)
-        warm = keep.tile([P, 1], F32, name="warm", tag="wt_slot", align_bytes=64)
-        nc.scalar.activation(warm[:], ident[:, 0:1], ACT.Tanh)
+            nc.gpsimd.memset(vs[h][96:128, :, :, :].rearrange("p a l n -> p (a l n)").bitcast(I32), 0)
 
         nc.sync.dma_start(src_list[:], offs)
         nc.sync.dma_start(dst_list[:], offs2)
-        nc.sync.dma_start(out=tabw[:], in_=tab_words[0].rearrange("p t b -> p (t b)").bitcast(I32))
         for q in range(4):
-            nc.sync.dma_start(out=tabs[32 * q : 32 * q + 8, :].bitcast(I32), in_=tab_scales[:, 4 * q : 4 * q + 4, :].bitcast(I32))
-        nc.sync.dma_start(out=wsw[:].bitcast(I32), in_=ws_words.rearrange("a p n -> p a n").bitcast(I32))
-        wtw = keep.tile([P, 2, R], I32, name="wtw", tag="wt_slot", align_bytes=64)
-        nc.sync.dma_start(out=wtw[:], in_=wt_words.rearrange("a p n b -> p a (n b)").bitcast(I32))
+            nc.sync.dma_start(out=tabs[32 * q + 24 : 32 * q + 32, :].bitcast(I32), in_=tab_scales[:, 4 * q : 4 * q + 4, :].bitcast(I32))
+        nc.sync.dma_start(out=tabw[:], in_=tab_words[0].rearrange("p t b -> p (t b)").bitcast(I32))
+        nc.sync.dma_start(out=wsw[:].bitcast(I32).rearrange("p (a n) -> p a n", a=2), in_=ws_words.rearrange("a p n -> p a n").bitcast(I32))
+        nc.sync.dma_start(out=wtw[:].bitcast(I32).rearrange("p (a n) -> p a n", a=2), in_=wt_words.rearrange("a p n b -> p a (n b)").bitcast(I32))
         for plane, rows, queue in ((wss, ws_scales, nc.sync), (wts, wt_scales, nc.gpsimd)):
             for q in range(4):
                 queue.dma_start(
                     out=plane[32 * q : 32 * q + 4, :, :].bitcast(I32),
                     in_=rows[:, 4 * q : 4 * q + 4, :].rearrange("a r n -> r a n").bitcast(I32),
                 )
-        nc.gpsimd.dma_start(out=sm_t[:], in_=sm.rearrange("(p t) -> p t", t=4))
-        nc.gpsimd.dma_start(out=wrow[0 : J // P, :], in_=wgo[0].rearrange("(c p) -> c p", p=P))
-        nc.gpsimd.dma_start(out=wdw[:].bitcast(I32), in_=wd_words[0].bitcast(I32))
-        for q in range(4):
-            nc.gpsimd.dma_start(out=wds[32 * q : 32 * q + 4, :].bitcast(I32), in_=wd_scales[0, 4 * q : 4 * q + 4, :].bitcast(I32))
+        nc.sync.dma_start(out=sm_t[:], in_=sm.rearrange("(p t) -> p t", t=4))
+        make_identity(nc, ident[:])
+        warm = keep.tile([P, 1], F32, name="warm")
+        nc.scalar.activation(warm[:], ident[:, 0:1], ACT.Tanh)
         for n in range(4):
-            (nc.vector if n < 2 else nc.gpsimd).memset(win[n][:], 0.0)
+            for j0 in range(0, T, 512):
+                nc.gpsimd.memset(win[n][:, j0 : j0 + 512], 0.0)
 
         def entries(lst, j0, count):
             return lst[:, j0 // 16 : (j0 + count) // 16]
 
-        def gather_scales(h):
+        def gather_scales(h, tag):
+            gs = keep.tile([P, 2, HALF], U8, name=f"gs{h}", tag=tag, align_bytes=64)
             for l in range(2):
-                nc.vector.tensor_copy(gs0[h][:, l, :], tabs[:].indirect(entries(lists[l], h * HALF, HALF)))
-            nc.sync.dma_start(
-                out=gs1[h][0:112, :, :].rearrange("p a n -> p (a n)").bitcast(I32),
-                in_=gs0[h][4:116, :, :].rearrange("p a n -> p (a n)").bitcast(I32),
-            )
+                nc.vector.tensor_copy(gs[:, l, :], tabs[:].indirect(entries(lists[l], h * HALF, HALF)))
+            for a in range(2):
+                first = 24 + 4 * a
+                nc.sync.dma_start(
+                    out=vs[h][0:100, a, :, :].rearrange("p l n -> p (l n)").bitcast(I32),
+                    in_=gs[first : first + 100, :, :].rearrange("p l n -> p (l n)").bitcast(I32),
+                )
 
         def gather_words(c):
             for l in range(2):
@@ -116,21 +110,22 @@ def tile_list_msg_tanh_gate_kernel(
             return gates
 
         def gather_gates(gates, n):
+            gg[n] = keep.tile([P, J], F32, name=f"gg{n}", tag=f"hi_gg{(4, 0, 1, 3)[n]}", align_bytes=64)
             nc.vector.tensor_copy(gg[n][:], gates[:, n % 2, :].indirect(src_list[:]))
 
         def stage1(c):
             h, base = divmod(c * CH, HALF)
-            th = ring.tile([P, CH // P, 4, P], F32, name="th")
+            th = keep.tile([P, CH // P, 4, P], F32, name="th")
             for u in range(CH // P):
                 acc = psum.tile([P, R], F32, name="acc")
                 for a in range(2):
-                    plane = (gs0, gs1)[a][h]
+                    plane = vs[h][:, a, :, :]
                     for l in range(2):
                         j0 = l * CH + u * P
                         if l == 0:
-                            w = wsw[:, a, :].bitcast(FP4X4)
+                            w = wsw[:, a * 2 * R : (a + 1) * 2 * R].bitcast(FP4X4)
                         else:
-                            w = wtw[:, a, :].bitcast(FP8X4)
+                            w = wtw[:, a * 4 * R : (a + 1) * 4 * R].bitcast(FP8X4)
                         nc.tensor.matmul_mx(
                             out=acc[:],
                             lhsT=vw[c][:, a, 2 * j0 : 2 * (j0 + P)].bitcast(FP4X4),
@@ -150,8 +145,9 @@ def tile_list_msg_tanh_gate_kernel(
                 for tt in range(2):
                     t = 2 * pair + tt
                     nc.scalar.activation(hb[:, t, :], ht[:, tt, :], ACT.Copy, scale=sm_t[:, t : t + 1])
-            hi = ring.tile([P, CH, 4], BF16, name="hi", align_bytes=64)
-            nc.scalar.copy(hi[:].rearrange("p (c i) t -> p c t i", i=4), hb[:].rearrange("p t (c i) -> p c t i", i=4))
+            hi = keep.tile([P, CH, 4], BF16, name=f"hi{c}", tag=f"hi_gg{c}", align_bytes=64)
+            weave = nc.vector.tensor_copy if c < 2 else nc.scalar.copy
+            weave(hi[:].rearrange("p (c i) t -> p c t i", i=4), hb[:].rearrange("p t (c i) -> p c t i", i=4))
             return hi
 
         def quantise(hi):
@@ -159,6 +155,18 @@ def tile_list_msg_tanh_gate_kernel(
             hs = ring.tile([P, CH], U8, name="hs", align_bytes=64)
             nc.vector.quantize_mx(out=hq[:].bitcast(FP8X4), scales=hs[:], in_=hi[:].rearrange("p j t -> p (j t)"))
             return hq, hs
+
+        def load_second():
+            second = keep.tile([P, 3 * N], U8, name="second", tag="gw1", align_bytes=64)
+            wdw, wds = second[:, 0 : 2 * N], second[:, 2 * N : 3 * N]
+            wcol = keep.tile([P, J // P], F32, name="wcol", tag="gw2", align_bytes=64)
+            nc.gpsimd.memset(wds.bitcast(I32), 0)
+            nc.sync.dma_start(out=wdw.bitcast(I32), in_=wd_words[0].bitcast(I32))
+            with nc.allow_non_contiguous_dma(reason="one edge weight a partition"):
+                nc.sync.dma_start(out=wcol[:], in_=wgo[0].rearrange("(c p) -> p c", p=P))
+            for q in range(4):
+                nc.sync.dma_start(out=wds[32 * q : 32 * q + 4, :].bitcast(I32), in_=wd_scales[0, 4 * q : 4 * q + 4, :].bitcast(I32))
+            return wdw, wds, wcol
 
         def stage2(c, hq, hs):
             yw = ring.tile([P, CH // P, N], F32, name="yw")
@@ -168,8 +176,8 @@ def tile_list_msg_tanh_gate_kernel(
                     out=yt[:],
                     lhsT=hq[:, u * P : (u + 1) * P].bitcast(FP8X4),
                     lhsT_scale=hs[:, u * P : (u + 1) * P],
-                    rhs=wdw[:].bitcast(FP4X4),
-                    rhs_scale=wds[:],
+                    rhs=wdw.bitcast(FP4X4),
+                    rhs_scale=wds,
                     start=True,
                     stop=True,
                 )
@@ -188,43 +196,39 @@ def tile_list_msg_tanh_gate_kernel(
                 win[n][:].indirect(entries(dst_list, j0, count)), ysb[:, n, j0 : j0 + count], gg[n][:, j0 : j0 + count], MULT
             )
 
-        wps = psum.tile([P, 2, CH], F32, name="yb")
-        nc.tensor.transpose(wps[:, 0, 0:P], wrow[:], ident[:])
-        nc.scalar.copy(wcol[:], wps[:, 0, 0 : J // P])
 
-        gather_scales(0)
+        gather_scales(0, "gs0")
         gather_words(0)
         part_words(0)
-        gates_a = load_gates(0, "late_a")
         gather_words(1)
         part_words(1)
         hi0 = stage1(0)
-        gather_scales(1)
-        gates_b = load_gates(1, "late_b")
+        gather_scales(1, "gw0")
+        gates_a = load_gates(0, "gs0")
         gather_words(2)
         part_words(2)
-        q0 = quantise(hi0)
-        hi1 = stage1(1)
-        stage2(0, *q0)
+        wdw, wds, wcol = load_second()
         gather_words(3)
         part_words(3)
+        gates_b = load_gates(1, "late_b")
         gather_gates(gates_a, 0)
+        q0 = quantise(hi0)
         gather_gates(gates_a, 1)
+        hi1 = stage1(1)
+        stage2(0, *q0)
         q1 = quantise(hi1)
+        gather_gates(gates_b, 2)
         hi2 = stage1(2)
         stage2(1, *q1)
-        gather_gates(gates_b, 2)
-        gather_gates(gates_b, 3)
         q2 = quantise(hi2)
         hi3 = stage1(3)
         stage2(2, *q2)
-        for n in range(4):
-            scatter(n, 0, CH)
         q3 = quantise(hi3)
+        gather_gates(gates_b, 3)
         stage2(3, *q3)
+        for c in range(2):
+            for n in range(4):
+                scatter(n, c * CH, CH)
         for n in range(4):
-            scatter(n, CH, CH)
-        for c, n in ((2, 0), (2, 1), (3, 0), (2, 2), (3, 1), (3, 2), (2, 3), (3, 3)):
-            scatter(n, c * CH, CH)
-            if c == 3:
-                nc.sync.dma_start(out=out[n * P : (n + 1) * P, :], in_=win[n][:])
+            scatter(n, HALF, HALF)
+            nc.sync.dma_start(out=out[n * P : (n + 1) * P, :], in_=win[n][:])

@@ -47,13 +47,17 @@ def tile_list_msg_tanh_gate_kernel(
         gw = [keep.tile([P, 2, CH], I32, name=f"gw{c}", tag=f"gw{c}", align_bytes=64) for c in range(NCH)]
         vw = [keep.tile([P, 2, 2 * 2 * CH], U8, name=f"vw{c}", align_bytes=64) for c in range(NCH)]
         gg = {}
-        win = [keep.tile([P, T], F32, name=f"win{n}") for n in range(4)]
+        win = {}
+        wrow = keep.tile([P, P], F32, name="wrow")
+        wcol = keep.tile([P, J // P], F32, name="wcol")
         ysb = keep.tile([P, 4, J], F32, name="ysb")
 
-        nc.gpsimd.memset(wts[:].rearrange("p a n -> p (a n)").bitcast(I32), 0)
-        nc.gpsimd.memset(wss[:].rearrange("p a n -> p (a n)").bitcast(I32), 0)
+        make_identity(nc, ident[:])
         for q in range(4):
             nc.vector.memset(tabs[32 * q : 32 * q + 24, :].bitcast(I32), 0)
+        nc.vector.memset(wss[:].rearrange("p a n -> p (a n)").bitcast(I32), 0)
+        nc.vector.memset(wts[:].rearrange("p a n -> p (a n)").bitcast(I32), 0)
+        nc.gpsimd.memset(wrow[:], 0.0)
         for h in range(2):
             nc.gpsimd.memset(vs[h][96:128, :, :, :].rearrange("p a l n -> p (a l n)").bitcast(I32), 0)
 
@@ -64,19 +68,19 @@ def tile_list_msg_tanh_gate_kernel(
         nc.sync.dma_start(out=tabw[:], in_=tab_words[0].rearrange("p t b -> p (t b)").bitcast(I32))
         nc.sync.dma_start(out=wsw[:].bitcast(I32).rearrange("p (a n) -> p a n", a=2), in_=ws_words.rearrange("a p n -> p a n").bitcast(I32))
         nc.sync.dma_start(out=wtw[:].bitcast(I32).rearrange("p (a n) -> p a n", a=2), in_=wt_words.rearrange("a p n b -> p a (n b)").bitcast(I32))
-        for plane, rows, queue in ((wss, ws_scales, nc.sync), (wts, wt_scales, nc.gpsimd)):
+        for plane, rows, queue in ((wss, ws_scales, nc.sync), (wts, wt_scales, nc.sync)):
             for q in range(4):
                 queue.dma_start(
                     out=plane[32 * q : 32 * q + 4, :, :].bitcast(I32),
                     in_=rows[:, 4 * q : 4 * q + 4, :].rearrange("a r n -> r a n").bitcast(I32),
                 )
         nc.sync.dma_start(out=sm_t[:], in_=sm.rearrange("(p t) -> p t", t=4))
-        make_identity(nc, ident[:])
+        nc.sync.dma_start(out=wrow[0 : J // P, :], in_=wgo[0].rearrange("(c p) -> c p", p=P))
         warm = keep.tile([P, 1], F32, name="warm")
         nc.scalar.activation(warm[:], ident[:, 0:1], ACT.Tanh)
-        for n in range(4):
-            for j0 in range(0, T, 512):
-                nc.gpsimd.memset(win[n][:, j0 : j0 + 512], 0.0)
+        wps = psum.tile([P, 2, CH], F32, name="yb")
+        nc.tensor.transpose(wps[:, 0, 0:P], wrow[:], ident[:])
+        nc.scalar.copy(wcol[:], wps[:, 0, 0 : J // P])
 
         def entries(lst, j0, count):
             return lst[:, j0 // 16 : (j0 + count) // 16]
@@ -91,6 +95,10 @@ def tile_list_msg_tanh_gate_kernel(
                     out=vs[h][0:100, a, :, :].rearrange("p l n -> p (l n)").bitcast(I32),
                     in_=gs[first : first + 100, :, :].rearrange("p l n -> p (l n)").bitcast(I32),
                 )
+
+        def clear_window(n, tag):
+            win[n] = keep.tile([P, T], F32, name=f"win{n}", tag=tag, align_bytes=64)
+            nc.vector.memset(win[n][:], 0.0)
 
         def gather_words(c):
             for l in range(2):
@@ -110,12 +118,11 @@ def tile_list_msg_tanh_gate_kernel(
             return gates
 
         def gather_gates(gates, n):
-            gg[n] = keep.tile([P, J], F32, name=f"gg{n}", tag=f"hi_gg{(4, 0, 1, 3)[n]}", align_bytes=64)
-            nc.vector.tensor_copy(gg[n][:], gates[:, n % 2, :].indirect(src_list[:]))
+            nc.vector.tensor_copy(gg[n], gates[:, n % 2, :].indirect(src_list[:]))
 
         def stage1(c):
             h, base = divmod(c * CH, HALF)
-            th = keep.tile([P, CH // P, 4, P], F32, name="th")
+            th = ring.tile([P, CH // P, 4, P], F32, name="th")
             for u in range(CH // P):
                 acc = psum.tile([P, R], F32, name="acc")
                 for a in range(2):
@@ -136,7 +143,7 @@ def tile_list_msg_tanh_gate_kernel(
                             stop=(a == 1 and l == 1),
                         )
                 nc.scalar.activation(th[:, u, :, :], acc[:].rearrange("p (m t) -> p t m", t=4), ACT.Tanh)
-            hb = ring.tile([P, 4, CH], BF16, name="hb")
+            hb = keep.tile([P, 4, CH], BF16, name=f"hb{c}", tag=f"hb{c}")
             for pair in range(2):
                 ht = psum.tile([P, 2, CH], F32, name="ht")
                 for tt in range(2):
@@ -145,31 +152,27 @@ def tile_list_msg_tanh_gate_kernel(
                 for tt in range(2):
                     t = 2 * pair + tt
                     nc.scalar.activation(hb[:, t, :], ht[:, tt, :], ACT.Copy, scale=sm_t[:, t : t + 1])
-            hi = keep.tile([P, CH, 4], BF16, name=f"hi{c}", tag=f"hi_gg{c}", align_bytes=64)
-            weave = nc.vector.tensor_copy if c < 2 else nc.scalar.copy
-            weave(hi[:].rearrange("p (c i) t -> p c t i", i=4), hb[:].rearrange("p t (c i) -> p c t i", i=4))
+            hi = keep.tile([P, CH, 4], BF16, name=f"hi{c}", tag=f"hi{c}", align_bytes=64)
+            nc.scalar.copy(hi[:].rearrange("p (c i) t -> p c t i", i=4), hb[:].rearrange("p t (c i) -> p c t i", i=4))
             return hi
 
         def quantise(hi):
-            hq = ring.tile([P, CH], U32, name="hq", align_bytes=64)
-            hs = ring.tile([P, CH], U8, name="hs", align_bytes=64)
+            hq = ring.tile([P, CH], U32, name="hq", align_bytes=64, bufs=4)
+            hs = ring.tile([P, CH], U8, name="hs", align_bytes=64, bufs=4)
             nc.vector.quantize_mx(out=hq[:].bitcast(FP8X4), scales=hs[:], in_=hi[:].rearrange("p j t -> p (j t)"))
             return hq, hs
 
         def load_second():
             second = keep.tile([P, 3 * N], U8, name="second", tag="gw1", align_bytes=64)
             wdw, wds = second[:, 0 : 2 * N], second[:, 2 * N : 3 * N]
-            wcol = keep.tile([P, J // P], F32, name="wcol", tag="gw2", align_bytes=64)
-            nc.gpsimd.memset(wds.bitcast(I32), 0)
+            nc.vector.memset(wds.bitcast(I32), 0)
             nc.sync.dma_start(out=wdw.bitcast(I32), in_=wd_words[0].bitcast(I32))
-            with nc.allow_non_contiguous_dma(reason="one edge weight a partition"):
-                nc.sync.dma_start(out=wcol[:], in_=wgo[0].rearrange("(c p) -> p c", p=P))
             for q in range(4):
                 nc.sync.dma_start(out=wds[32 * q : 32 * q + 4, :].bitcast(I32), in_=wd_scales[0, 4 * q : 4 * q + 4, :].bitcast(I32))
-            return wdw, wds, wcol
+            return wdw, wds
 
         def stage2(c, hq, hs):
-            yw = ring.tile([P, CH // P, N], F32, name="yw")
+            yw = keep.tile([P, CH // P, N], F32, name=f"yw{c}", tag=("hb1", "hb3", "yw2", "yw3")[c])
             for u in range(CH // P):
                 yt = psum.tile([P, N], F32, name="yt")
                 nc.tensor.matmul_mx(
@@ -202,29 +205,31 @@ def tile_list_msg_tanh_gate_kernel(
         part_words(0)
         gather_words(1)
         part_words(1)
+        wdw, wds = load_second()
         hi0 = stage1(0)
         gather_scales(1, "gw0")
         gates_a = load_gates(0, "gs0")
+        gates_b = load_gates(1, "late_b")
         gather_words(2)
         part_words(2)
-        wdw, wds, wcol = load_second()
         gather_words(3)
         part_words(3)
-        gates_b = load_gates(1, "late_b")
+        for n, tag in enumerate(("tabw", "gw2", "gw3", "vw0")):
+            clear_window(n, tag)
+        gg[0] = keep.tile([P, J], F32, name="gg0")[:, :]
         gather_gates(gates_a, 0)
         q0 = quantise(hi0)
-        gather_gates(gates_a, 1)
+        gg_rest = keep.tile([P, 3 * J], F32, name="gg_rest", tag="hi0", align_bytes=64)
+        for n in range(1, 4):
+            gg[n] = gg_rest[:, (n - 1) * J : n * J]
+            gather_gates((gates_a, gates_b)[n // 2], n)
         hi1 = stage1(1)
         stage2(0, *q0)
         q1 = quantise(hi1)
-        gather_gates(gates_b, 2)
-        hi2 = stage1(2)
+        q2 = quantise(stage1(2))
+        q3 = quantise(stage1(3))
         stage2(1, *q1)
-        q2 = quantise(hi2)
-        hi3 = stage1(3)
         stage2(2, *q2)
-        q3 = quantise(hi3)
-        gather_gates(gates_b, 3)
         stage2(3, *q3)
         for c in range(2):
             for n in range(4):

@@ -96,9 +96,9 @@ def tile_list_msg_tanh_gate_kernel(
                     in_=gs[first : first + 100, :, :].rearrange("p l n -> p (l n)").bitcast(I32),
                 )
 
-        def clear_window(n, tag):
+        def clear_window(n, tag, engine):
             win[n] = keep.tile([P, T], F32, name=f"win{n}", tag=tag, align_bytes=64)
-            nc.vector.memset(win[n][:], 0.0)
+            engine.memset(win[n][:].bitcast(I32), 0)
 
         def gather_words(c):
             for l in range(2):
@@ -214,8 +214,8 @@ def tile_list_msg_tanh_gate_kernel(
         part_words(2)
         gather_words(3)
         part_words(3)
-        for n, tag in enumerate(("tabw", "gw2", "gw3", "vw0")):
-            clear_window(n, tag)
+        clear_window(0, "tabw", nc.vector)
+        clear_window(1, "gw3", nc.vector)
         gg[0] = keep.tile([P, J], F32, name="gg0")[:, :]
         gather_gates(gates_a, 0)
         q0 = quantise(hi0)
@@ -223,9 +223,11 @@ def tile_list_msg_tanh_gate_kernel(
         for n in range(1, 4):
             gg[n] = gg_rest[:, (n - 1) * J : n * J]
             gather_gates((gates_a, gates_b)[n // 2], n)
+        clear_window(2, "late_b", nc.gpsimd)
         hi1 = stage1(1)
         stage2(0, *q0)
         q1 = quantise(hi1)
+        clear_window(3, "hi1", nc.gpsimd)
         q2 = quantise(stage1(2))
         q3 = quantise(stage1(3))
         stage2(1, *q1)

@@ -21,6 +21,7 @@ P = 128
 CH = 256
 NCH = J // CH
 HALF = J // 2
+NWIN = 3
 
 
 def tile_list_msg_tanh_gate_kernel(
@@ -35,49 +36,57 @@ def tile_list_msg_tanh_gate_kernel(
         src_list = keep.tile([P, J // 16], U16, name="src_list")
         dst_list = keep.tile([P, J // 16], U16, name="dst_list")
         lists = (src_list, dst_list)
-        tabw = keep.tile([P, T], I32, name="tabw", align_bytes=64)
+        tabw = keep.tile([P, T], I32, name="tabw", tag="tabw", align_bytes=64)
         wsw = keep.tile([P, 4 * R], U8, name="wsw", align_bytes=64)
         wtw = keep.tile([P, 8 * R], U8, name="wtw", align_bytes=64)
-        tabs = keep.tile([P, T], U8, name="tabs", tag="late_b", align_bytes=64)
-        wss = keep.tile([P, 2, R], U8, name="wss", align_bytes=64)
-        wts = keep.tile([P, 2, R], U8, name="wts", align_bytes=64)
+        wdw = keep.tile([P, 2 * N], U8, name="wdw", align_bytes=64)
+        tabs = keep.tile([P, T], U8, name="tabs", tag="tabs", align_bytes=64)
+        planes = keep.tile([P, 5, R], U8, name="planes", align_bytes=64)
         sm_t = keep.tile([P, 4], F32, name="sm_t")
         ident = keep.tile([P, P], F32, name="ident")
-        vs = [keep.tile([P, 2, 2, HALF], U8, name=f"vs{h}", align_bytes=64) for h in range(2)]
+        lifted = [keep.tile([P, 2, HALF], U8, name=f"lifted{h}", align_bytes=64) for h in range(2)]
         gw = [keep.tile([P, 2, CH], I32, name=f"gw{c}", tag=f"gw{c}", align_bytes=64) for c in range(NCH)]
         vw = [keep.tile([P, 2, 2 * 2 * CH], U8, name=f"vw{c}", align_bytes=64) for c in range(NCH)]
-        gg = {}
         win = {}
         wrow = keep.tile([P, P], F32, name="wrow")
         wcol = keep.tile([P, J // P], F32, name="wcol")
         ysb = keep.tile([P, 4, J], F32, name="ysb")
+        gs = {}
+        gg = {}
 
-        make_identity(nc, ident[:])
-        for q in range(4):
-            nc.vector.memset(tabs[32 * q : 32 * q + 24, :].bitcast(I32), 0)
-        nc.vector.memset(wss[:].rearrange("p a n -> p (a n)").bitcast(I32), 0)
-        nc.vector.memset(wts[:].rearrange("p a n -> p (a n)").bitcast(I32), 0)
+        def clear_window(w, tag):
+            win[w] = keep.tile([P, T], F32, name=f"win{w}", tag=tag, align_bytes=64)
+            nc.vector.memset(win[w][:].bitcast(I32), 0)
+
+        nc.vector.memset(tabs[:].bitcast(I32), 0)
+        nc.vector.memset(planes[:].rearrange("p a n -> p (a n)").bitcast(I32), 0)
+        clear_window(0, "win0")
         nc.gpsimd.memset(wrow[:], 0.0)
-        for h in range(2):
-            nc.gpsimd.memset(vs[h][96:128, :, :, :].rearrange("p a l n -> p (a l n)").bitcast(I32), 0)
+        make_identity(nc, ident[:])
 
         nc.sync.dma_start(src_list[:], offs)
         nc.sync.dma_start(dst_list[:], offs2)
-        for q in range(4):
-            nc.sync.dma_start(out=tabs[32 * q + 24 : 32 * q + 32, :].bitcast(I32), in_=tab_scales[:, 4 * q : 4 * q + 4, :].bitcast(I32))
+        for q in range(2):
+            nc.sync.dma_start(out=tabs[32 * q : 32 * q + 8, :].bitcast(I32), in_=tab_scales[:, 4 * q : 4 * q + 4, :].bitcast(I32))
+        for q in range(2, 4):
+            for a in range(2):
+                first = 32 * q - 4 * a
+                nc.sync.dma_start(out=tabs[first : first + 4, :].bitcast(I32), in_=tab_scales[a, 4 * q : 4 * q + 4, :].bitcast(I32))
         nc.sync.dma_start(out=tabw[:], in_=tab_words[0].rearrange("p t b -> p (t b)").bitcast(I32))
-        nc.sync.dma_start(out=wsw[:].bitcast(I32).rearrange("p (a n) -> p a n", a=2), in_=ws_words.rearrange("a p n -> p a n").bitcast(I32))
-        nc.sync.dma_start(out=wtw[:].bitcast(I32).rearrange("p (a n) -> p a n", a=2), in_=wt_words.rearrange("a p n b -> p a (n b)").bitcast(I32))
-        for plane, rows, queue in ((wss, ws_scales, nc.sync), (wts, wt_scales, nc.sync)):
+
+        def load_planes(first, rows, passes):
             for q in range(4):
-                queue.dma_start(
-                    out=plane[32 * q : 32 * q + 4, :, :].bitcast(I32),
+                nc.sync.dma_start(
+                    out=planes[32 * q : 32 * q + 4, first : first + passes, :].bitcast(I32),
                     in_=rows[:, 4 * q : 4 * q + 4, :].rearrange("a r n -> r a n").bitcast(I32),
                 )
+
+        load_planes(0, ws_scales, 2)
+        load_planes(2, wt_scales, 2)
+        nc.sync.dma_start(out=wsw[:].bitcast(I32).rearrange("p (a n) -> p a n", a=2), in_=ws_words.rearrange("a p n -> p a n").bitcast(I32))
+        nc.sync.dma_start(out=wtw[:].bitcast(I32).rearrange("p (a n) -> p a n", a=2), in_=wt_words.rearrange("a p n b -> p a (n b)").bitcast(I32))
         nc.sync.dma_start(out=sm_t[:], in_=sm.rearrange("(p t) -> p t", t=4))
         nc.sync.dma_start(out=wrow[0 : J // P, :], in_=wgo[0].rearrange("(c p) -> c p", p=P))
-        warm = keep.tile([P, 1], F32, name="warm")
-        nc.scalar.activation(warm[:], ident[:, 0:1], ACT.Tanh)
         wps = psum.tile([P, 2, CH], F32, name="yb")
         nc.tensor.transpose(wps[:, 0, 0:P], wrow[:], ident[:])
         nc.scalar.copy(wcol[:], wps[:, 0, 0 : J // P])
@@ -86,39 +95,25 @@ def tile_list_msg_tanh_gate_kernel(
             return lst[:, j0 // 16 : (j0 + count) // 16]
 
         def gather_scales(h, tag):
-            gs = keep.tile([P, 2, HALF], U8, name=f"gs{h}", tag=tag, align_bytes=64)
+            gs[h] = keep.tile([P, 2, HALF], U8, name=f"gs{h}", tag=tag, align_bytes=64)
             for l in range(2):
-                nc.vector.tensor_copy(gs[:, l, :], tabs[:].indirect(entries(lists[l], h * HALF, HALF)))
-            for a in range(2):
-                first = 24 + 4 * a
+                nc.vector.tensor_copy(gs[h][:, l, :], tabs[:].indirect(entries(lists[l], h * HALF, HALF)))
+            for lo, shift in ((0, 4), (64, -4)):
                 nc.sync.dma_start(
-                    out=vs[h][0:100, a, :, :].rearrange("p l n -> p (l n)").bitcast(I32),
-                    in_=gs[first : first + 100, :, :].rearrange("p l n -> p (l n)").bitcast(I32),
+                    out=lifted[h][lo : lo + 64, :, :].rearrange("p l n -> p (l n)").bitcast(I32),
+                    in_=gs[h][lo + shift : lo + shift + 64, :, :].rearrange("p l n -> p (l n)").bitcast(I32),
                 )
-
-        def clear_window(n, tag, engine):
-            win[n] = keep.tile([P, T], F32, name=f"win{n}", tag=tag, align_bytes=64)
-            engine.memset(win[n][:].bitcast(I32), 0)
 
         def gather_words(c):
             for l in range(2):
                 nc.vector.tensor_copy(gw[c][:, l, :].bitcast(U32), tabw[:].bitcast(U32).indirect(entries(lists[l], c * CH, CH)))
-
-        def part_words(c):
             nc.vector.tensor_copy(
                 vw[c][:].bitcast(U16),
                 gw[c][:].rearrange("p l j -> p (l j)").bitcast(U16).rearrange("p (j a) -> p a j", a=2),
             )
 
-        def load_gates(pair, tag):
-            gates = keep.tile([P, 2, T], F32, name=f"gates{pair}", tag=tag, align_bytes=64)
-            for nn in range(2):
-                n = 2 * pair + nn
-                nc.sync.dma_start(out=gates[:, nn, :], in_=gT[n * P : (n + 1) * P, :])
-            return gates
-
-        def gather_gates(gates, n):
-            nc.vector.tensor_copy(gg[n], gates[:, n % 2, :].indirect(src_list[:]))
+        def gather_gates(n):
+            nc.vector.tensor_copy(gg[n], gates[:, n, :].indirect(src_list[:]))
 
         def stage1(c):
             h, base = divmod(c * CH, HALF)
@@ -126,7 +121,7 @@ def tile_list_msg_tanh_gate_kernel(
             for u in range(CH // P):
                 acc = psum.tile([P, R], F32, name="acc")
                 for a in range(2):
-                    plane = vs[h][:, a, :, :]
+                    plane = (gs, lifted)[a][h]
                     for l in range(2):
                         j0 = l * CH + u * P
                         if l == 0:
@@ -138,12 +133,12 @@ def tile_list_msg_tanh_gate_kernel(
                             lhsT=vw[c][:, a, 2 * j0 : 2 * (j0 + P)].bitcast(FP4X4),
                             lhsT_scale=plane[:, l, base + u * P : base + (u + 1) * P],
                             rhs=w,
-                            rhs_scale=(wss, wts)[l][:, a, :],
+                            rhs_scale=planes[:, 2 * l + a, :],
                             start=(a == 0 and l == 0),
                             stop=(a == 1 and l == 1),
                         )
                 nc.scalar.activation(th[:, u, :, :], acc[:].rearrange("p (m t) -> p t m", t=4), ACT.Tanh)
-            hb = keep.tile([P, 4, CH], BF16, name=f"hb{c}", tag=f"hb{c}")
+            hb = ring.tile([P, 4, CH], BF16, name="hb")
             for pair in range(2):
                 ht = psum.tile([P, 2, CH], F32, name="ht")
                 for tt in range(2):
@@ -162,25 +157,16 @@ def tile_list_msg_tanh_gate_kernel(
             nc.vector.quantize_mx(out=hq[:].bitcast(FP8X4), scales=hs[:], in_=hi[:].rearrange("p j t -> p (j t)"))
             return hq, hs
 
-        def load_second():
-            second = keep.tile([P, 3 * N], U8, name="second", tag="gw1", align_bytes=64)
-            wdw, wds = second[:, 0 : 2 * N], second[:, 2 * N : 3 * N]
-            nc.vector.memset(wds.bitcast(I32), 0)
-            nc.sync.dma_start(out=wdw.bitcast(I32), in_=wd_words[0].bitcast(I32))
-            for q in range(4):
-                nc.sync.dma_start(out=wds[32 * q : 32 * q + 4, :].bitcast(I32), in_=wd_scales[0, 4 * q : 4 * q + 4, :].bitcast(I32))
-            return wdw, wds
-
         def stage2(c, hq, hs):
-            yw = keep.tile([P, CH // P, N], F32, name=f"yw{c}", tag=("hb1", "hb3", "yw2", "yw3")[c])
+            yw = ring.tile([P, CH // P, N], F32, name="yw")
             for u in range(CH // P):
                 yt = psum.tile([P, N], F32, name="yt")
                 nc.tensor.matmul_mx(
                     out=yt[:],
                     lhsT=hq[:, u * P : (u + 1) * P].bitcast(FP8X4),
                     lhsT_scale=hs[:, u * P : (u + 1) * P],
-                    rhs=wdw.bitcast(FP4X4),
-                    rhs_scale=wds,
+                    rhs=wdw[:].bitcast(FP4X4),
+                    rhs_scale=planes[:, 4, :],
                     start=True,
                     stop=True,
                 )
@@ -196,46 +182,49 @@ def tile_list_msg_tanh_gate_kernel(
 
         def scatter(n, j0, count):
             nc.vector.tensor_tensor(
-                win[n][:].indirect(entries(dst_list, j0, count)), ysb[:, n, j0 : j0 + count], gg[n][:, j0 : j0 + count], MULT
+                win[n % NWIN][:].indirect(entries(dst_list, j0, count)), ysb[:, n, j0 : j0 + count], gg[n][:, j0 : j0 + count], MULT
             )
 
+        def store(n):
+            nc.sync.dma_start(out=out[n * P : (n + 1) * P, :], in_=win[n % NWIN][:])
 
         gather_scales(0, "gs0")
+        nc.sync.dma_start(out=wdw[:].bitcast(I32), in_=wd_words[0].bitcast(I32))
+        load_planes(4, wd_scales, 1)
         gather_words(0)
-        part_words(0)
         gather_words(1)
-        part_words(1)
-        wdw, wds = load_second()
-        hi0 = stage1(0)
         gather_scales(1, "gw0")
-        gates_a = load_gates(0, "gs0")
-        gates_b = load_gates(1, "late_b")
+        gates = keep.tile([P, 4, T], F32, name="gates", tag="tabs", align_bytes=64)
+        for n in range(4):
+            nc.sync.dma_start(out=gates[:, n, :], in_=gT[n * P : (n + 1) * P, :])
         gather_words(2)
-        part_words(2)
         gather_words(3)
-        part_words(3)
-        clear_window(0, "tabw", nc.vector)
-        clear_window(1, "gw3", nc.vector)
-        gg[0] = keep.tile([P, J], F32, name="gg0")[:, :]
-        gather_gates(gates_a, 0)
-        q0 = quantise(hi0)
-        gg_rest = keep.tile([P, 3 * J], F32, name="gg_rest", tag="hi0", align_bytes=64)
-        for n in range(1, 4):
-            gg[n] = gg_rest[:, (n - 1) * J : n * J]
-            gather_gates((gates_a, gates_b)[n // 2], n)
-        clear_window(2, "late_b", nc.gpsimd)
+        clear_window(1, "tabw")
+        clear_window(2, "gw3")
+        hi0 = stage1(0)
         hi1 = stage1(1)
+        q0 = quantise(hi0)
+        gg[0] = keep.tile([P, J], F32, name="gg0", tag="hi0", align_bytes=64)[:, :]
+        gather_gates(0)
         stage2(0, *q0)
         q1 = quantise(hi1)
-        clear_window(3, "hi1", nc.gpsimd)
-        q2 = quantise(stage1(2))
-        q3 = quantise(stage1(3))
+        gg[1] = keep.tile([P, J], F32, name="gg1", tag="hi1", align_bytes=64)[:, :]
+        gather_gates(1)
+        hi2 = stage1(2)
         stage2(1, *q1)
+        q2 = quantise(hi2)
+        gg[2] = keep.tile([P, J], F32, name="gg2", tag="hi2", align_bytes=64)[:, :]
+        gather_gates(2)
+        hi3 = stage1(3)
         stage2(2, *q2)
+        q3 = quantise(hi3)
         stage2(3, *q3)
-        for c in range(2):
-            for n in range(4):
+        for c in range(NCH):
+            for n in range(NWIN):
                 scatter(n, c * CH, CH)
-        for n in range(4):
-            scatter(n, HALF, HALF)
-            nc.sync.dma_start(out=out[n * P : (n + 1) * P, :], in_=win[n][:])
+                if c == NCH - 1:
+                    store(n)
+        gg[3] = keep.tile([P, J], F32, name="gg3", tag="hi0", align_bytes=64)[:, :]
+        gather_gates(3)
+        scatter(3, 0, J)
+        store(3)

@@ -22,6 +22,7 @@ CH = 256
 NCH = J // CH
 HALF = J // 2
 NWIN = 3
+ROW0 = (24, 56, 88, 80)
 
 
 def tile_list_msg_tanh_gate_kernel(
@@ -44,34 +45,30 @@ def tile_list_msg_tanh_gate_kernel(
         planes = keep.tile([P, 5, R], U8, name="planes", align_bytes=64)
         sm_t = keep.tile([P, 4], F32, name="sm_t")
         ident = keep.tile([P, P], F32, name="ident")
-        lifted = [keep.tile([P, 2, HALF], U8, name=f"lifted{h}", align_bytes=64) for h in range(2)]
+        lifted = [keep.tile([P, 2, 2, HALF], U8, name=f"lifted{h}", align_bytes=64) for h in range(2)]
         gw = [keep.tile([P, 2, CH], I32, name=f"gw{c}", tag=f"gw{c}", align_bytes=64) for c in range(NCH)]
         vw = [keep.tile([P, 2, 2 * 2 * CH], U8, name=f"vw{c}", align_bytes=64) for c in range(NCH)]
         win = {}
-        wrow = keep.tile([P, P], F32, name="wrow")
-        wcol = keep.tile([P, J // P], F32, name="wcol")
-        ysb = keep.tile([P, 4, J], F32, name="ysb")
-        gs = {}
+        wgo_t = keep.tile([P, J], F32, name="wgo_t", align_bytes=64)
+        y_late = keep.tile([P, 2, J], F32, name="y_late")
+        y_early = {}
         gg = {}
+        gates = {}
 
         def clear_window(w, tag):
             win[w] = keep.tile([P, T], F32, name=f"win{w}", tag=tag, align_bytes=64)
             nc.vector.memset(win[w][:].bitcast(I32), 0)
 
-        nc.vector.memset(tabs[:].bitcast(I32), 0)
         nc.vector.memset(planes[:].rearrange("p a n -> p (a n)").bitcast(I32), 0)
+        for first, last in ((0, 24), (32, 56), (64, 80), (96, 128)):
+            nc.vector.memset(tabs[first:last, :].bitcast(I32), 0)
         clear_window(0, "win0")
-        nc.gpsimd.memset(wrow[:], 0.0)
         make_identity(nc, ident[:])
 
         nc.sync.dma_start(src_list[:], offs)
         nc.sync.dma_start(dst_list[:], offs2)
-        for q in range(2):
-            nc.sync.dma_start(out=tabs[32 * q : 32 * q + 8, :].bitcast(I32), in_=tab_scales[:, 4 * q : 4 * q + 4, :].bitcast(I32))
-        for q in range(2, 4):
-            for a in range(2):
-                first = 32 * q - 4 * a
-                nc.sync.dma_start(out=tabs[first : first + 4, :].bitcast(I32), in_=tab_scales[a, 4 * q : 4 * q + 4, :].bitcast(I32))
+        for q in range(4):
+            nc.sync.dma_start(out=tabs[ROW0[q] : ROW0[q] + 8, :].bitcast(I32), in_=tab_scales[:, 4 * q : 4 * q + 4, :].bitcast(I32))
         nc.sync.dma_start(out=tabw[:], in_=tab_words[0].rearrange("p t b -> p (t b)").bitcast(I32))
 
         def load_planes(first, rows, passes):
@@ -86,23 +83,21 @@ def tile_list_msg_tanh_gate_kernel(
         nc.sync.dma_start(out=wsw[:].bitcast(I32).rearrange("p (a n) -> p a n", a=2), in_=ws_words.rearrange("a p n -> p a n").bitcast(I32))
         nc.sync.dma_start(out=wtw[:].bitcast(I32).rearrange("p (a n) -> p a n", a=2), in_=wt_words.rearrange("a p n b -> p a (n b)").bitcast(I32))
         nc.sync.dma_start(out=sm_t[:], in_=sm.rearrange("(p t) -> p t", t=4))
-        nc.sync.dma_start(out=wrow[0 : J // P, :], in_=wgo[0].rearrange("(c p) -> c p", p=P))
-        wps = psum.tile([P, 2, CH], F32, name="yb")
-        nc.tensor.transpose(wps[:, 0, 0:P], wrow[:], ident[:])
-        nc.scalar.copy(wcol[:], wps[:, 0, 0 : J // P])
 
         def entries(lst, j0, count):
             return lst[:, j0 // 16 : (j0 + count) // 16]
 
         def gather_scales(h, tag):
-            gs[h] = keep.tile([P, 2, HALF], U8, name=f"gs{h}", tag=tag, align_bytes=64)
+            gs = keep.tile([P, 2, HALF], U8, name=f"gs{h}", tag=tag, align_bytes=64)
             for l in range(2):
-                nc.vector.tensor_copy(gs[h][:, l, :], tabs[:].indirect(entries(lists[l], h * HALF, HALF)))
-            for lo, shift in ((0, 4), (64, -4)):
-                nc.sync.dma_start(
-                    out=lifted[h][lo : lo + 64, :, :].rearrange("p l n -> p (l n)").bitcast(I32),
-                    in_=gs[h][lo + shift : lo + shift + 64, :, :].rearrange("p l n -> p (l n)").bitcast(I32),
-                )
+                nc.vector.tensor_copy(gs[:, l, :], tabs[:].indirect(entries(lists[l], h * HALF, HALF)))
+            for a in range(2):
+                for q, count in ((0, 64), (2, 32), (3, 32)):
+                    first = ROW0[q] + 4 * a
+                    nc.sync.dma_start(
+                        out=lifted[h][32 * q : 32 * q + count, a, :, :].rearrange("p l n -> p (l n)").bitcast(I32),
+                        in_=gs[first : first + count, :, :].rearrange("p l n -> p (l n)").bitcast(I32),
+                    )
 
         def gather_words(c):
             for l in range(2):
@@ -113,7 +108,7 @@ def tile_list_msg_tanh_gate_kernel(
             )
 
         def gather_gates(n):
-            nc.vector.tensor_copy(gg[n], gates[:, n, :].indirect(src_list[:]))
+            nc.vector.tensor_tensor(gg[n], gates[n][:].indirect(src_list[:]), wgo_t[:], MULT)
 
         def stage1(c):
             h, base = divmod(c * CH, HALF)
@@ -121,7 +116,7 @@ def tile_list_msg_tanh_gate_kernel(
             for u in range(CH // P):
                 acc = psum.tile([P, R], F32, name="acc")
                 for a in range(2):
-                    plane = (gs, lifted)[a][h]
+                    plane = lifted[h][:, a, :, :]
                     for l in range(2):
                         j0 = l * CH + u * P
                         if l == 0:
@@ -138,9 +133,9 @@ def tile_list_msg_tanh_gate_kernel(
                             stop=(a == 1 and l == 1),
                         )
                 nc.scalar.activation(th[:, u, :, :], acc[:].rearrange("p (m t) -> p t m", t=4), ACT.Tanh)
-            hb = ring.tile([P, 4, CH], BF16, name="hb")
+            hb = keep.tile([P, 4, CH], BF16, name=f"hb{c}", tag=f"hb{c}")
             for pair in range(2):
-                ht = psum.tile([P, 2, CH], F32, name="ht")
+                ht = psum.tile([P, 2, CH], F32, name="ht", tag="mid")
                 for tt in range(2):
                     for u in range(CH // P):
                         nc.tensor.transpose(ht[:, tt, u * P : (u + 1) * P], th[:, u, 2 * pair + tt, :], ident[:])
@@ -158,32 +153,29 @@ def tile_list_msg_tanh_gate_kernel(
             return hq, hs
 
         def stage2(c, hq, hs):
-            yw = ring.tile([P, CH // P, N], F32, name="yw")
-            for u in range(CH // P):
-                yt = psum.tile([P, N], F32, name="yt")
-                nc.tensor.matmul_mx(
-                    out=yt[:],
-                    lhsT=hq[:, u * P : (u + 1) * P].bitcast(FP8X4),
-                    lhsT_scale=hs[:, u * P : (u + 1) * P],
-                    rhs=wdw[:].bitcast(FP4X4),
-                    rhs_scale=planes[:, 4, :],
-                    start=True,
-                    stop=True,
-                )
-                col = c * (CH // P) + u
-                nc.scalar.activation(yw[:, u, :], yt[:], ACT.Copy, scale=wcol[:, col : col + 1])
+            y_early[c] = keep.tile([P, 2, CH], F32, name=f"y_early{c}", tag=f"hb{(c + 1) % NCH}")
             for pair in range(2):
-                yb = psum.tile([P, 2, CH], F32, name="yb")
+                yt = psum.tile([P, 2, CH], F32, name="yt", tag="mid")
                 for nn in range(2):
                     n = 2 * pair + nn
-                    for u in range(CH // P):
-                        nc.tensor.transpose(yb[:, nn, u * P : (u + 1) * P], yw[:, u, n * P : (n + 1) * P], ident[:])
-                nc.scalar.copy(ysb[:, 2 * pair : 2 * pair + 2, c * CH : (c + 1) * CH], yb[:])
+                    nc.tensor.matmul_mx(
+                        out=yt[:, nn, :],
+                        lhsT=wdw[:, 2 * n * P : 2 * (n + 1) * P].bitcast(FP4X4),
+                        lhsT_scale=planes[:, 4, n * P : (n + 1) * P],
+                        rhs=hq[:].bitcast(FP8X4),
+                        rhs_scale=hs[:],
+                        start=True,
+                        stop=True,
+                    )
+                nc.scalar.copy(y_early[c][:] if pair == 0 else y_late[:, :, c * CH : (c + 1) * CH], yt[:])
+
+        def load_gates(n, tag):
+            gates[n] = keep.tile([P, T], F32, name=f"gates{n}", tag=tag, align_bytes=64)
+            nc.sync.dma_start(out=gates[n][:], in_=gT[n * P : (n + 1) * P, :])
 
         def scatter(n, j0, count):
-            nc.vector.tensor_tensor(
-                win[n % NWIN][:].indirect(entries(dst_list, j0, count)), ysb[:, n, j0 : j0 + count], gg[n][:, j0 : j0 + count], MULT
-            )
+            y = y_early[j0 // CH][:, n, :] if n < 2 else y_late[:, n - 2, j0 : j0 + count]
+            nc.vector.tensor_tensor(win[n % NWIN][:].indirect(entries(dst_list, j0, count)), y, gg[n][:, j0 : j0 + count], MULT)
 
         def store(n):
             nc.sync.dma_start(out=out[n * P : (n + 1) * P, :], in_=win[n % NWIN][:])
@@ -191,30 +183,32 @@ def tile_list_msg_tanh_gate_kernel(
         gather_scales(0, "gs0")
         nc.sync.dma_start(out=wdw[:].bitcast(I32), in_=wd_words[0].bitcast(I32))
         load_planes(4, wd_scales, 1)
+        nc.sync.dma_start(out=wgo_t[:], in_=wgo)
         gather_words(0)
         gather_words(1)
         gather_scales(1, "gw0")
-        gates = keep.tile([P, 4, T], F32, name="gates", tag="tabs", align_bytes=64)
-        for n in range(4):
-            nc.sync.dma_start(out=gates[:, n, :], in_=gT[n * P : (n + 1) * P, :])
+        load_gates(0, "gw1")
+        load_gates(1, "tabs")
         gather_words(2)
+        load_gates(2, "gw2")
         gather_words(3)
+        load_gates(3, "gw3")
         clear_window(1, "tabw")
-        clear_window(2, "gw3")
+        clear_window(2, "gs0")
+        gg[0] = keep.tile([P, J], F32, name="gg0", tag="gg0", align_bytes=64)[:, :]
+        gather_gates(0)
         hi0 = stage1(0)
         hi1 = stage1(1)
         q0 = quantise(hi0)
-        gg[0] = keep.tile([P, J], F32, name="gg0", tag="hi0", align_bytes=64)[:, :]
-        gather_gates(0)
+        gg[1] = keep.tile([P, J], F32, name="gg1", tag="hi0", align_bytes=64)[:, :]
+        gather_gates(1)
         stage2(0, *q0)
         q1 = quantise(hi1)
-        gg[1] = keep.tile([P, J], F32, name="gg1", tag="hi1", align_bytes=64)[:, :]
-        gather_gates(1)
+        gg[2] = keep.tile([P, J], F32, name="gg2", tag="hi1", align_bytes=64)[:, :]
+        gather_gates(2)
         hi2 = stage1(2)
         stage2(1, *q1)
         q2 = quantise(hi2)
-        gg[2] = keep.tile([P, J], F32, name="gg2", tag="hi2", align_bytes=64)[:, :]
-        gather_gates(2)
         hi3 = stage1(3)
         stage2(2, *q2)
         q3 = quantise(hi3)
@@ -224,7 +218,7 @@ def tile_list_msg_tanh_gate_kernel(
                 scatter(n, c * CH, CH)
                 if c == NCH - 1:
                     store(n)
-        gg[3] = keep.tile([P, J], F32, name="gg3", tag="hi0", align_bytes=64)[:, :]
+        gg[3] = keep.tile([P, J], F32, name="gg3", tag="gg0", align_bytes=64)[:, :]
         gather_gates(3)
         scatter(3, 0, J)
         store(3)

@@ -21,8 +21,9 @@ P = 128
 CH = 256
 NCH = J // CH
 HALF = J // 2
-NWIN = 3
+NWIN = 2
 ROW0 = (24, 56, 88, 80)
+BATCH = ((0, CH), (CH, J - CH))
 
 
 def tile_list_msg_tanh_gate_kernel(
@@ -45,7 +46,7 @@ def tile_list_msg_tanh_gate_kernel(
         planes = keep.tile([P, 5, R], U8, name="planes", align_bytes=64)
         sm_t = keep.tile([P, 4], F32, name="sm_t")
         ident = keep.tile([P, P], F32, name="ident")
-        lifted = [keep.tile([P, 2, 2, HALF], U8, name=f"lifted{h}", align_bytes=64) for h in range(2)]
+        lifted = [keep.tile([P, 2, 2, BATCH[h][1]], U8, name=f"lifted{h}", align_bytes=64) for h in range(2)]
         gw = [keep.tile([P, 2, CH], I32, name=f"gw{c}", tag=f"gw{c}", align_bytes=64) for c in range(NCH)]
         vw = [keep.tile([P, 2, 2 * 2 * CH], U8, name=f"vw{c}", align_bytes=64) for c in range(NCH)]
         win = {}
@@ -88,9 +89,9 @@ def tile_list_msg_tanh_gate_kernel(
             return lst[:, j0 // 16 : (j0 + count) // 16]
 
         def gather_scales(h, tag):
-            gs = keep.tile([P, 2, HALF], U8, name=f"gs{h}", tag=tag, align_bytes=64)
+            gs = keep.tile([P, 2, BATCH[h][1]], U8, name=f"gs{h}", tag=tag, align_bytes=64)
             for l in range(2):
-                nc.vector.tensor_copy(gs[:, l, :], tabs[:].indirect(entries(lists[l], h * HALF, HALF)))
+                nc.vector.tensor_copy(gs[:, l, :], tabs[:].indirect(entries(lists[l], *BATCH[h])))
             for a in range(2):
                 for q, count in ((0, 64), (2, 32), (3, 32)):
                     first = ROW0[q] + 4 * a
@@ -111,7 +112,8 @@ def tile_list_msg_tanh_gate_kernel(
             nc.vector.tensor_tensor(gg[n], gates[n][:].indirect(src_list[:]), wgo_t[:], MULT)
 
         def stage1(c):
-            h, base = divmod(c * CH, HALF)
+            h = min(c, 1)
+            base = c * CH - BATCH[h][0]
             th = ring.tile([P, CH // P, 4, P], F32, name="th")
             for u in range(CH // P):
                 acc = psum.tile([P, R], F32, name="acc")
@@ -135,7 +137,7 @@ def tile_list_msg_tanh_gate_kernel(
                 nc.scalar.activation(th[:, u, :, :], acc[:].rearrange("p (m t) -> p t m", t=4), ACT.Tanh)
             hb = keep.tile([P, 4, CH], BF16, name=f"hb{c}", tag=f"hb{c}")
             for pair in range(2):
-                ht = psum.tile([P, 2, CH], F32, name="ht", tag="mid")
+                ht = psum.tile([P, 2, CH], F32, name="ht", tag=f"mid{c % 2}{pair}", bufs=1)
                 for tt in range(2):
                     for u in range(CH // P):
                         nc.tensor.transpose(ht[:, tt, u * P : (u + 1) * P], th[:, u, 2 * pair + tt, :], ident[:])
@@ -146,79 +148,102 @@ def tile_list_msg_tanh_gate_kernel(
             nc.scalar.copy(hi[:].rearrange("p (c i) t -> p c t i", i=4), hb[:].rearrange("p t (c i) -> p c t i", i=4))
             return hi
 
-        def quantise(hi):
-            hq = ring.tile([P, CH], U32, name="hq", align_bytes=64, bufs=4)
-            hs = ring.tile([P, CH], U8, name="hs", align_bytes=64, bufs=4)
-            nc.vector.quantize_mx(out=hq[:].bitcast(FP8X4), scales=hs[:], in_=hi[:].rearrange("p j t -> p (j t)"))
-            return hq, hs
+        hq = keep.tile([P, J], U32, name="hq", align_bytes=64)
+        hs = keep.tile([P, J], U8, name="hs", align_bytes=64)
 
-        def stage2(c, hq, hs):
-            y_early[c] = keep.tile([P, 2, CH], F32, name=f"y_early{c}", tag=f"hb{(c + 1) % NCH}")
-            for pair in range(2):
-                yt = psum.tile([P, 2, CH], F32, name="yt", tag="mid")
-                for nn in range(2):
-                    n = 2 * pair + nn
-                    nc.tensor.matmul_mx(
-                        out=yt[:, nn, :],
-                        lhsT=wdw[:, 2 * n * P : 2 * (n + 1) * P].bitcast(FP4X4),
-                        lhsT_scale=planes[:, 4, n * P : (n + 1) * P],
-                        rhs=hq[:].bitcast(FP8X4),
-                        rhs_scale=hs[:],
-                        start=True,
-                        stop=True,
-                    )
-                nc.scalar.copy(y_early[c][:] if pair == 0 else y_late[:, :, c * CH : (c + 1) * CH], yt[:])
+        def quantise(c, hi):
+            cols = slice(c * CH, (c + 1) * CH)
+            nc.vector.quantize_mx(out=hq[:, cols].bitcast(FP8X4), scales=hs[:, cols], in_=hi[:].rearrange("p j t -> p (j t)"))
+
+        def second_product(n, j0, count, bank):
+            nc.tensor.matmul_mx(
+                out=bank,
+                lhsT=wdw[:, 2 * n * P : 2 * (n + 1) * P].bitcast(FP4X4),
+                lhsT_scale=planes[:, 4, n * P : (n + 1) * P],
+                rhs=hq[:, j0 : j0 + count].bitcast(FP8X4),
+                rhs_scale=hs[:, j0 : j0 + count],
+                start=True,
+                stop=True,
+            )
+
+        def stage2(c):
+            if c < 2:
+                y_early[c] = keep.tile([P, 2, CH], F32, name=f"y_early{c}", tag=f"hb{c + 1}")[:, :, :]
+            else:
+                if c == 2:
+                    y_early["half"] = keep.tile([P, 2, HALF], F32, name="y_half", tag="hb3")
+                y_early[c] = y_early["half"][:, :, (c - 2) * CH : (c - 1) * CH]
+            yt = psum.tile([P, 2, CH], F32, name="yt", tag=f"mid{(c + 1) % 2}0", bufs=1)
+            for n in range(2):
+                second_product(n, c * CH, CH, yt[:, n, :])
+            nc.scalar.copy(y_early[c], yt[:])
+
+        def stage2_late(n, h):
+            yt = psum.tile([P, HALF], F32, name="yt_late", tag=f"mid{h}1", bufs=1)
+            second_product(n, h * HALF, HALF, yt[:])
+            nc.scalar.copy(y_late[:, n - 2, h * HALF : (h + 1) * HALF], yt[:])
 
         def load_gates(n, tag):
             gates[n] = keep.tile([P, T], F32, name=f"gates{n}", tag=tag, align_bytes=64)
             nc.sync.dma_start(out=gates[n][:], in_=gT[n * P : (n + 1) * P, :])
 
         def scatter(n, j0, count):
-            y = y_early[j0 // CH][:, n, :] if n < 2 else y_late[:, n - 2, j0 : j0 + count]
+            if n >= 2:
+                y = y_late[:, n - 2, j0 : j0 + count]
+            elif count == CH:
+                y = y_early[j0 // CH][:, n, :]
+            else:
+                y = y_early["half"][:, n, :]
             nc.vector.tensor_tensor(win[n % NWIN][:].indirect(entries(dst_list, j0, count)), y, gg[n][:, j0 : j0 + count], MULT)
 
         def store(n):
             nc.sync.dma_start(out=out[n * P : (n + 1) * P, :], in_=win[n % NWIN][:])
+
+        def gather_gates_into(n, tag):
+            gg[n] = keep.tile([P, J], F32, name=f"gg{n}", tag=tag, align_bytes=64)[:, :]
+            gather_gates(n)
 
         gather_scales(0, "gs0")
         nc.sync.dma_start(out=wdw[:].bitcast(I32), in_=wd_words[0].bitcast(I32))
         load_planes(4, wd_scales, 1)
         nc.sync.dma_start(out=wgo_t[:], in_=wgo)
         gather_words(0)
-        gather_words(1)
+        load_gates(2, "gs0")
         gather_scales(1, "gw0")
-        load_gates(0, "gw1")
         load_gates(1, "tabs")
+        gather_words(1)
+        load_gates(0, "gw1")
         gather_words(2)
-        load_gates(2, "gw2")
         gather_words(3)
         load_gates(3, "gw3")
         clear_window(1, "tabw")
-        clear_window(2, "gs0")
-        gg[0] = keep.tile([P, J], F32, name="gg0", tag="gg0", align_bytes=64)[:, :]
-        gather_gates(0)
+        gather_gates_into(2, "gg2")
         hi0 = stage1(0)
         hi1 = stage1(1)
-        q0 = quantise(hi0)
-        gg[1] = keep.tile([P, J], F32, name="gg1", tag="hi0", align_bytes=64)[:, :]
-        gather_gates(1)
-        stage2(0, *q0)
-        q1 = quantise(hi1)
-        gg[2] = keep.tile([P, J], F32, name="gg2", tag="hi1", align_bytes=64)[:, :]
-        gather_gates(2)
+        quantise(0, hi0)
+        gather_gates_into(1, "hi0")
+        stage2(0)
+        quantise(1, hi1)
+        gather_gates_into(0, "hi1")
         hi2 = stage1(2)
-        stage2(1, *q1)
-        q2 = quantise(hi2)
+        stage2(1)
+        quantise(2, hi2)
         hi3 = stage1(3)
-        stage2(2, *q2)
-        q3 = quantise(hi3)
-        stage2(3, *q3)
-        for c in range(NCH):
-            for n in range(NWIN):
+        stage2(2)
+        quantise(3, hi3)
+        stage2(3)
+        for n in (2, 3):
+            for h in range(2):
+                stage2_late(n, h)
+        for c in range(2):
+            for n in range(2):
                 scatter(n, c * CH, CH)
-                if c == NCH - 1:
-                    store(n)
-        gg[3] = keep.tile([P, J], F32, name="gg3", tag="gg0", align_bytes=64)[:, :]
-        gather_gates(3)
-        scatter(3, 0, J)
-        store(3)
+        scatter(0, 2 * CH, CH)
+        scatter(0, 3 * CH, CH)
+        store(0)
+        scatter(1, HALF, HALF)
+        store(1)
+        gather_gates_into(3, "hi1")
+        for n in (2, 3):
+            scatter(n, 0, J)
+            store(n)

@@ -22,7 +22,6 @@ CH = 256
 NCH = J // CH
 HALF = J // 2
 NWIN = 2
-ROW0 = (24, 56, 88, 80)
 BATCH = ((0, CH), (CH, J - CH))
 
 
@@ -32,6 +31,7 @@ def tile_list_msg_tanh_gate_kernel(
     nc = tc.nc
     with ExitStack() as ctx:
         keep = ctx.enter_context(tc.tile_pool(name="keep", bufs=1))
+        lay = ctx.enter_context(tc.tile_pool(name="lay", bufs=1))
         ring = ctx.enter_context(tc.tile_pool(name="ring", bufs=2))
         psum = ctx.enter_context(tc.psum_pool(name="psum", bufs=2))
 
@@ -47,10 +47,10 @@ def tile_list_msg_tanh_gate_kernel(
         sm_t = keep.tile([P, 4], F32, name="sm_t")
         ident = keep.tile([P, P], F32, name="ident")
         lifted = [keep.tile([P, 2, 2, BATCH[h][1]], U8, name=f"lifted{h}", align_bytes=64) for h in range(2)]
-        gw = [keep.tile([P, 2, CH], I32, name=f"gw{c}", tag=f"gw{c}", align_bytes=64) for c in range(NCH)]
+        gw = [lay.tile([P, 2, CH], I32, name="gw0", align_bytes=64, offset=0)]
+        gw.extend(keep.tile([P, 2, CH], I32, name=f"gw{c}", tag=f"gw{c}", align_bytes=64) for c in range(1, NCH))
         vw = [keep.tile([P, 2, 2 * 2 * CH], U8, name=f"vw{c}", align_bytes=64) for c in range(NCH)]
         win = {}
-        wgo_t = keep.tile([P, J], F32, name="wgo_t", align_bytes=64)
         y_late = keep.tile([P, 2, J], F32, name="y_late")
         y_early = {}
         gg = {}
@@ -61,15 +61,14 @@ def tile_list_msg_tanh_gate_kernel(
             nc.vector.memset(win[w][:].bitcast(I32), 0)
 
         nc.vector.memset(planes[:].rearrange("p a n -> p (a n)").bitcast(I32), 0)
-        for first, last in ((0, 24), (32, 56), (64, 80), (96, 128)):
+        for first, last in ((0, 32), (64, 128)):
             nc.vector.memset(tabs[first:last, :].bitcast(I32), 0)
         clear_window(0, "win0")
         make_identity(nc, ident[:])
 
         nc.sync.dma_start(src_list[:], offs)
         nc.sync.dma_start(dst_list[:], offs2)
-        for q in range(4):
-            nc.sync.dma_start(out=tabs[ROW0[q] : ROW0[q] + 8, :].bitcast(I32), in_=tab_scales[:, 4 * q : 4 * q + 4, :].bitcast(I32))
+        nc.sync.dma_start(out=tabs[32:64, :].bitcast(I32), in_=tab_scales.rearrange("a r t -> (a r) t").bitcast(I32))
         nc.sync.dma_start(out=tabw[:], in_=tab_words[0].rearrange("p t b -> p (t b)").bitcast(I32))
 
         def load_planes(first, rows, passes):
@@ -89,12 +88,15 @@ def tile_list_msg_tanh_gate_kernel(
             return lst[:, j0 // 16 : (j0 + count) // 16]
 
         def gather_scales(h, tag):
-            gs = keep.tile([P, 2, BATCH[h][1]], U8, name=f"gs{h}", tag=tag, align_bytes=64)
+            if h == 0:
+                gs = keep.tile([P, 2, BATCH[h][1]], U8, name="gs0", tag=tag, align_bytes=64)
+            else:
+                gs = lay.tile([P, 2, BATCH[h][1]], U8, name="gs1", align_bytes=64, offset=0)
             for l in range(2):
                 nc.vector.tensor_copy(gs[:, l, :], tabs[:].indirect(entries(lists[l], *BATCH[h])))
             for a in range(2):
-                for q, count in ((0, 64), (2, 32), (3, 32)):
-                    first = ROW0[q] + 4 * a
+                for q in range(4):
+                    first, count = 32 + 16 * a + 4 * q, 32
                     nc.sync.dma_start(
                         out=lifted[h][32 * q : 32 * q + count, a, :, :].rearrange("p l n -> p (l n)").bitcast(I32),
                         in_=gs[first : first + count, :, :].rearrange("p l n -> p (l n)").bitcast(I32),
@@ -116,7 +118,7 @@ def tile_list_msg_tanh_gate_kernel(
             base = c * CH - BATCH[h][0]
             th = ring.tile([P, CH // P, 4, P], F32, name="th")
             for u in range(CH // P):
-                acc = psum.tile([P, R], F32, name="acc")
+                acc = psum.tile([P, R], F32, name="acc", tag="acc")
                 for a in range(2):
                     plane = lifted[h][:, a, :, :]
                     for l in range(2):
@@ -148,20 +150,23 @@ def tile_list_msg_tanh_gate_kernel(
             nc.scalar.copy(hi[:].rearrange("p (c i) t -> p c t i", i=4), hb[:].rearrange("p t (c i) -> p c t i", i=4))
             return hi
 
-        hq = keep.tile([P, J], U32, name="hq", align_bytes=64)
+        hq = {}
         hs = keep.tile([P, J], U8, name="hs", align_bytes=64)
 
-        def quantise(c, hi):
-            cols = slice(c * CH, (c + 1) * CH)
-            nc.vector.quantize_mx(out=hq[:, cols].bitcast(FP8X4), scales=hs[:, cols], in_=hi[:].rearrange("p j t -> p (j t)"))
+        def quantise(c, hi, tag):
+            if c == 0:
+                hq[c] = lay.tile([P, CH], U32, name="hq0", align_bytes=64, offset=4096)
+            else:
+                hq[c] = keep.tile([P, CH], U32, name=f"hq{c}", tag=tag, align_bytes=64)
+            nc.vector.quantize_mx(out=hq[c][:].bitcast(FP8X4), scales=hs[:, c * CH : (c + 1) * CH], in_=hi[:].rearrange("p j t -> p (j t)"))
 
-        def second_product(n, j0, count, bank):
+        def second_product(n, c, bank):
             nc.tensor.matmul_mx(
                 out=bank,
                 lhsT=wdw[:, 2 * n * P : 2 * (n + 1) * P].bitcast(FP4X4),
                 lhsT_scale=planes[:, 4, n * P : (n + 1) * P],
-                rhs=hq[:, j0 : j0 + count].bitcast(FP8X4),
-                rhs_scale=hs[:, j0 : j0 + count],
+                rhs=hq[c][:].bitcast(FP8X4),
+                rhs_scale=hs[:, c * CH : (c + 1) * CH],
                 start=True,
                 stop=True,
             )
@@ -175,16 +180,20 @@ def tile_list_msg_tanh_gate_kernel(
                 y_early[c] = y_early["half"][:, :, (c - 2) * CH : (c - 1) * CH]
             yt = psum.tile([P, 2, CH], F32, name="yt", tag=f"mid{(c + 1) % 2}0", bufs=1)
             for n in range(2):
-                second_product(n, c * CH, CH, yt[:, n, :])
+                second_product(n, c, yt[:, n, :])
             nc.scalar.copy(y_early[c], yt[:])
 
-        def stage2_late(n, h):
-            yt = psum.tile([P, HALF], F32, name="yt_late", tag=f"mid{h}1", bufs=1)
-            second_product(n, h * HALF, HALF, yt[:])
-            nc.scalar.copy(y_late[:, n - 2, h * HALF : (h + 1) * HALF], yt[:])
+        def stage2_late(c):
+            yt = psum.tile([P, 2, CH], F32, name="yt_late", tag="acc")
+            for n in range(2):
+                second_product(2 + n, c, yt[:, n, :])
+            nc.scalar.copy(y_late[:, :, c * CH : (c + 1) * CH], yt[:])
 
         def load_gates(n, tag):
-            gates[n] = keep.tile([P, T], F32, name=f"gates{n}", tag=tag, align_bytes=64)
+            if n == 2:
+                gates[n] = lay.tile([P, T], F32, name="gates2", align_bytes=64, offset=2 * BATCH[1][1])
+            else:
+                gates[n] = keep.tile([P, T], F32, name=f"gates{n}", tag=tag, align_bytes=64)
             nc.sync.dma_start(out=gates[n][:], in_=gT[n * P : (n + 1) * P, :])
 
         def scatter(n, j0, count):
@@ -206,10 +215,11 @@ def tile_list_msg_tanh_gate_kernel(
         gather_scales(0, "gs0")
         nc.sync.dma_start(out=wdw[:].bitcast(I32), in_=wd_words[0].bitcast(I32))
         load_planes(4, wd_scales, 1)
-        nc.sync.dma_start(out=wgo_t[:], in_=wgo)
         gather_words(0)
-        load_gates(2, "gs0")
-        gather_scales(1, "gw0")
+        wgo_t = keep.tile([P, J], F32, name="wgo_t", tag="gs0", align_bytes=64)
+        nc.sync.dma_start(out=wgo_t[:], in_=wgo)
+        load_gates(2, "gw0")
+        gather_scales(1, "gs1")
         load_gates(1, "tabs")
         gather_words(1)
         load_gates(0, "gw1")
@@ -220,21 +230,20 @@ def tile_list_msg_tanh_gate_kernel(
         gather_gates_into(2, "gg2")
         hi0 = stage1(0)
         hi1 = stage1(1)
-        quantise(0, hi0)
+        quantise(0, hi0, "gw0")
         gather_gates_into(1, "hi0")
         stage2(0)
-        quantise(1, hi1)
+        quantise(1, hi1, "tabs")
         gather_gates_into(0, "hi1")
         hi2 = stage1(2)
         stage2(1)
-        quantise(2, hi2)
+        quantise(2, hi2, "gw1")
         hi3 = stage1(3)
         stage2(2)
-        quantise(3, hi3)
+        quantise(3, hi3, "hq3")
         stage2(3)
-        for n in (2, 3):
-            for h in range(2):
-                stage2_late(n, h)
+        for c in range(NCH):
+            stage2_late(c)
         for c in range(2):
             for n in range(2):
                 scatter(n, c * CH, CH)

@@ -21,8 +21,14 @@ P = 128
 CH = 256
 NCH = J // CH
 HALF = J // 2
-NWIN = 2
+NWIN = 3
 BATCH = ((0, CH), (CH, J - CH))
+AT = {
+    "gw0": 0, "gs1": 0, "gates2": 1536, "hq0": 4096,
+    "gw3": 18432 - 1024, "win1": 18432 - 8192, "win2": 18432,
+    "hb0": 30720, "gg0": 30720 + 1024 - 4096, "y_early3": 30720 + 1024,
+    "hb1": 40960, "y_early0": 40960, "gg3": 40960 + 1024 - 4096,
+}
 
 
 def tile_list_msg_tanh_gate_kernel(
@@ -34,6 +40,11 @@ def tile_list_msg_tanh_gate_kernel(
         lay = ctx.enter_context(tc.tile_pool(name="lay", bufs=1))
         ring = ctx.enter_context(tc.tile_pool(name="ring", bufs=2))
         psum = ctx.enter_context(tc.psum_pool(name="psum", bufs=2))
+
+        def tile(name, shape, dtype, tag=None):
+            if name in AT:
+                return lay.tile(shape, dtype, name=name, align_bytes=64, offset=AT[name])
+            return keep.tile(shape, dtype, name=name, tag=tag or name, align_bytes=64)
 
         src_list = keep.tile([P, J // 16], U16, name="src_list")
         dst_list = keep.tile([P, J // 16], U16, name="dst_list")
@@ -47,8 +58,7 @@ def tile_list_msg_tanh_gate_kernel(
         sm_t = keep.tile([P, 4], F32, name="sm_t")
         ident = keep.tile([P, P], F32, name="ident")
         lifted = [keep.tile([P, 2, 2, BATCH[h][1]], U8, name=f"lifted{h}", align_bytes=64) for h in range(2)]
-        gw = [lay.tile([P, 2, CH], I32, name="gw0", align_bytes=64, offset=0)]
-        gw.extend(keep.tile([P, 2, CH], I32, name=f"gw{c}", tag=f"gw{c}", align_bytes=64) for c in range(1, NCH))
+        gw = [tile(f"gw{c}", [P, 2, CH], I32) for c in range(NCH)]
         vw = [keep.tile([P, 2, 2 * 2 * CH], U8, name=f"vw{c}", align_bytes=64) for c in range(NCH)]
         win = {}
         y_late = keep.tile([P, 2, J], F32, name="y_late")
@@ -56,14 +66,14 @@ def tile_list_msg_tanh_gate_kernel(
         gg = {}
         gates = {}
 
-        def clear_window(w, tag):
-            win[w] = keep.tile([P, T], F32, name=f"win{w}", tag=tag, align_bytes=64)
-            nc.vector.memset(win[w][:].bitcast(I32), 0)
+        def clear_window(w, engine):
+            win[w] = tile(f"win{w}", [P, T], F32)
+            engine.memset(win[w][:].bitcast(I32), 0)
 
         nc.vector.memset(planes[:].rearrange("p a n -> p (a n)").bitcast(I32), 0)
         for first, last in ((0, 32), (64, 128)):
             nc.vector.memset(tabs[first:last, :].bitcast(I32), 0)
-        clear_window(0, "win0")
+        clear_window(0, nc.vector)
         make_identity(nc, ident[:])
 
         nc.sync.dma_start(src_list[:], offs)
@@ -87,11 +97,8 @@ def tile_list_msg_tanh_gate_kernel(
         def entries(lst, j0, count):
             return lst[:, j0 // 16 : (j0 + count) // 16]
 
-        def gather_scales(h, tag):
-            if h == 0:
-                gs = keep.tile([P, 2, BATCH[h][1]], U8, name="gs0", tag=tag, align_bytes=64)
-            else:
-                gs = lay.tile([P, 2, BATCH[h][1]], U8, name="gs1", align_bytes=64, offset=0)
+        def gather_scales(h):
+            gs = tile(f"gs{h}", [P, 2, BATCH[h][1]], U8)
             for l in range(2):
                 nc.vector.tensor_copy(gs[:, l, :], tabs[:].indirect(entries(lists[l], *BATCH[h])))
             for a in range(2):
@@ -111,6 +118,7 @@ def tile_list_msg_tanh_gate_kernel(
             )
 
         def gather_gates(n):
+            gg[n] = tile(f"gg{n}", [P, J], F32)[:, :]
             nc.vector.tensor_tensor(gg[n], gates[n][:].indirect(src_list[:]), wgo_t[:], MULT)
 
         def stage1(c):
@@ -137,7 +145,7 @@ def tile_list_msg_tanh_gate_kernel(
                             stop=(a == 1 and l == 1),
                         )
                 nc.scalar.activation(th[:, u, :, :], acc[:].rearrange("p (m t) -> p t m", t=4), ACT.Tanh)
-            hb = keep.tile([P, 4, CH], BF16, name=f"hb{c}", tag=f"hb{c}")
+            hb = tile(f"hb{c}", [P, 4, CH], BF16)
             for pair in range(2):
                 ht = psum.tile([P, 2, CH], F32, name="ht", tag=f"mid{c % 2}{pair}", bufs=1)
                 for tt in range(2):
@@ -146,18 +154,15 @@ def tile_list_msg_tanh_gate_kernel(
                 for tt in range(2):
                     t = 2 * pair + tt
                     nc.scalar.activation(hb[:, t, :], ht[:, tt, :], ACT.Copy, scale=sm_t[:, t : t + 1])
-            hi = keep.tile([P, CH, 4], BF16, name=f"hi{c}", tag=f"hi{c}", align_bytes=64)
+            hi = tile(f"hi{c}", [P, CH, 4], BF16)
             nc.scalar.copy(hi[:].rearrange("p (c i) t -> p c t i", i=4), hb[:].rearrange("p t (c i) -> p c t i", i=4))
             return hi
 
         hq = {}
         hs = keep.tile([P, J], U8, name="hs", align_bytes=64)
 
-        def quantise(c, hi, tag):
-            if c == 0:
-                hq[c] = lay.tile([P, CH], U32, name="hq0", align_bytes=64, offset=4096)
-            else:
-                hq[c] = keep.tile([P, CH], U32, name=f"hq{c}", tag=tag, align_bytes=64)
+        def quantise(c, hi):
+            hq[c] = tile(f"hq{c}", [P, CH], U32)
             nc.vector.quantize_mx(out=hq[c][:].bitcast(FP8X4), scales=hs[:, c * CH : (c + 1) * CH], in_=hi[:].rearrange("p j t -> p (j t)"))
 
         def second_product(n, c, bank):
@@ -172,12 +177,7 @@ def tile_list_msg_tanh_gate_kernel(
             )
 
         def stage2(c):
-            if c < 2:
-                y_early[c] = keep.tile([P, 2, CH], F32, name=f"y_early{c}", tag=f"hb{c + 1}")[:, :, :]
-            else:
-                if c == 2:
-                    y_early["half"] = keep.tile([P, 2, HALF], F32, name="y_half", tag="hb3")
-                y_early[c] = y_early["half"][:, :, (c - 2) * CH : (c - 1) * CH]
+            y_early[c] = tile(f"y_early{c}", [P, 2, CH], F32, f"hb{c + 1}")[:, :, :]
             yt = psum.tile([P, 2, CH], F32, name="yt", tag=f"mid{(c + 1) % 2}0", bufs=1)
             for n in range(2):
                 second_product(n, c, yt[:, n, :])
@@ -190,69 +190,60 @@ def tile_list_msg_tanh_gate_kernel(
             nc.scalar.copy(y_late[:, :, c * CH : (c + 1) * CH], yt[:])
 
         def load_gates(n, tag):
-            if n == 2:
-                gates[n] = lay.tile([P, T], F32, name="gates2", align_bytes=64, offset=2 * BATCH[1][1])
-            else:
-                gates[n] = keep.tile([P, T], F32, name=f"gates{n}", tag=tag, align_bytes=64)
+            gates[n] = tile(f"gates{n}", [P, T], F32, tag)
             nc.sync.dma_start(out=gates[n][:], in_=gT[n * P : (n + 1) * P, :])
 
         def scatter(n, j0, count):
             if n >= 2:
                 y = y_late[:, n - 2, j0 : j0 + count]
-            elif count == CH:
-                y = y_early[j0 // CH][:, n, :]
             else:
-                y = y_early["half"][:, n, :]
+                y = y_early[j0 // CH][:, n, :]
             nc.vector.tensor_tensor(win[n % NWIN][:].indirect(entries(dst_list, j0, count)), y, gg[n][:, j0 : j0 + count], MULT)
 
         def store(n):
             nc.sync.dma_start(out=out[n * P : (n + 1) * P, :], in_=win[n % NWIN][:])
 
-        def gather_gates_into(n, tag):
-            gg[n] = keep.tile([P, J], F32, name=f"gg{n}", tag=tag, align_bytes=64)[:, :]
-            gather_gates(n)
-
-        gather_scales(0, "gs0")
+        gather_scales(0)
         nc.sync.dma_start(out=wdw[:].bitcast(I32), in_=wd_words[0].bitcast(I32))
         load_planes(4, wd_scales, 1)
         gather_words(0)
-        wgo_t = keep.tile([P, J], F32, name="wgo_t", tag="gs0", align_bytes=64)
+        wgo_t = tile("wgo_t", [P, J], F32, "gs0")
         nc.sync.dma_start(out=wgo_t[:], in_=wgo)
-        load_gates(2, "gw0")
-        gather_scales(1, "gs1")
+        load_gates(2, None)
+        gather_scales(1)
         load_gates(1, "tabs")
         gather_words(1)
         load_gates(0, "gw1")
         gather_words(2)
         gather_words(3)
-        load_gates(3, "gw3")
-        clear_window(1, "tabw")
-        gather_gates_into(2, "gg2")
+        load_gates(3, "tabw")
+        clear_window(1, nc.gpsimd)
+        clear_window(2, nc.gpsimd)
+        gather_gates(2)
+        gather_gates(1)
         hi0 = stage1(0)
         hi1 = stage1(1)
-        quantise(0, hi0, "gw0")
-        gather_gates_into(1, "hi0")
+        quantise(0, hi0)
+        gather_gates(0)
         stage2(0)
-        quantise(1, hi1, "tabs")
-        gather_gates_into(0, "hi1")
+        quantise(1, hi1)
         hi2 = stage1(2)
         stage2(1)
-        quantise(2, hi2, "gw1")
+        for n in range(2):
+            scatter(n, 0, CH)
+        gather_gates(3)
+        quantise(2, hi2)
         hi3 = stage1(3)
         stage2(2)
-        quantise(3, hi3, "hq3")
+        quantise(3, hi3)
         stage2(3)
         for c in range(NCH):
             stage2_late(c)
-        for c in range(2):
+        for c in range(1, NCH):
             for n in range(2):
                 scatter(n, c * CH, CH)
-        scatter(0, 2 * CH, CH)
-        scatter(0, 3 * CH, CH)
-        store(0)
-        scatter(1, HALF, HALF)
-        store(1)
-        gather_gates_into(3, "hi1")
+                if c == NCH - 1:
+                    store(n)
         for n in (2, 3):
             scatter(n, 0, J)
             store(n)

@@ -25,7 +25,6 @@ NWIN = 3
 BATCH = ((0, CH), (CH, J - CH))
 AT = {
     "gw0": 0, "gs1": 0, "gates2": 1536, "hq0": 4096,
-    "gw3": 18432 - 1024, "win1": 18432 - 8192, "win2": 18432,
     "hb0": 30720, "gg0": 30720 + 1024 - 4096, "y_early3": 30720 + 1024,
     "hb1": 40960, "y_early0": 40960, "gg3": 40960 + 1024 - 4096,
 }
@@ -66,14 +65,15 @@ def tile_list_msg_tanh_gate_kernel(
         gg = {}
         gates = {}
 
-        def clear_window(w, engine):
-            win[w] = tile(f"win{w}", [P, T], F32)
+        def clear_window(w, engine, tag=None):
+            win[w] = tile(f"win{w}", [P, T], F32, tag)
             engine.memset(win[w][:].bitcast(I32), 0)
 
         nc.vector.memset(planes[:].rearrange("p a n -> p (a n)").bitcast(I32), 0)
         for first, last in ((0, 32), (64, 128)):
             nc.vector.memset(tabs[first:last, :].bitcast(I32), 0)
         clear_window(0, nc.vector)
+        clear_window(1, nc.gpsimd)
         make_identity(nc, ident[:])
 
         nc.sync.dma_start(src_list[:], offs)
@@ -217,8 +217,6 @@ def tile_list_msg_tanh_gate_kernel(
         gather_words(2)
         gather_words(3)
         load_gates(3, "tabw")
-        clear_window(1, nc.gpsimd)
-        clear_window(2, nc.gpsimd)
         gather_gates(2)
         gather_gates(1)
         hi0 = stage1(0)
@@ -233,6 +231,7 @@ def tile_list_msg_tanh_gate_kernel(
             scatter(n, 0, CH)
         gather_gates(3)
         quantise(2, hi2)
+        clear_window(2, nc.gpsimd, "hi2")
         hi3 = stage1(3)
         stage2(2)
         quantise(3, hi3)

@@ -22,11 +22,12 @@ CH = 256
 NCH = J // CH
 HALF = J // 2
 NWIN = 3
-BATCH = ((0, CH), (CH, J - CH))
+BATCH = ((0, HALF), (HALF, HALF))
 AT = {
-    "gw0": 0, "gs1": 0, "gates2": 1536, "hq0": 4096,
-    "hb0": 30720, "gg0": 30720 + 1024 - 4096, "y_early3": 30720 + 1024,
-    "hb1": 40960, "y_early0": 40960, "gg3": 40960 + 1024 - 4096,
+    "gates1": 2560, "gw0a": 10240, "gw1a": 10752, "gs1": 10752, "sm_t": 17920, "gates2": 17984,
+    "gates3": 26624, "gw2": 34304, "gw0b": 34304 + 1536, "gw1b": 34304 + 1536, "gw3": 34304 + 2048, "win0": 34304 + 3584,
+    "hb0": 51200, "gg1": 51200 + 1024 - 4096, "gg0": 51200 + 1024,
+    "hb1": 61440, "gg3": 61440 + 1024 - 4096, "y_early0": 61440 + 1024,
 }
 
 
@@ -51,18 +52,17 @@ def tile_list_msg_tanh_gate_kernel(
         tabw = keep.tile([P, T], I32, name="tabw", tag="tabw", align_bytes=64)
         wsw = keep.tile([P, 4 * R], U8, name="wsw", align_bytes=64)
         wtw = keep.tile([P, 8 * R], U8, name="wtw", align_bytes=64)
-        wdw = keep.tile([P, 2 * N], U8, name="wdw", align_bytes=64)
-        tabs = keep.tile([P, T], U8, name="tabs", tag="tabs", align_bytes=64)
+        tabs = tile("tabs", [P, T], U8)
         planes = keep.tile([P, 5, R], U8, name="planes", align_bytes=64)
-        sm_t = keep.tile([P, 4], F32, name="sm_t")
         ident = keep.tile([P, P], F32, name="ident")
-        lifted = [keep.tile([P, 2, 2, BATCH[h][1]], U8, name=f"lifted{h}", align_bytes=64) for h in range(2)]
-        gw = [tile(f"gw{c}", [P, 2, CH], I32) for c in range(NCH)]
+        lifted = [keep.tile([P, 2, BATCH[h][1]], U8, name=f"lifted{h}", align_bytes=64) for h in range(2)]
         vw = [keep.tile([P, 2, 2 * 2 * CH], U8, name=f"vw{c}", align_bytes=64) for c in range(NCH)]
         win = {}
         y_late = keep.tile([P, 2, J], F32, name="y_late")
         y_early = {}
         gg = {}
+        gw = {}
+        gs = {}
         gates = {}
 
         def clear_window(w, engine, tag=None):
@@ -70,46 +70,54 @@ def tile_list_msg_tanh_gate_kernel(
             engine.memset(win[w][:].bitcast(I32), 0)
 
         nc.vector.memset(planes[:].rearrange("p a n -> p (a n)").bitcast(I32), 0)
-        for first, last in ((0, 32), (64, 128)):
-            nc.vector.memset(tabs[first:last, :].bitcast(I32), 0)
-        clear_window(0, nc.vector)
-        clear_window(1, nc.gpsimd)
+        nc.gpsimd.memset(tabs[:].bitcast(I32), 0)
+        for h in range(2):
+            nc.gpsimd.memset(lifted[h][96:128, :, :].rearrange("p l n -> p (l n)").bitcast(I32), 0)
         make_identity(nc, ident[:])
 
         nc.sync.dma_start(src_list[:], offs)
         nc.sync.dma_start(dst_list[:], offs2)
-        nc.sync.dma_start(out=tabs[32:64, :].bitcast(I32), in_=tab_scales.rearrange("a r t -> (a r) t").bitcast(I32))
+        for q in range(4):
+            nc.sync.dma_start(out=tabs[32 * q : 32 * q + 8, :].bitcast(I32), in_=tab_scales[:, 4 * q : 4 * q + 4, :].bitcast(I32))
         nc.sync.dma_start(out=tabw[:], in_=tab_words[0].rearrange("p t b -> p (t b)").bitcast(I32))
 
-        def load_planes(first, rows, passes):
+        def load_planes(dst, first, rows, passes):
             for q in range(4):
                 nc.sync.dma_start(
-                    out=planes[32 * q : 32 * q + 4, first : first + passes, :].bitcast(I32),
+                    out=dst[32 * q : 32 * q + 4, first : first + passes, :].bitcast(I32),
                     in_=rows[:, 4 * q : 4 * q + 4, :].rearrange("a r n -> r a n").bitcast(I32),
                 )
 
-        load_planes(0, ws_scales, 2)
-        load_planes(2, wt_scales, 2)
+        load_planes(planes, 0, ws_scales, 2)
         nc.sync.dma_start(out=wsw[:].bitcast(I32).rearrange("p (a n) -> p a n", a=2), in_=ws_words.rearrange("a p n -> p a n").bitcast(I32))
         nc.sync.dma_start(out=wtw[:].bitcast(I32).rearrange("p (a n) -> p a n", a=2), in_=wt_words.rearrange("a p n b -> p a (n b)").bitcast(I32))
-        nc.sync.dma_start(out=sm_t[:], in_=sm.rearrange("(p t) -> p t", t=4))
+        load_planes(planes, 2, wt_scales, 2)
 
         def entries(lst, j0, count):
             return lst[:, j0 // 16 : (j0 + count) // 16]
 
         def gather_scales(h):
-            gs = tile(f"gs{h}", [P, 2, BATCH[h][1]], U8)
+            gs[h] = tile(f"gs{h}", [P, 2, BATCH[h][1]], U8)
             for l in range(2):
-                nc.vector.tensor_copy(gs[:, l, :], tabs[:].indirect(entries(lists[l], *BATCH[h])))
-            for a in range(2):
-                for q in range(4):
-                    first, count = 32 + 16 * a + 4 * q, 32
-                    nc.sync.dma_start(
-                        out=lifted[h][32 * q : 32 * q + count, a, :, :].rearrange("p l n -> p (l n)").bitcast(I32),
-                        in_=gs[first : first + count, :, :].rearrange("p l n -> p (l n)").bitcast(I32),
-                    )
+                nc.vector.tensor_copy(gs[h][:, l, :], tabs[:].indirect(entries(lists[l], *BATCH[h])))
+            for first, count in ((0, 64), (64, 32), (96, 4)):
+                nc.sync.dma_start(
+                    out=lifted[h][first : first + count, :, :].rearrange("p l n -> p (l n)").bitcast(I32),
+                    in_=gs[h][first + 4 : first + 4 + count, :, :].rearrange("p l n -> p (l n)").bitcast(I32),
+                )
+
+        def gather_words_by_list(c):
+            words = (tile(f"gw{c}a", [P, 8 * CH if c == 0 else CH], I32), tile(f"gw{c}b", [P, CH], I32))
+            for l in range(2):
+                nc.vector.tensor_copy(words[l][:, 0:CH].bitcast(U32), tabw[:].bitcast(U32).indirect(entries(lists[l], c * CH, CH)))
+            for l in range(2):
+                nc.vector.tensor_copy(
+                    vw[c][:, :, 2 * l * CH : 2 * (l + 1) * CH].bitcast(U16),
+                    words[l][:, 0:CH].bitcast(U16).rearrange("p (j a) -> p a j", a=2),
+                )
 
         def gather_words(c):
+            gw[c] = tile(f"gw{c}", [P, 2, CH], I32)
             for l in range(2):
                 nc.vector.tensor_copy(gw[c][:, l, :].bitcast(U32), tabw[:].bitcast(U32).indirect(entries(lists[l], c * CH, CH)))
             nc.vector.tensor_copy(
@@ -122,13 +130,13 @@ def tile_list_msg_tanh_gate_kernel(
             nc.vector.tensor_tensor(gg[n], gates[n][:].indirect(src_list[:]), wgo_t[:], MULT)
 
         def stage1(c):
-            h = min(c, 1)
+            h = c // 2
             base = c * CH - BATCH[h][0]
             th = ring.tile([P, CH // P, 4, P], F32, name="th")
-            for u in range(CH // P):
-                acc = psum.tile([P, R], F32, name="acc", tag="acc")
-                for a in range(2):
-                    plane = lifted[h][:, a, :, :]
+            acc = [psum.tile([P, R], F32, name="acc", tag="acc") for u in range(CH // P)]
+            for a in range(2):
+                plane = (gs, lifted)[a][h]
+                for u in range(CH // P):
                     for l in range(2):
                         j0 = l * CH + u * P
                         if l == 0:
@@ -136,7 +144,7 @@ def tile_list_msg_tanh_gate_kernel(
                         else:
                             w = wtw[:, a * 4 * R : (a + 1) * 4 * R].bitcast(FP8X4)
                         nc.tensor.matmul_mx(
-                            out=acc[:],
+                            out=acc[u][:],
                             lhsT=vw[c][:, a, 2 * j0 : 2 * (j0 + P)].bitcast(FP4X4),
                             lhsT_scale=plane[:, l, base + u * P : base + (u + 1) * P],
                             rhs=w,
@@ -144,7 +152,8 @@ def tile_list_msg_tanh_gate_kernel(
                             start=(a == 0 and l == 0),
                             stop=(a == 1 and l == 1),
                         )
-                nc.scalar.activation(th[:, u, :, :], acc[:].rearrange("p (m t) -> p t m", t=4), ACT.Tanh)
+            for u in range(CH // P):
+                nc.scalar.activation(th[:, u, :, :], acc[u][:].rearrange("p (m t) -> p t m", t=4), ACT.Tanh)
             hb = tile(f"hb{c}", [P, 4, CH], BF16)
             for pair in range(2):
                 ht = psum.tile([P, 2, CH], F32, name="ht", tag=f"mid{c % 2}{pair}", bufs=1)
@@ -184,13 +193,13 @@ def tile_list_msg_tanh_gate_kernel(
             nc.scalar.copy(y_early[c], yt[:])
 
         def stage2_late(c):
-            yt = psum.tile([P, 2, CH], F32, name="yt_late", tag="acc")
+            yt = psum.tile([P, 2, CH], F32, name="yt_late", tag=f"mid1{1 - c % 2}", bufs=1)
             for n in range(2):
                 second_product(2 + n, c, yt[:, n, :])
             nc.scalar.copy(y_late[:, :, c * CH : (c + 1) * CH], yt[:])
 
-        def load_gates(n, tag):
-            gates[n] = tile(f"gates{n}", [P, T], F32, tag)
+        def load_gates(n):
+            gates[n] = tile(f"gates{n}", [P, T], F32, "tabs" if n == 0 else None)
             nc.sync.dma_start(out=gates[n][:], in_=gT[n * P : (n + 1) * P, :])
 
         def scatter(n, j0, count):
@@ -204,41 +213,48 @@ def tile_list_msg_tanh_gate_kernel(
             nc.sync.dma_start(out=out[n * P : (n + 1) * P, :], in_=win[n % NWIN][:])
 
         gather_scales(0)
+        wdw = tile("wdw", [P, 2 * N], U8)
         nc.sync.dma_start(out=wdw[:].bitcast(I32), in_=wd_words[0].bitcast(I32))
-        load_planes(4, wd_scales, 1)
-        gather_words(0)
-        wgo_t = tile("wgo_t", [P, J], F32, "gs0")
+        load_planes(planes, 4, wd_scales, 1)
+        gather_words_by_list(0)
+        sm_t = tile("sm_t", [P, 4], F32)
+        nc.sync.dma_start(out=sm_t[:], in_=sm.rearrange("(p t) -> p t", t=4))
+        wgo_t = tile("wgo_t", [P, J], F32)
         nc.sync.dma_start(out=wgo_t[:], in_=wgo)
-        load_gates(2, None)
+        load_gates(2)
+        load_gates(1)
+        gather_words_by_list(1)
         gather_scales(1)
-        load_gates(1, "tabs")
-        gather_words(1)
-        load_gates(0, "gw1")
+        load_gates(0)
         gather_words(2)
+        load_gates(3)
         gather_words(3)
-        load_gates(3, "tabw")
+        clear_window(0, nc.gpsimd)
         gather_gates(2)
-        gather_gates(1)
         hi0 = stage1(0)
         hi1 = stage1(1)
         quantise(0, hi0)
+        clear_window(1, nc.gpsimd, "hi0")
+        gather_gates(1)
         gather_gates(0)
         stage2(0)
         quantise(1, hi1)
+        gather_gates(3)
         hi2 = stage1(2)
         stage2(1)
         for n in range(2):
             scatter(n, 0, CH)
-        gather_gates(3)
         quantise(2, hi2)
-        clear_window(2, nc.gpsimd, "hi2")
         hi3 = stage1(3)
         stage2(2)
+        for n in range(2):
+            scatter(n, CH, CH)
         quantise(3, hi3)
+        clear_window(2, nc.gpsimd, "hi3")
         stage2(3)
         for c in range(NCH):
             stage2_late(c)
-        for c in range(1, NCH):
+        for c in range(2, NCH):
             for n in range(2):
                 scatter(n, c * CH, CH)
                 if c == NCH - 1:

@@ -21,13 +21,14 @@ P = 128
 CH = 256
 NCH = J // CH
 HALF = J // 2
-NWIN = 3
+NWIN = 4
 BATCH = ((0, HALF), (HALF, HALF))
 AT = {
     "gates1": 2560, "gw0a": 10240, "gw1a": 10752, "gs1": 10752, "sm_t": 17920, "gates2": 17984,
     "gates3": 26624, "gw2": 34304, "gw0b": 34304 + 1536, "gw1b": 34304 + 1536, "gw3": 34304 + 2048, "win0": 34304 + 3584,
     "hb0": 51200, "gg1": 51200 + 1024 - 4096, "gg0": 51200 + 1024,
     "hb1": 61440, "gg3": 61440 + 1024 - 4096, "y_early0": 61440 + 1024,
+    "hi1": 73728, "win2": 73728 + 1024 - 8192, "win3": 73728 + 1024,
 }
 
 
@@ -193,7 +194,7 @@ def tile_list_msg_tanh_gate_kernel(
             nc.scalar.copy(y_early[c], yt[:])
 
         def stage2_late(c):
-            yt = psum.tile([P, 2, CH], F32, name="yt_late", tag=f"mid1{1 - c % 2}", bufs=1)
+            yt = psum.tile([P, 2, CH], F32, name="yt_late", tag=f"mid{(c + 1) % 2}1", bufs=1)
             for n in range(2):
                 second_product(2 + n, c, yt[:, n, :])
             nc.scalar.copy(y_late[:, :, c * CH : (c + 1) * CH], yt[:])
@@ -238,27 +239,30 @@ def tile_list_msg_tanh_gate_kernel(
         gather_gates(1)
         gather_gates(0)
         stage2(0)
+        stage2_late(0)
         quantise(1, hi1)
+        clear_window(2, nc.gpsimd)
+        clear_window(3, nc.gpsimd)
         gather_gates(3)
         hi2 = stage1(2)
         stage2(1)
-        for n in range(2):
+        stage2_late(1)
+        for n in range(4):
             scatter(n, 0, CH)
         quantise(2, hi2)
         hi3 = stage1(3)
         stage2(2)
-        for n in range(2):
+        stage2_late(2)
+        for n in range(4):
             scatter(n, CH, CH)
         quantise(3, hi3)
-        clear_window(2, nc.gpsimd, "hi3")
         stage2(3)
-        for c in range(NCH):
-            stage2_late(c)
+        stage2_late(3)
         for c in range(2, NCH):
             for n in range(2):
                 scatter(n, c * CH, CH)
                 if c == NCH - 1:
                     store(n)
         for n in (2, 3):
-            scatter(n, 0, J)
+            scatter(n, HALF, HALF)
             store(n)

@@ -22,13 +22,16 @@ CH = 256
 NCH = J // CH
 HALF = J // 2
 NWIN = 4
+PIECES = ((0, CH), (CH, CH), (HALF, HALF))
+SUM_BANKS = (0, 2, 6, 2)
+TURN_BANKS = (4, 6, 4, 6)
 BATCH = ((0, HALF), (HALF, HALF))
 AT = {
     "gates1": 2560, "gw0a": 10240, "gw1a": 10752, "gs1": 10752, "sm_t": 17920, "gates2": 17984,
-    "gates3": 26624, "gw2": 34304, "gw0b": 34304 + 1536, "gw1b": 34304 + 1536, "gw3": 34304 + 2048, "win0": 34304 + 3584,
-    "hb0": 51200, "gg1": 51200 + 1024 - 4096, "gg0": 51200 + 1024,
-    "hb1": 61440, "gg3": 61440 + 1024 - 4096, "y_early0": 61440 + 1024,
-    "hi1": 73728, "win2": 73728 + 1024 - 8192, "win3": 73728 + 1024,
+    "gates3": 61440 - 8192, "gw2a": 34304, "gw0b": 34304 + 1536, "gw1b": 34304 + 1536, "gw2b": 34304 + 2048, "win1": 34304 + 3584,
+    "win2": 17984,
+    "tabs": 61440 - 1024, "gates0": 61440, "wd_rows": 61440 - 8192 - 512, "hq0": 61440 - 8192 - 2048,
+    "hb3": 71680, "y03": 71680 + 1024,
 }
 
 
@@ -40,7 +43,7 @@ def tile_list_msg_tanh_gate_kernel(
         keep = ctx.enter_context(tc.tile_pool(name="keep", bufs=1))
         lay = ctx.enter_context(tc.tile_pool(name="lay", bufs=1))
         ring = ctx.enter_context(tc.tile_pool(name="ring", bufs=2))
-        psum = ctx.enter_context(tc.psum_pool(name="psum", bufs=2))
+        psum = ctx.enter_context(tc.psum_pool(name="psum", bufs=1))
 
         def tile(name, shape, dtype, tag=None):
             if name in AT:
@@ -57,12 +60,11 @@ def tile_list_msg_tanh_gate_kernel(
         planes = keep.tile([P, 5, R], U8, name="planes", align_bytes=64)
         ident = keep.tile([P, P], F32, name="ident")
         lifted = [keep.tile([P, 2, BATCH[h][1]], U8, name=f"lifted{h}", align_bytes=64) for h in range(2)]
-        vw = [keep.tile([P, 2, 2 * 2 * CH], U8, name=f"vw{c}", align_bytes=64) for c in range(NCH)]
+        vw = [[keep.tile([P, 2, 2 * count], U8, name=f"vw{i}{l}", align_bytes=64) for l in range(2)] for i, (j0, count) in enumerate(PIECES)]
         win = {}
-        y_late = keep.tile([P, 2, J], F32, name="y_late")
-        y_early = {}
+        y = {}
+        hi = [keep.tile([P, HALF, 4], BF16, name=f"hi{h}", tag=f"hi{h}", align_bytes=64) for h in range(2)]
         gg = {}
-        gw = {}
         gs = {}
         gates = {}
 
@@ -71,6 +73,7 @@ def tile_list_msg_tanh_gate_kernel(
             engine.memset(win[w][:].bitcast(I32), 0)
 
         nc.vector.memset(planes[:].rearrange("p a n -> p (a n)").bitcast(I32), 0)
+        clear_window(0, nc.vector)
         nc.gpsimd.memset(tabs[:].bitcast(I32), 0)
         for h in range(2):
             nc.gpsimd.memset(lifted[h][96:128, :, :].rearrange("p l n -> p (l n)").bitcast(I32), 0)
@@ -107,24 +110,13 @@ def tile_list_msg_tanh_gate_kernel(
                     in_=gs[h][first + 4 : first + 4 + count, :, :].rearrange("p l n -> p (l n)").bitcast(I32),
                 )
 
-        def gather_words_by_list(c):
-            words = (tile(f"gw{c}a", [P, 8 * CH if c == 0 else CH], I32), tile(f"gw{c}b", [P, CH], I32))
+        def gather_words(i):
+            j0, count = PIECES[i]
+            words = (tile(f"gw{i}a", [P, 8 * CH if i == 0 else count], I32), tile(f"gw{i}b", [P, count], I32))
             for l in range(2):
-                nc.vector.tensor_copy(words[l][:, 0:CH].bitcast(U32), tabw[:].bitcast(U32).indirect(entries(lists[l], c * CH, CH)))
+                nc.vector.tensor_copy(words[l][:, 0:count].bitcast(U32), tabw[:].bitcast(U32).indirect(entries(lists[l], j0, count)))
             for l in range(2):
-                nc.vector.tensor_copy(
-                    vw[c][:, :, 2 * l * CH : 2 * (l + 1) * CH].bitcast(U16),
-                    words[l][:, 0:CH].bitcast(U16).rearrange("p (j a) -> p a j", a=2),
-                )
-
-        def gather_words(c):
-            gw[c] = tile(f"gw{c}", [P, 2, CH], I32)
-            for l in range(2):
-                nc.vector.tensor_copy(gw[c][:, l, :].bitcast(U32), tabw[:].bitcast(U32).indirect(entries(lists[l], c * CH, CH)))
-            nc.vector.tensor_copy(
-                vw[c][:].bitcast(U16),
-                gw[c][:].rearrange("p l j -> p (l j)").bitcast(U16).rearrange("p (j a) -> p a j", a=2),
-            )
+                nc.vector.tensor_copy(vw[i][l][:].bitcast(U16), words[l][:, 0:count].bitcast(U16).rearrange("p (j a) -> p a j", a=2))
 
         def gather_gates(n):
             gg[n] = tile(f"gg{n}", [P, J], F32)[:, :]
@@ -134,19 +126,19 @@ def tile_list_msg_tanh_gate_kernel(
             h = c // 2
             base = c * CH - BATCH[h][0]
             th = ring.tile([P, CH // P, 4, P], F32, name="th")
-            acc = [psum.tile([P, R], F32, name="acc", tag="acc") for u in range(CH // P)]
+            acc = [psum.tile([P, R], F32, name="acc", tag=f"bank{SUM_BANKS[c] + u}") for u in range(CH // P)]
             for a in range(2):
                 plane = (gs, lifted)[a][h]
                 for u in range(CH // P):
                     for l in range(2):
-                        j0 = l * CH + u * P
+                        j0 = c * CH + u * P - PIECES[min(c, 2)][0]
                         if l == 0:
                             w = wsw[:, a * 2 * R : (a + 1) * 2 * R].bitcast(FP4X4)
                         else:
                             w = wtw[:, a * 4 * R : (a + 1) * 4 * R].bitcast(FP8X4)
                         nc.tensor.matmul_mx(
                             out=acc[u][:],
-                            lhsT=vw[c][:, a, 2 * j0 : 2 * (j0 + P)].bitcast(FP4X4),
+                            lhsT=vw[min(c, 2)][l][:, a, 2 * j0 : 2 * (j0 + P)].bitcast(FP4X4),
                             lhsT_scale=plane[:, l, base + u * P : base + (u + 1) * P],
                             rhs=w,
                             rhs_scale=planes[:, 2 * l + a, :],
@@ -157,58 +149,44 @@ def tile_list_msg_tanh_gate_kernel(
                 nc.scalar.activation(th[:, u, :, :], acc[u][:].rearrange("p (m t) -> p t m", t=4), ACT.Tanh)
             hb = tile(f"hb{c}", [P, 4, CH], BF16)
             for pair in range(2):
-                ht = psum.tile([P, 2, CH], F32, name="ht", tag=f"mid{c % 2}{pair}", bufs=1)
+                ht = psum.tile([P, 2, CH], F32, name="ht", tag=f"bank{TURN_BANKS[c] + pair}")
                 for tt in range(2):
                     for u in range(CH // P):
                         nc.tensor.transpose(ht[:, tt, u * P : (u + 1) * P], th[:, u, 2 * pair + tt, :], ident[:])
                 for tt in range(2):
                     t = 2 * pair + tt
                     nc.scalar.activation(hb[:, t, :], ht[:, tt, :], ACT.Copy, scale=sm_t[:, t : t + 1])
-            hi = tile(f"hi{c}", [P, CH, 4], BF16)
-            nc.scalar.copy(hi[:].rearrange("p (c i) t -> p c t i", i=4), hb[:].rearrange("p t (c i) -> p c t i", i=4))
-            return hi
+            nc.scalar.copy(hi[h][:, base : base + CH, :].rearrange("p (c i) t -> p c t i", i=4), hb[:].rearrange("p t (c i) -> p c t i", i=4))
 
         hq = {}
         hs = keep.tile([P, J], U8, name="hs", align_bytes=64)
 
-        def quantise(c, hi):
-            hq[c] = tile(f"hq{c}", [P, CH], U32)
-            nc.vector.quantize_mx(out=hq[c][:].bitcast(FP8X4), scales=hs[:, c * CH : (c + 1) * CH], in_=hi[:].rearrange("p j t -> p (j t)"))
+        def quantise(h):
+            hq[h] = tile(f"hq{h}", [P, HALF], U32)
+            nc.vector.quantize_mx(out=hq[h][:].bitcast(FP8X4), scales=hs[:, h * HALF : (h + 1) * HALF], in_=hi[h][:].rearrange("p j t -> p (j t)"))
 
-        def second_product(n, c, bank):
+        def stage2(h, n, bank):
+            yt = psum.tile([P, HALF], F32, name="yt", tag=f"bank{bank}")
             nc.tensor.matmul_mx(
-                out=bank,
+                out=yt[:],
                 lhsT=wdw[:, 2 * n * P : 2 * (n + 1) * P].bitcast(FP4X4),
                 lhsT_scale=planes[:, 4, n * P : (n + 1) * P],
-                rhs=hq[c][:].bitcast(FP8X4),
-                rhs_scale=hs[:, c * CH : (c + 1) * CH],
+                rhs=hq[h][:].bitcast(FP8X4),
+                rhs_scale=hs[:, h * HALF : (h + 1) * HALF],
                 start=True,
                 stop=True,
             )
+            y[h, n] = tile(f"y{h}{n}", [P, HALF], F32)
+            nc.scalar.copy(y[h, n][:], yt[:])
 
-        def stage2(c):
-            y_early[c] = tile(f"y_early{c}", [P, 2, CH], F32, f"hb{c + 1}")[:, :, :]
-            yt = psum.tile([P, 2, CH], F32, name="yt", tag=f"mid{(c + 1) % 2}0", bufs=1)
-            for n in range(2):
-                second_product(n, c, yt[:, n, :])
-            nc.scalar.copy(y_early[c], yt[:])
+        def load_gates(n, first=0, count=T):
+            if first == 0:
+                gates[n] = tile(f"gates{n}", [P, T], F32)
+            nc.sync.dma_start(out=gates[n][:, first : first + count], in_=gT[n * P : (n + 1) * P, first : first + count])
 
-        def stage2_late(c):
-            yt = psum.tile([P, 2, CH], F32, name="yt_late", tag=f"mid{(c + 1) % 2}1", bufs=1)
-            for n in range(2):
-                second_product(2 + n, c, yt[:, n, :])
-            nc.scalar.copy(y_late[:, :, c * CH : (c + 1) * CH], yt[:])
-
-        def load_gates(n):
-            gates[n] = tile(f"gates{n}", [P, T], F32, "tabs" if n == 0 else None)
-            nc.sync.dma_start(out=gates[n][:], in_=gT[n * P : (n + 1) * P, :])
-
-        def scatter(n, j0, count):
-            if n >= 2:
-                y = y_late[:, n - 2, j0 : j0 + count]
-            else:
-                y = y_early[j0 // CH][:, n, :]
-            nc.vector.tensor_tensor(win[n % NWIN][:].indirect(entries(dst_list, j0, count)), y, gg[n][:, j0 : j0 + count], MULT)
+        def scatter(h, n):
+            j0 = h * HALF
+            nc.vector.tensor_tensor(win[n][:].indirect(entries(dst_list, j0, HALF)), y[h, n][:], gg[n][:, j0 : j0 + HALF], MULT)
 
         def store(n):
             nc.sync.dma_start(out=out[n * P : (n + 1) * P, :], in_=win[n % NWIN][:])
@@ -216,53 +194,44 @@ def tile_list_msg_tanh_gate_kernel(
         gather_scales(0)
         wdw = tile("wdw", [P, 2 * N], U8)
         nc.sync.dma_start(out=wdw[:].bitcast(I32), in_=wd_words[0].bitcast(I32))
-        load_planes(planes, 4, wd_scales, 1)
-        gather_words_by_list(0)
+        wd_rows = tile("wd_rows", [P, N], U8)
+        nc.sync.dma_start(out=wd_rows[0:16, :].bitcast(I32), in_=wd_scales[0].bitcast(I32))
+        gather_words(0)
         sm_t = tile("sm_t", [P, 4], F32)
         nc.sync.dma_start(out=sm_t[:], in_=sm.rearrange("(p t) -> p t", t=4))
         wgo_t = tile("wgo_t", [P, J], F32)
         nc.sync.dma_start(out=wgo_t[:], in_=wgo)
         load_gates(2)
         load_gates(1)
-        gather_words_by_list(1)
+        gather_words(1)
         gather_scales(1)
+        load_gates(3, 0, T // 2)
         load_gates(0)
+        for q in range(4):
+            nc.sync.dma_start(out=planes[32 * q : 32 * q + 4, 4, :].bitcast(I32), in_=wd_rows[4 * q : 4 * q + 4, :].bitcast(I32))
+        load_gates(3, T // 2, T // 2)
         gather_words(2)
-        load_gates(3)
-        gather_words(3)
-        clear_window(0, nc.gpsimd)
+        clear_window(1, nc.gpsimd)
         gather_gates(2)
-        hi0 = stage1(0)
-        hi1 = stage1(1)
-        quantise(0, hi0)
-        clear_window(1, nc.gpsimd, "hi0")
+        clear_window(2, nc.gpsimd)
         gather_gates(1)
         gather_gates(0)
-        stage2(0)
-        stage2_late(0)
-        quantise(1, hi1)
-        clear_window(2, nc.gpsimd)
-        clear_window(3, nc.gpsimd)
+        stage1(0)
+        stage1(1)
+        quantise(0)
+        clear_window(3, nc.gpsimd, "hi0")
         gather_gates(3)
-        hi2 = stage1(2)
-        stage2(1)
-        stage2_late(1)
+        for n, bank in enumerate((2, 3, 0)):
+            stage2(0, n, bank)
+        stage1(2)
+        for n in range(3):
+            scatter(0, n)
+        stage1(3)
+        quantise(1)
+        stage2(0, 3, 1)
+        scatter(0, 3)
+        for n, bank in enumerate((4, 5, 0, 2)):
+            stage2(1, n, bank)
         for n in range(4):
-            scatter(n, 0, CH)
-        quantise(2, hi2)
-        hi3 = stage1(3)
-        stage2(2)
-        stage2_late(2)
-        for n in range(4):
-            scatter(n, CH, CH)
-        quantise(3, hi3)
-        stage2(3)
-        stage2_late(3)
-        for c in range(2, NCH):
-            for n in range(2):
-                scatter(n, c * CH, CH)
-                if c == NCH - 1:
-                    store(n)
-        for n in (2, 3):
-            scatter(n, HALF, HALF)
+            scatter(1, n)
             store(n)

@@ -28,9 +28,10 @@ TURN_BANKS = (4, 6, 4, 6)
 BATCH = ((0, HALF), (HALF, HALF))
 AT = {
     "gates1": 2560, "gw0a": 10240, "gw1a": 10752, "gs1": 10752, "sm_t": 17920, "gates2": 17984,
-    "gates3": 61440 - 8192, "gw2a": 34304, "gw0b": 34304 + 1536, "gw1b": 34304 + 1536, "gw2b": 34304 + 2048, "win1": 34304 + 3584,
-    "win2": 17984,
+    "gates3": 61440 - 8192, "gw2a": 34304, "gw0b": 34304 + 1536, "gw1b": 34304 + 1536, "gw2b": 34304 + 2048, "win0": 34304 + 3584,
+    "win1": 17984,
     "tabs": 61440 - 1024, "gates0": 61440, "wd_rows": 61440 - 8192 - 512, "hq0": 61440 - 8192 - 2048,
+    "hi0": 90112, "win2": 90112 + 2048 - 8192, "win3": 90112 + 2048,
     "hb3": 71680, "y03": 71680 + 1024,
 }
 
@@ -63,7 +64,7 @@ def tile_list_msg_tanh_gate_kernel(
         vw = [[keep.tile([P, 2, 2 * count], U8, name=f"vw{i}{l}", align_bytes=64) for l in range(2)] for i, (j0, count) in enumerate(PIECES)]
         win = {}
         y = {}
-        hi = [keep.tile([P, HALF, 4], BF16, name=f"hi{h}", tag=f"hi{h}", align_bytes=64) for h in range(2)]
+        hi = [tile(f"hi{h}", [P, HALF, 4], BF16) for h in range(2)]
         gg = {}
         gs = {}
         gates = {}
@@ -73,7 +74,6 @@ def tile_list_msg_tanh_gate_kernel(
             engine.memset(win[w][:].bitcast(I32), 0)
 
         nc.vector.memset(planes[:].rearrange("p a n -> p (a n)").bitcast(I32), 0)
-        clear_window(0, nc.vector)
         nc.gpsimd.memset(tabs[:].bitcast(I32), 0)
         for h in range(2):
             nc.gpsimd.memset(lifted[h][96:128, :, :].rearrange("p l n -> p (l n)").bitcast(I32), 0)
@@ -211,15 +211,16 @@ def tile_list_msg_tanh_gate_kernel(
             nc.sync.dma_start(out=planes[32 * q : 32 * q + 4, 4, :].bitcast(I32), in_=wd_rows[4 * q : 4 * q + 4, :].bitcast(I32))
         load_gates(3, T // 2, T // 2)
         gather_words(2)
-        clear_window(1, nc.gpsimd)
+        clear_window(0, nc.gpsimd)
         gather_gates(2)
-        clear_window(2, nc.gpsimd)
+        clear_window(1, nc.gpsimd)
         gather_gates(1)
         gather_gates(0)
         stage1(0)
         stage1(1)
         quantise(0)
-        clear_window(3, nc.gpsimd, "hi0")
+        clear_window(2, nc.gpsimd)
+        clear_window(3, nc.gpsimd)
         gather_gates(3)
         for n, bank in enumerate((2, 3, 0)):
             stage2(0, n, bank)

@@ -23,16 +23,17 @@ NCH = J // CH
 HALF = J // 2
 NWIN = 4
 PIECES = ((0, CH), (CH, CH), (HALF, HALF))
-SUM_BANKS = (0, 2, 6, 2)
-TURN_BANKS = (4, 6, 4, 6)
+SUM_BANKS = (0, 2, 4, 6)
+TURN_BANKS = (4, 6, 0, 2)
 BATCH = ((0, HALF), (HALF, HALF))
 AT = {
     "gates1": 2560, "gw0a": 10240, "gw1a": 10752, "gs1": 10752, "sm_t": 17920, "gates2": 17984,
     "gates3": 61440 - 8192, "gw2a": 34304, "gw0b": 34304 + 1536, "gw1b": 34304 + 1536, "gw2b": 34304 + 2048, "win0": 34304 + 3584,
     "win1": 17984,
-    "tabs": 61440 - 1024, "gates0": 61440, "wd_rows": 61440 - 8192 - 512, "hq0": 61440 - 8192 - 2048,
-    "hi0": 90112, "win2": 90112 + 2048 - 8192, "win3": 90112 + 2048,
-    "hb3": 71680, "y03": 71680 + 1024,
+    "tabs": 61440 - 1024, "gates0": 61440, "wd_rows": 61440 - 8192 - 512, "hq0": 61440 - 8192 - 1024,
+    "hi0": 92160, "win2": 92160 + 1024 - 8192, "win3": 92160 + 1024,
+    "y00": 71680, "hq1": 71680, "hb3": 79872, "y10": 79872 - 960, "y11": 79872 + 64, "y12": 79872 + 1088, "hq2": 79872 + 64 - 2048,
+    "hi2": 61440 - 8192 - 1024 - 4096 + 64,
 }
 
 
@@ -64,7 +65,8 @@ def tile_list_msg_tanh_gate_kernel(
         vw = [[keep.tile([P, 2, 2 * count], U8, name=f"vw{i}{l}", align_bytes=64) for l in range(2)] for i, (j0, count) in enumerate(PIECES)]
         win = {}
         y = {}
-        hi = [tile(f"hi{h}", [P, HALF, 4], BF16) for h in range(2)]
+        hi = {}
+        rounded = {}
         gg = {}
         gs = {}
         gates = {}
@@ -156,37 +158,54 @@ def tile_list_msg_tanh_gate_kernel(
                 for tt in range(2):
                     t = 2 * pair + tt
                     nc.scalar.activation(hb[:, t, :], ht[:, tt, :], ACT.Copy, scale=sm_t[:, t : t + 1])
-            nc.scalar.copy(hi[h][:, base : base + CH, :].rearrange("p (c i) t -> p c t i", i=4), hb[:].rearrange("p t (c i) -> p c t i", i=4))
+            rounded[c] = hb
+
+        def interleave(c):
+            i = min(c, 2)
+            base = c * CH - PIECES[i][0]
+            if base == 0:
+                hi[i] = tile(f"hi{i}", [P, PIECES[i][1], 4], BF16)
+            nc.scalar.copy(hi[i][:, base : base + CH, :].rearrange("p (c i) t -> p c t i", i=4), rounded[c][:].rearrange("p t (c i) -> p c t i", i=4))
 
         hq = {}
         hs = keep.tile([P, J], U8, name="hs", align_bytes=64)
 
-        def quantise(h):
-            hq[h] = tile(f"hq{h}", [P, HALF], U32)
-            nc.vector.quantize_mx(out=hq[h][:].bitcast(FP8X4), scales=hs[:, h * HALF : (h + 1) * HALF], in_=hi[h][:].rearrange("p j t -> p (j t)"))
+        def quantise(i):
+            j0, count = PIECES[i]
+            hq[i] = tile(f"hq{i}", [P, count], U32)
+            nc.vector.quantize_mx(out=hq[i][:].bitcast(FP8X4), scales=hs[:, j0 : j0 + count], in_=hi[i][:].rearrange("p j t -> p (j t)"))
 
-        def stage2(h, n, bank):
-            yt = psum.tile([P, HALF], F32, name="yt", tag=f"bank{bank}")
-            nc.tensor.matmul_mx(
-                out=yt[:],
-                lhsT=wdw[:, 2 * n * P : 2 * (n + 1) * P].bitcast(FP4X4),
-                lhsT_scale=planes[:, 4, n * P : (n + 1) * P],
-                rhs=hq[h][:].bitcast(FP8X4),
-                rhs_scale=hs[:, h * HALF : (h + 1) * HALF],
-                start=True,
-                stop=True,
-            )
-            y[h, n] = tile(f"y{h}{n}", [P, HALF], F32)
-            nc.scalar.copy(y[h, n][:], yt[:])
+        def stage2(i, blocks, bank, joint=False):
+            j0, count = PIECES[i]
+            yt = psum.tile([P, len(blocks) * count], F32, name="yt", tag=f"bank{bank}")
+            for b, n in enumerate(blocks):
+                nc.tensor.matmul_mx(
+                    out=yt[:, b * count : (b + 1) * count],
+                    lhsT=wdw[:, 2 * n * P : 2 * (n + 1) * P].bitcast(FP4X4),
+                    lhsT_scale=planes[:, 4, n * P : (n + 1) * P],
+                    rhs=hq[i][:].bitcast(FP8X4),
+                    rhs_scale=hs[:, j0 : j0 + count],
+                    start=True,
+                    stop=True,
+                )
+            if joint:
+                both = tile(f"y{i}{blocks[0]}", [P, len(blocks) * count], F32)
+                nc.scalar.copy(both[:], yt[:])
+            for b, n in enumerate(blocks):
+                if joint:
+                    y[i, n] = both[:, b * count : (b + 1) * count]
+                else:
+                    y[i, n] = tile(f"y{i}{n}", [P, count], F32)[:, :]
+                    nc.scalar.copy(y[i, n], yt[:, b * count : (b + 1) * count])
 
         def load_gates(n, first=0, count=T):
             if first == 0:
                 gates[n] = tile(f"gates{n}", [P, T], F32)
             nc.sync.dma_start(out=gates[n][:, first : first + count], in_=gT[n * P : (n + 1) * P, first : first + count])
 
-        def scatter(h, n):
-            j0 = h * HALF
-            nc.vector.tensor_tensor(win[n][:].indirect(entries(dst_list, j0, HALF)), y[h, n][:], gg[n][:, j0 : j0 + HALF], MULT)
+        def scatter(i, n):
+            j0, count = PIECES[i]
+            nc.vector.tensor_tensor(win[n][:].indirect(entries(dst_list, j0, count)), y[i, n], gg[n][:, j0 : j0 + count], MULT)
 
         def store(n):
             nc.sync.dma_start(out=out[n * P : (n + 1) * P, :], in_=win[n % NWIN][:])
@@ -216,23 +235,33 @@ def tile_list_msg_tanh_gate_kernel(
         clear_window(1, nc.gpsimd)
         gather_gates(1)
         gather_gates(0)
-        stage1(0)
-        stage1(1)
+        for c in range(2):
+            stage1(c)
+            interleave(c)
         quantise(0)
         clear_window(2, nc.gpsimd)
         clear_window(3, nc.gpsimd)
         gather_gates(3)
-        for n, bank in enumerate((2, 3, 0)):
-            stage2(0, n, bank)
+        stage2(0, (0, 1), 2)
+        stage2(0, (2, 3), 3, True)
         stage1(2)
-        for n in range(3):
-            scatter(0, n)
-        stage1(3)
+        interleave(2)
+        scatter(0, 0)
+        scatter(0, 1)
         quantise(1)
-        stage2(0, 3, 1)
+        scatter(0, 2)
         scatter(0, 3)
-        for n, bank in enumerate((4, 5, 0, 2)):
-            stage2(1, n, bank)
+        stage1(3)
+        interleave(3)
+        stage2(1, (0, 1), 4)
+        stage2(1, (2, 3), 5, True)
+        scatter(1, 0)
+        scatter(1, 1)
+        quantise(2)
+        scatter(1, 2)
+        scatter(1, 3)
+        for n, bank in enumerate((6, 7, 0, 1)):
+            stage2(2, (n,), bank)
         for n in range(4):
-            scatter(1, n)
+            scatter(2, n)
             store(n)

@@ -25,14 +25,13 @@ NWIN = 4
 PIECES = ((0, CH), (CH, CH), (HALF, HALF))
 SUM_BANKS = (0, 2, 4, 6)
 TURN_BANKS = (4, 6, 0, 2)
-BATCH = ((0, HALF), (HALF, HALF))
 AT = {
-    "gates1": 2560, "gw0a": 10240, "gw1a": 10752, "gs1": 10752, "sm_t": 17920, "gates2": 17984,
-    "gates3": 61440 - 8192, "gw2a": 34304, "gw0b": 34304 + 1536, "gw1b": 34304 + 1536, "gw2b": 34304 + 2048, "win0": 34304 + 3584,
-    "win1": 17984,
-    "tabs": 61440 - 1024, "gates0": 61440, "wd_rows": 61440 - 8192 - 512, "hq0": 61440 - 8192 - 1024,
+    "gates0": 2560, "gw0a": 10240, "gw1a": 10752, "sm_t": 17920, "gates3": 17984,
+    "gates2": 61440 - 8192, "gw2a": 34304, "gw0b": 34304 + 1536, "gw1b": 34304 + 1536, "gw2b": 34304 + 2048, "win0": 34304 + 3584,
+    "win1": 61440 - 8192,
+    "tabs": 61440 - 1024, "gates1": 61440, "wd_rows": 61440 - 8192 - 512, "hq0": 61440 - 8192 - 1024,
     "hi0": 92160, "win2": 92160 + 1024 - 8192, "win3": 92160 + 1024,
-    "y00": 71680, "hq1": 71680, "hb3": 79872, "y10": 79872 - 960, "y11": 79872 + 64, "y12": 79872 + 1088, "hq2": 79872 + 64 - 2048,
+    "y00": 71680, "hq1": 71680, "hb2": 76800, "y10": 76800 - 960, "y11": 76800 + 64, "hq2": 76800 + 64 - 2048, "hb3": 79872, "y12": 79872,
     "hi2": 61440 - 8192 - 1024 - 4096 + 64,
 }
 
@@ -44,7 +43,6 @@ def tile_list_msg_tanh_gate_kernel(
     with ExitStack() as ctx:
         keep = ctx.enter_context(tc.tile_pool(name="keep", bufs=1))
         lay = ctx.enter_context(tc.tile_pool(name="lay", bufs=1))
-        ring = ctx.enter_context(tc.tile_pool(name="ring", bufs=2))
         psum = ctx.enter_context(tc.psum_pool(name="psum", bufs=1))
 
         def tile(name, shape, dtype, tag=None):
@@ -61,14 +59,13 @@ def tile_list_msg_tanh_gate_kernel(
         tabs = tile("tabs", [P, T], U8)
         planes = keep.tile([P, 5, R], U8, name="planes", align_bytes=64)
         ident = keep.tile([P, P], F32, name="ident")
-        lifted = [keep.tile([P, 2, BATCH[h][1]], U8, name=f"lifted{h}", align_bytes=64) for h in range(2)]
+        lifted = keep.tile([P, 2, 2 * J], U8, name="lifted", align_bytes=64)
         vw = [[keep.tile([P, 2, 2 * count], U8, name=f"vw{i}{l}", align_bytes=64) for l in range(2)] for i, (j0, count) in enumerate(PIECES)]
         win = {}
         y = {}
         hi = {}
         rounded = {}
         gg = {}
-        gs = {}
         gates = {}
 
         def clear_window(w, engine, tag=None):
@@ -76,15 +73,13 @@ def tile_list_msg_tanh_gate_kernel(
             engine.memset(win[w][:].bitcast(I32), 0)
 
         nc.vector.memset(planes[:].rearrange("p a n -> p (a n)").bitcast(I32), 0)
-        nc.gpsimd.memset(tabs[:].bitcast(I32), 0)
-        for h in range(2):
-            nc.gpsimd.memset(lifted[h][96:128, :, :].rearrange("p l n -> p (l n)").bitcast(I32), 0)
+        nc.gpsimd.memset(tabs[0:96, :].bitcast(I32), 0)
+        nc.vector.memset(lifted[:].rearrange("p a n -> p (a n)").bitcast(I32), 0)
         make_identity(nc, ident[:])
 
         nc.sync.dma_start(src_list[:], offs)
+        nc.sync.dma_start(out=tabs[96:128, :].bitcast(I32), in_=tab_scales.rearrange("a q t -> (a q) t").bitcast(I32))
         nc.sync.dma_start(dst_list[:], offs2)
-        for q in range(4):
-            nc.sync.dma_start(out=tabs[32 * q : 32 * q + 8, :].bitcast(I32), in_=tab_scales[:, 4 * q : 4 * q + 4, :].bitcast(I32))
         nc.sync.dma_start(out=tabw[:], in_=tab_words[0].rearrange("p t b -> p (t b)").bitcast(I32))
 
         def load_planes(dst, first, rows, passes):
@@ -102,15 +97,14 @@ def tile_list_msg_tanh_gate_kernel(
         def entries(lst, j0, count):
             return lst[:, j0 // 16 : (j0 + count) // 16]
 
-        def gather_scales(h):
-            gs[h] = tile(f"gs{h}", [P, 2, BATCH[h][1]], U8)
+        def gather_scales():
+            picked = tile("picked", [P, 2 * J], U8)
             for l in range(2):
-                nc.vector.tensor_copy(gs[h][:, l, :], tabs[:].indirect(entries(lists[l], *BATCH[h])))
-            for first, count in ((0, 64), (64, 32), (96, 4)):
-                nc.sync.dma_start(
-                    out=lifted[h][first : first + count, :, :].rearrange("p l n -> p (l n)").bitcast(I32),
-                    in_=gs[h][first + 4 : first + 4 + count, :, :].rearrange("p l n -> p (l n)").bitcast(I32),
-                )
+                nc.vector.tensor_copy(picked[:, l * J : (l + 1) * J], tabs[:].indirect(lists[l][:]))
+            for a in range(2):
+                for q in range(4):
+                    row = 96 + 16 * a + 4 * q
+                    nc.sync.dma_start(out=lifted[32 * q : 32 * q + 4, a, :].bitcast(I32), in_=picked[row : row + 4, :].bitcast(I32))
 
         def gather_words(i):
             j0, count = PIECES[i]
@@ -125,13 +119,10 @@ def tile_list_msg_tanh_gate_kernel(
             nc.vector.tensor_tensor(gg[n], gates[n][:].indirect(src_list[:]), wgo_t[:], MULT)
 
         def stage1(c):
-            h = c // 2
-            base = c * CH - BATCH[h][0]
-            th = ring.tile([P, CH // P, 4, P], F32, name="th")
+            th = keep.tile([P, CH // P, 4, P], F32, name="th", tag="th1" if c == 1 else "th0")
             acc = [psum.tile([P, R], F32, name="acc", tag=f"bank{SUM_BANKS[c] + u}") for u in range(CH // P)]
-            for a in range(2):
-                plane = (gs, lifted)[a][h]
-                for u in range(CH // P):
+            for u in range(CH // P):
+                for a in range(2):
                     for l in range(2):
                         j0 = c * CH + u * P - PIECES[min(c, 2)][0]
                         if l == 0:
@@ -141,7 +132,7 @@ def tile_list_msg_tanh_gate_kernel(
                         nc.tensor.matmul_mx(
                             out=acc[u][:],
                             lhsT=vw[min(c, 2)][l][:, a, 2 * j0 : 2 * (j0 + P)].bitcast(FP4X4),
-                            lhsT_scale=plane[:, l, base + u * P : base + (u + 1) * P],
+                            lhsT_scale=lifted[:, a, l * J + c * CH + u * P : l * J + c * CH + (u + 1) * P],
                             rhs=w,
                             rhs_scale=planes[:, 2 * l + a, :],
                             start=(a == 0 and l == 0),
@@ -210,20 +201,19 @@ def tile_list_msg_tanh_gate_kernel(
         def store(n):
             nc.sync.dma_start(out=out[n * P : (n + 1) * P, :], in_=win[n % NWIN][:])
 
-        gather_scales(0)
+        wgo_t = tile("wgo_t", [P, J], F32)
+        nc.sync.dma_start(out=wgo_t[:], in_=wgo)
         wdw = tile("wdw", [P, 2 * N], U8)
         nc.sync.dma_start(out=wdw[:].bitcast(I32), in_=wd_words[0].bitcast(I32))
         wd_rows = tile("wd_rows", [P, N], U8)
         nc.sync.dma_start(out=wd_rows[0:16, :].bitcast(I32), in_=wd_scales[0].bitcast(I32))
+        gather_scales()
+        load_gates(2)
+        load_gates(1)
         gather_words(0)
         sm_t = tile("sm_t", [P, 4], F32)
         nc.sync.dma_start(out=sm_t[:], in_=sm.rearrange("(p t) -> p t", t=4))
-        wgo_t = tile("wgo_t", [P, J], F32)
-        nc.sync.dma_start(out=wgo_t[:], in_=wgo)
-        load_gates(2)
-        load_gates(1)
         gather_words(1)
-        gather_scales(1)
         load_gates(3, 0, T // 2)
         load_gates(0)
         for q in range(4):
@@ -242,8 +232,8 @@ def tile_list_msg_tanh_gate_kernel(
         clear_window(2, nc.gpsimd)
         clear_window(3, nc.gpsimd)
         gather_gates(3)
-        stage2(0, (0, 1), 2)
-        stage2(0, (2, 3), 3, True)
+        stage2(0, (0, 1), 0)
+        stage2(0, (2, 3), 1, True)
         stage1(2)
         interleave(2)
         scatter(0, 0)
@@ -251,9 +241,9 @@ def tile_list_msg_tanh_gate_kernel(
         quantise(1)
         scatter(0, 2)
         scatter(0, 3)
+        stage2(1, (0, 1), 4)
         stage1(3)
         interleave(3)
-        stage2(1, (0, 1), 4)
         stage2(1, (2, 3), 5, True)
         scatter(1, 0)
         scatter(1, 1)

@@ -1,7 +1,6 @@
 from contextlib import ExitStack
 
 import concourse.mybir as mybir
-from concourse.masks import make_identity
 
 K, R, N, T, J = 1024, 512, 512, 2048, 1024
 FLOPS = 2 * J * (2 * K * R + R * N)
@@ -18,21 +17,23 @@ ACT = mybir.ActivationFunctionType
 MULT = mybir.AluOpType.mult
 
 P = 128
-CH = 256
-NCH = J // CH
-HALF = J // 2
-NWIN = 4
-PIECES = ((0, CH), (CH, CH), (HALF, HALF))
-SUM_BANKS = (0, 2, 4, 6)
-TURN_BANKS = (4, 6, 0, 2)
+BANK = 512
+PIECES = ((0, 256), (256, 256), (512, 512))
+BANKS = {"sums": ((0, 1), (2, 3), (0, 1, 4, 5)), "yt": ((4, 5), (4, 5), (2, 3, 6, 7))}
+ROW = 4 * T
+GATES_AT = 4096
+WINS_AT = GATES_AT + 4 * ROW + 2 * N
+REST_AT = WINS_AT + 4 * ROW
 AT = {
-    "gates0": 2560, "gw0a": 10240, "gw1a": 10752, "sm_t": 17920, "gates3": 17984,
-    "gates2": 61440 - 8192, "gw2a": 34304, "gw0b": 34304 + 1536, "gw1b": 34304 + 1536, "gw2b": 34304 + 2048, "win0": 34304 + 3584,
-    "win1": 61440 - 8192,
-    "tabs": 61440 - 1024, "gates1": 61440, "wd_rows": 61440 - 8192 - 512, "hq0": 61440 - 8192 - 1024,
-    "hi0": 92160, "win2": 92160 + 1024 - 8192, "win3": 92160 + 1024,
-    "y00": 71680, "hq1": 71680, "hb2": 76800, "y10": 76800 - 960, "y11": 76800 + 64, "hq2": 76800 + 64 - 2048, "hb3": 79872, "y12": 79872,
-    "hi2": 61440 - 8192 - 1024 - 4096 + 64,
+    "raw": 0, "lifted": 0,
+    "wt_raw": GATES_AT + ROW - 64,
+    "gates0": GATES_AT, "gates1": GATES_AT + ROW, "wdw": GATES_AT + 2 * ROW,
+    "gates2": GATES_AT + 2 * ROW + 2 * N, "gates3": GATES_AT + 3 * ROW + 2 * N,
+    "win0": WINS_AT, "win1": WINS_AT + ROW, "win2": WINS_AT + 2 * ROW, "win3": WINS_AT + 3 * ROW,
+    "gw01": WINS_AT + ROW, "gw11": WINS_AT + ROW, "gw21": WINS_AT + ROW,
+    "hi0": WINS_AT + 2 * ROW, "hi1": WINS_AT + 3 * ROW,
+    "hq0": REST_AT, "hq1": REST_AT,
+    "hb2": REST_AT + 2048, "y12": REST_AT + 2048,
 }
 
 
@@ -53,205 +54,199 @@ def tile_list_msg_tanh_gate_kernel(
         src_list = keep.tile([P, J // 16], U16, name="src_list")
         dst_list = keep.tile([P, J // 16], U16, name="dst_list")
         lists = (src_list, dst_list)
-        tabw = keep.tile([P, T], I32, name="tabw", tag="tabw", align_bytes=64)
-        wsw = keep.tile([P, 4 * R], U8, name="wsw", align_bytes=64)
-        wtw = keep.tile([P, 8 * R], U8, name="wtw", align_bytes=64)
+        tabw = tile("tabw", [P, T], I32)
         tabs = tile("tabs", [P, T], U8)
-        planes = keep.tile([P, 5, R], U8, name="planes", align_bytes=64)
-        ident = keep.tile([P, P], F32, name="ident")
-        lifted = keep.tile([P, 2, 2 * J], U8, name="lifted", align_bytes=64)
-        vw = [[keep.tile([P, 2, 2 * count], U8, name=f"vw{i}{l}", align_bytes=64) for l in range(2)] for i, (j0, count) in enumerate(PIECES)]
-        win = {}
-        y = {}
-        hi = {}
-        rounded = {}
-        gg = {}
-        gates = {}
+        raw = tile("raw", [P, 5, R], U8)
+        planes = tile("planes", [P, 5 * R], U8)
+        ws_raw = tile("ws_raw", [P, 4 * R], U8)
+        wt_raw = tile("wt_raw", [P, 2 * ROW + 2 * N + 128], U8)
+        wsw = tile("wsw", [P, 4 * R], U8)
+        wtw = tile("wtw", [P, 8 * R], U8)
+        wgo_t = tile("wgo_t", [P, J], F32)
+        sm_t = tile("sm_t", [P, 4], F32)
 
-        def clear_window(w, engine, tag=None):
-            win[w] = tile(f"win{w}", [P, T], F32, tag)
-            engine.memset(win[w][:].bitcast(I32), 0)
-
-        nc.vector.memset(planes[:].rearrange("p a n -> p (a n)").bitcast(I32), 0)
+        win = {0: tile("win0", [P, T], F32)}
         nc.gpsimd.memset(tabs[0:96, :].bitcast(I32), 0)
-        nc.vector.memset(lifted[:].rearrange("p a n -> p (a n)").bitcast(I32), 0)
-        make_identity(nc, ident[:])
+        nc.gpsimd.memset(raw[0:112, :, :].rearrange("p a n -> p (a n)").bitcast(I32), 0)
+        nc.vector.memset(win[0][:].bitcast(I32), 0)
 
         nc.sync.dma_start(src_list[:], offs)
         nc.sync.dma_start(out=tabs[96:128, :].bitcast(I32), in_=tab_scales.rearrange("a q t -> (a q) t").bitcast(I32))
         nc.sync.dma_start(dst_list[:], offs2)
+        for first, rows, passes in ((0, ws_scales, 2), (2, wt_scales, 2), (4, wd_scales, 1)):
+            nc.sync.dma_start(out=raw[112:128, first : first + passes, :].bitcast(I32), in_=rows.rearrange("a q n -> q a n").bitcast(I32))
         nc.sync.dma_start(out=tabw[:], in_=tab_words[0].rearrange("p t b -> p (t b)").bitcast(I32))
+        nc.sync.dma_start(out=ws_raw[:].bitcast(I32).rearrange("p (a n) -> p a n", a=2), in_=ws_words.rearrange("a p n -> p a n").bitcast(I32))
+        nc.sync.dma_start(out=wt_raw[:, 0 : 8 * R].bitcast(I32).rearrange("p (a n) -> p a n", a=2), in_=wt_words.rearrange("a p n b -> p a (n b)").bitcast(I32))
+        nc.sync.dma_start(out=wgo_t[:], in_=wgo)
+        nc.sync.dma_start(out=sm_t[:], in_=sm.rearrange("(p t) -> p t", t=4))
 
-        def load_planes(dst, first, rows, passes):
-            for q in range(4):
-                nc.sync.dma_start(
-                    out=dst[32 * q : 32 * q + 4, first : first + passes, :].bitcast(I32),
-                    in_=rows[:, 4 * q : 4 * q + 4, :].rearrange("a r n -> r a n").bitcast(I32),
-                )
+        nc.gpsimd.tensor_copy(
+            planes[:, 0 : 4 * R].rearrange("p (a t m) -> p a t m", a=4, t=4), raw[:, 0:4, :].rearrange("p a (m t) -> p a t m", t=4)
+        )
+        nc.gpsimd.tensor_copy(planes[:, 4 * R : 5 * R].bitcast(I32), raw[:, 4, :].bitcast(I32))
+        for q in range(4):
+            nc.sync.dma_start(out=planes[32 * q : 32 * q + 4, :].bitcast(I32), in_=planes[112 + 4 * q : 116 + 4 * q, :].bitcast(I32))
+        lifted = tile("lifted", [P, 2, 2 * J], U8)
+        nc.gpsimd.memset(lifted[:].rearrange("p a n -> p (a n)").bitcast(I32), 0)
 
-        load_planes(planes, 0, ws_scales, 2)
-        nc.sync.dma_start(out=wsw[:].bitcast(I32).rearrange("p (a n) -> p a n", a=2), in_=ws_words.rearrange("a p n -> p a n").bitcast(I32))
-        nc.sync.dma_start(out=wtw[:].bitcast(I32).rearrange("p (a n) -> p a n", a=2), in_=wt_words.rearrange("a p n b -> p a (n b)").bitcast(I32))
-        load_planes(planes, 2, wt_scales, 2)
+        nc.scalar.copy(
+            wsw[:].bitcast(U16).rearrange("p (a t m) -> p a t m", a=2, t=4), ws_raw[:].bitcast(U16).rearrange("p (a m t) -> p a t m", a=2, t=4)
+        )
+        nc.scalar.copy(
+            wtw[:].bitcast(U32).rearrange("p (a t m) -> p a t m", a=2, t=4), wt_raw[:, 0 : 8 * R].bitcast(U32).rearrange("p (a m t) -> p a t m", a=2, t=4)
+        )
 
         def entries(lst, j0, count):
             return lst[:, j0 // 16 : (j0 + count) // 16]
 
-        def gather_scales():
-            picked = tile("picked", [P, 2 * J], U8)
-            for l in range(2):
-                nc.vector.tensor_copy(picked[:, l * J : (l + 1) * J], tabs[:].indirect(lists[l][:]))
+        picked = tile("picked", [P, 2 * J], U8)
+        for l in range(2):
+            nc.vector.tensor_copy(picked[:, l * J : (l + 1) * J], tabs[:].indirect(lists[l][:]))
+        for q in range(4):
             for a in range(2):
-                for q in range(4):
-                    row = 96 + 16 * a + 4 * q
-                    nc.sync.dma_start(out=lifted[32 * q : 32 * q + 4, a, :].bitcast(I32), in_=picked[row : row + 4, :].bitcast(I32))
+                row = 96 + 16 * a + 4 * q
+                nc.sync.dma_start(out=lifted[32 * q : 32 * q + 4, a, :].bitcast(I32), in_=picked[row : row + 4, :].bitcast(I32))
 
-        def gather_words(i):
-            j0, count = PIECES[i]
-            words = (tile(f"gw{i}a", [P, 8 * CH if i == 0 else count], I32), tile(f"gw{i}b", [P, count], I32))
+        gates = [tile(f"gates{n}", [P, T], F32) for n in range(4)]
+        for n in range(4):
+            nc.sync.dma_start(out=gates[n][:], in_=gT[n * P : (n + 1) * P, :])
+        wdw = tile("wdw", [P, 2 * N], U8)
+        nc.sync.dma_start(out=wdw[:].bitcast(I32), in_=wd_words[0].bitcast(I32))
+
+        vw = {}
+        for i, (j0, count) in enumerate(PIECES):
+            words = [tile(f"gw{i}{l}", [P, count], I32, f"gw{l}") for l in range(2)]
             for l in range(2):
-                nc.vector.tensor_copy(words[l][:, 0:count].bitcast(U32), tabw[:].bitcast(U32).indirect(entries(lists[l], j0, count)))
+                nc.vector.tensor_copy(words[l][:].bitcast(U32), tabw[:].bitcast(U32).indirect(entries(lists[l], j0, count)))
             for l in range(2):
-                nc.vector.tensor_copy(vw[i][l][:].bitcast(U16), words[l][:, 0:count].bitcast(U16).rearrange("p (j a) -> p a j", a=2))
+                vw[i, l] = tile(f"vw{i}{l}", [P, 2, 2 * count], U8)
+                nc.vector.tensor_copy(vw[i, l][:].bitcast(U16), words[l][:].bitcast(U16).rearrange("p (j a) -> p a j", a=2))
+
+        gg, sums, hb, hi, hq, yt, y = {}, {}, {}, {}, {}, {}, {}
+        hs = tile("hs", [P, J], U8)
+
+        def clear_window(n):
+            win[n] = tile(f"win{n}", [P, T], F32)
+            nc.gpsimd.memset(win[n][:].bitcast(I32), 0)
 
         def gather_gates(n):
-            gg[n] = tile(f"gg{n}", [P, J], F32)[:, :]
-            nc.vector.tensor_tensor(gg[n], gates[n][:].indirect(src_list[:]), wgo_t[:], MULT)
+            gg[n] = tile(f"gg{n}", [P, J], F32)
+            nc.vector.tensor_tensor(gg[n][:], gates[n][:].indirect(src_list[:]), wgo_t[:], MULT)
 
-        def stage1(c):
-            th = keep.tile([P, CH // P, 4, P], F32, name="th", tag="th1" if c == 1 else "th0")
-            acc = [psum.tile([P, R], F32, name="acc", tag=f"bank{SUM_BANKS[c] + u}") for u in range(CH // P)]
-            for u in range(CH // P):
-                for a in range(2):
-                    for l in range(2):
-                        j0 = c * CH + u * P - PIECES[min(c, 2)][0]
+        def place(tiles, name, i, t):
+            count = PIECES[i][1]
+            b, first = divmod(t * count, BANK)
+            if first == 0:
+                tiles[i, b] = psum.tile([P, BANK], F32, name=name, tag=f"bank{BANKS[name][i][b]}")
+            return tiles[i, b][:, first : first + count]
+
+        def product1(i, ts):
+            j0, count = PIECES[i]
+            for t in ts:
+                acc = place(sums, "sums", i, t)
+                for l in range(2):
+                    for a in range(2):
+                        col = a * R + t * P
                         if l == 0:
-                            w = wsw[:, a * 2 * R : (a + 1) * 2 * R].bitcast(FP4X4)
+                            w = wsw[:, 2 * col : 2 * (col + P)].bitcast(FP4X4)
                         else:
-                            w = wtw[:, a * 4 * R : (a + 1) * 4 * R].bitcast(FP8X4)
+                            w = wtw[:, 4 * col : 4 * (col + P)].bitcast(FP8X4)
                         nc.tensor.matmul_mx(
-                            out=acc[u][:],
-                            lhsT=vw[min(c, 2)][l][:, a, 2 * j0 : 2 * (j0 + P)].bitcast(FP4X4),
-                            lhsT_scale=lifted[:, a, l * J + c * CH + u * P : l * J + c * CH + (u + 1) * P],
-                            rhs=w,
-                            rhs_scale=planes[:, 2 * l + a, :],
+                            out=acc,
+                            lhsT=w,
+                            lhsT_scale=planes[:, 2 * l * R + col : 2 * l * R + col + P],
+                            rhs=vw[i, l][:, a, :].bitcast(FP4X4),
+                            rhs_scale=lifted[:, a, l * J + j0 : l * J + j0 + count],
                             start=(a == 0 and l == 0),
                             stop=(a == 1 and l == 1),
                         )
-            for u in range(CH // P):
-                nc.scalar.activation(th[:, u, :, :], acc[u][:].rearrange("p (m t) -> p t m", t=4), ACT.Tanh)
-            hb = tile(f"hb{c}", [P, 4, CH], BF16)
-            for pair in range(2):
-                ht = psum.tile([P, 2, CH], F32, name="ht", tag=f"bank{TURN_BANKS[c] + pair}")
-                for tt in range(2):
-                    for u in range(CH // P):
-                        nc.tensor.transpose(ht[:, tt, u * P : (u + 1) * P], th[:, u, 2 * pair + tt, :], ident[:])
-                for tt in range(2):
-                    t = 2 * pair + tt
-                    nc.scalar.activation(hb[:, t, :], ht[:, tt, :], ACT.Copy, scale=sm_t[:, t : t + 1])
-            rounded[c] = hb
 
-        def interleave(c):
-            i = min(c, 2)
-            base = c * CH - PIECES[i][0]
-            if base == 0:
-                hi[i] = tile(f"hi{i}", [P, PIECES[i][1], 4], BF16)
-            nc.scalar.copy(hi[i][:, base : base + CH, :].rearrange("p (c i) t -> p c t i", i=4), rounded[c][:].rearrange("p t (c i) -> p c t i", i=4))
+        def activate(i, ts):
+            count = PIECES[i][1]
+            if ts[0] == 0:
+                hb[i] = tile(f"hb{i}", [P, 4, count], BF16)
+            th = tile(f"th{i}{ts[0]}", [P, BANK], F32)
+            nc.scalar.activation(th[:], sums[i, ts[0] * count // BANK][:], ACT.Tanh)
+            for t in ts:
+                first = (t - ts[0]) * count
+                nc.scalar.activation(hb[i][:, t, :], th[:, first : first + count], ACT.Copy, scale=sm_t[:, t : t + 1])
 
-        hq = {}
-        hs = keep.tile([P, J], U8, name="hs", align_bytes=64)
+        def interleave(i):
+            count = PIECES[i][1]
+            hi[i] = tile(f"hi{i}", [P, 4 * count], BF16)
+            nc.scalar.copy(
+                hi[i][:].rearrange("p (c i t) -> p c t i", i=4, t=4), hb[i][:].rearrange("p t (c i) -> p c t i", i=4)
+            )
 
         def quantise(i):
             j0, count = PIECES[i]
             hq[i] = tile(f"hq{i}", [P, count], U32)
-            nc.vector.quantize_mx(out=hq[i][:].bitcast(FP8X4), scales=hs[:, j0 : j0 + count], in_=hi[i][:].rearrange("p j t -> p (j t)"))
+            nc.vector.quantize_mx(out=hq[i][:].bitcast(FP8X4), scales=hs[:, j0 : j0 + count], in_=hi[i][:])
 
-        def stage2(i, blocks, bank, joint=False):
+        def product2(i, blocks, joint=False):
             j0, count = PIECES[i]
-            yt = psum.tile([P, len(blocks) * count], F32, name="yt", tag=f"bank{bank}")
-            for b, n in enumerate(blocks):
+            made = {}
+            for n in blocks:
+                made[n] = place(yt, "yt", i, n)
                 nc.tensor.matmul_mx(
-                    out=yt[:, b * count : (b + 1) * count],
+                    out=made[n],
                     lhsT=wdw[:, 2 * n * P : 2 * (n + 1) * P].bitcast(FP4X4),
-                    lhsT_scale=planes[:, 4, n * P : (n + 1) * P],
+                    lhsT_scale=planes[:, 4 * R + n * P : 4 * R + (n + 1) * P],
                     rhs=hq[i][:].bitcast(FP8X4),
                     rhs_scale=hs[:, j0 : j0 + count],
                     start=True,
                     stop=True,
                 )
             if joint:
-                both = tile(f"y{i}{blocks[0]}", [P, len(blocks) * count], F32)
-                nc.scalar.copy(both[:], yt[:])
+                both = tile(f"y{i}{blocks[0]}", [P, BANK], F32)
+                nc.scalar.copy(both[:], yt[i, blocks[0] * count // BANK][:])
             for b, n in enumerate(blocks):
                 if joint:
                     y[i, n] = both[:, b * count : (b + 1) * count]
                 else:
                     y[i, n] = tile(f"y{i}{n}", [P, count], F32)[:, :]
-                    nc.scalar.copy(y[i, n], yt[:, b * count : (b + 1) * count])
-
-        def load_gates(n, first=0, count=T):
-            if first == 0:
-                gates[n] = tile(f"gates{n}", [P, T], F32)
-            nc.sync.dma_start(out=gates[n][:, first : first + count], in_=gT[n * P : (n + 1) * P, first : first + count])
+                    nc.scalar.copy(y[i, n], made[n])
 
         def scatter(i, n):
             j0, count = PIECES[i]
             nc.vector.tensor_tensor(win[n][:].indirect(entries(dst_list, j0, count)), y[i, n], gg[n][:, j0 : j0 + count], MULT)
 
-        def store(n):
-            nc.sync.dma_start(out=out[n * P : (n + 1) * P, :], in_=win[n % NWIN][:])
-
-        wgo_t = tile("wgo_t", [P, J], F32)
-        nc.sync.dma_start(out=wgo_t[:], in_=wgo)
-        wdw = tile("wdw", [P, 2 * N], U8)
-        nc.sync.dma_start(out=wdw[:].bitcast(I32), in_=wd_words[0].bitcast(I32))
-        wd_rows = tile("wd_rows", [P, N], U8)
-        nc.sync.dma_start(out=wd_rows[0:16, :].bitcast(I32), in_=wd_scales[0].bitcast(I32))
-        gather_scales()
-        load_gates(2)
-        load_gates(1)
-        gather_words(0)
-        sm_t = tile("sm_t", [P, 4], F32)
-        nc.sync.dma_start(out=sm_t[:], in_=sm.rearrange("(p t) -> p t", t=4))
-        gather_words(1)
-        load_gates(3, 0, T // 2)
-        load_gates(0)
-        for q in range(4):
-            nc.sync.dma_start(out=planes[32 * q : 32 * q + 4, 4, :].bitcast(I32), in_=wd_rows[4 * q : 4 * q + 4, :].bitcast(I32))
-        load_gates(3, T // 2, T // 2)
-        gather_words(2)
-        clear_window(0, nc.gpsimd)
-        gather_gates(2)
-        clear_window(1, nc.gpsimd)
-        gather_gates(1)
+        clear_window(1)
         gather_gates(0)
-        for c in range(2):
-            stage1(c)
-            interleave(c)
+        gather_gates(1)
+        for i in range(2):
+            product1(i, (0, 1, 2, 3))
+            activate(i, (0, 1))
+            activate(i, (2, 3))
+            interleave(i)
+        product1(2, (0, 1))
+        activate(2, (0,))
+        activate(2, (1,))
         quantise(0)
-        clear_window(2, nc.gpsimd)
-        clear_window(3, nc.gpsimd)
+        clear_window(2)
+        product2(0, (0, 1))
+        product2(0, (2, 3), True)
+        gather_gates(2)
         gather_gates(3)
-        stage2(0, (0, 1), 0)
-        stage2(0, (2, 3), 1, True)
-        stage1(2)
-        interleave(2)
-        scatter(0, 0)
-        scatter(0, 1)
         quantise(1)
-        scatter(0, 2)
-        scatter(0, 3)
-        stage2(1, (0, 1), 4)
-        stage1(3)
-        interleave(3)
-        stage2(1, (2, 3), 5, True)
+        clear_window(3)
+        product1(2, (2,))
+        product1(2, (3,))
+        activate(2, (2,))
+        activate(2, (3,))
+        product2(1, (0, 1), True)
+        interleave(2)
+        product2(1, (2, 3), True)
+        for n in range(4):
+            scatter(0, n)
         scatter(1, 0)
         scatter(1, 1)
         quantise(2)
+        for n in range(4):
+            product2(2, (n,))
         scatter(1, 2)
         scatter(1, 3)
-        for n, bank in enumerate((6, 7, 0, 1)):
-            stage2(2, (n,), bank)
         for n in range(4):
             scatter(2, n)
-            store(n)
+            nc.sync.dma_start(out=out[n * P : (n + 1) * P, :], in_=win[n][:])

@@ -68,7 +68,7 @@ def tile_list_msg_tanh_gate_kernel(
         win = {0: tile("win0", [P, T], F32)}
         nc.gpsimd.memset(tabs[0:96, :].bitcast(I32), 0)
         nc.gpsimd.memset(raw[0:112, :, :].rearrange("p a n -> p (a n)").bitcast(I32), 0)
-        nc.vector.memset(win[0][:].bitcast(I32), 0)
+        nc.gpsimd.memset(win[0][:].bitcast(I32), 0)
 
         nc.sync.dma_start(src_list[:], offs)
         nc.sync.dma_start(out=tabs[96:128, :].bitcast(I32), in_=tab_scales.rearrange("a q t -> (a q) t").bitcast(I32))

@@ -18,6 +18,7 @@ MULT = mybir.AluOpType.mult
 
 P = 128
 BANK = 512
+HALF = J // 2
 PIECES = ((0, 256), (256, 256), (512, 512))
 BANKS = {"sums": ((0, 1), (2, 3), (0, 1, 4, 5)), "yt": ((4, 5), (4, 5), (2, 3, 6, 7))}
 ROW = 4 * T
@@ -30,7 +31,7 @@ AT = {
     "gates0": GATES_AT, "gates1": GATES_AT + ROW, "wdw": GATES_AT + 2 * ROW,
     "gates2": GATES_AT + 2 * ROW + 2 * N, "gates3": GATES_AT + 3 * ROW + 2 * N,
     "win0": WINS_AT, "win1": WINS_AT + ROW, "win2": WINS_AT + 2 * ROW, "win3": WINS_AT + 3 * ROW,
-    "gw01": WINS_AT + ROW, "gw11": WINS_AT + ROW, "gw21": WINS_AT + ROW,
+    "gw01": WINS_AT + ROW, "gw11": WINS_AT + ROW,
     "hi0": WINS_AT + 2 * ROW, "hi1": WINS_AT + 3 * ROW,
     "hq0": REST_AT, "hq1": REST_AT,
     "hb2": REST_AT + 2048, "y12": REST_AT + 2048,
@@ -71,7 +72,7 @@ def tile_list_msg_tanh_gate_kernel(
         nc.gpsimd.memset(win[0][:].bitcast(I32), 0)
 
         nc.sync.dma_start(src_list[:], offs)
-        nc.sync.dma_start(out=tabs[96:128, :].bitcast(I32), in_=tab_scales.rearrange("a q t -> (a q) t").bitcast(I32))
+        nc.scalar.dma_start(out=tabs[96:128, :].bitcast(I32), in_=tab_scales.rearrange("a q t -> (a q) t").bitcast(I32))
         nc.sync.dma_start(dst_list[:], offs2)
         for first, rows, passes in ((0, ws_scales, 2), (2, wt_scales, 2), (4, wd_scales, 1)):
             nc.sync.dma_start(out=raw[112:128, first : first + passes, :].bitcast(I32), in_=rows.rearrange("a q n -> q a n").bitcast(I32))
@@ -115,7 +116,7 @@ def tile_list_msg_tanh_gate_kernel(
         nc.sync.dma_start(out=wdw[:].bitcast(I32), in_=wd_words[0].bitcast(I32))
 
         vw = {}
-        for i, (j0, count) in enumerate(PIECES):
+        for i, (j0, count) in enumerate(((0, HALF), (HALF, HALF))):
             words = [tile(f"gw{i}{l}", [P, count], I32, f"gw{l}") for l in range(2)]
             for l in range(2):
                 nc.vector.tensor_copy(words[l][:].bitcast(U32), tabw[:].bitcast(U32).indirect(entries(lists[l], j0, count)))
@@ -156,7 +157,7 @@ def tile_list_msg_tanh_gate_kernel(
                             out=acc,
                             lhsT=w,
                             lhsT_scale=planes[:, 2 * l * R + col : 2 * l * R + col + P],
-                            rhs=vw[i, l][:, a, :].bitcast(FP4X4),
+                            rhs=vw[j0 // HALF, l][:, a, 2 * (j0 % HALF) : 2 * (j0 % HALF + count)].bitcast(FP4X4),
                             rhs_scale=lifted[:, a, l * J + j0 : l * J + j0 + count],
                             start=(a == 0 and l == 0),
                             stop=(a == 1 and l == 1),

@@ -20,7 +20,7 @@ P = 128
 BANK = 512
 HALF = J // 2
 PIECES = ((0, 256), (256, 256), (512, 512))
-BANKS = {"sums": ((0, 1), (2, 3), (0, 1, 4, 5)), "yt": ((4, 5), (4, 5), (2, 3, 6, 7))}
+BANKS = {"sums": ((0, 1, 2, 3), (6, 7), (0, 4, 5, 4)), "yt": ((4, 5), (5, 4), (2, 3, 6, 7))}
 ROW = 4 * T
 GATES_AT = 4096
 WINS_AT = GATES_AT + 4 * ROW + 2 * N
@@ -28,12 +28,13 @@ REST_AT = WINS_AT + 4 * ROW
 AT = {
     "raw": 0, "lifted": 0,
     "wt_raw": GATES_AT + ROW - 64,
-    "gates0": GATES_AT, "gates1": GATES_AT + ROW, "wdw": GATES_AT + 2 * ROW,
+    "wgo_t": GATES_AT + ROW - 4 * J, "gates1": GATES_AT + ROW, "wdw": GATES_AT + 2 * ROW,
     "gates2": GATES_AT + 2 * ROW + 2 * N, "gates3": GATES_AT + 3 * ROW + 2 * N,
     "win0": WINS_AT, "win1": WINS_AT + ROW, "win2": WINS_AT + 2 * ROW, "win3": WINS_AT + 3 * ROW,
     "gw01": WINS_AT + ROW, "gw11": WINS_AT + ROW,
     "hi0": WINS_AT + 2 * ROW, "hi1": WINS_AT + 3 * ROW,
     "hq0": REST_AT, "hq1": REST_AT,
+    "hb0": REST_AT + 8192, "th10": REST_AT + 8192,
     "hb2": REST_AT + 2048, "y12": REST_AT + 2048,
 }
 
@@ -63,7 +64,7 @@ def tile_list_msg_tanh_gate_kernel(
         wt_raw = tile("wt_raw", [P, 2 * ROW + 2 * N + 128], U8)
         wsw = tile("wsw", [P, 4 * R], U8)
         wtw = tile("wtw", [P, 8 * R], U8)
-        wgo_t = tile("wgo_t", [P, J], F32)
+        gates = [tile(f"gates{n}", [P, T], F32) for n in range(4)]
         sm_t = tile("sm_t", [P, 4], F32)
 
         win = {0: tile("win0", [P, T], F32)}
@@ -79,7 +80,7 @@ def tile_list_msg_tanh_gate_kernel(
         nc.sync.dma_start(out=tabw[:], in_=tab_words[0].rearrange("p t b -> p (t b)").bitcast(I32))
         nc.sync.dma_start(out=ws_raw[:].bitcast(I32).rearrange("p (a n) -> p a n", a=2), in_=ws_words.rearrange("a p n -> p a n").bitcast(I32))
         nc.sync.dma_start(out=wt_raw[:, 0 : 8 * R].bitcast(I32).rearrange("p (a n) -> p a n", a=2), in_=wt_words.rearrange("a p n b -> p a (n b)").bitcast(I32))
-        nc.sync.dma_start(out=wgo_t[:], in_=wgo)
+        nc.sync.dma_start(out=gates[0][:], in_=gT[0:P, :])
         nc.sync.dma_start(out=sm_t[:], in_=sm.rearrange("(p t) -> p t", t=4))
 
         nc.gpsimd.tensor_copy(
@@ -109,8 +110,9 @@ def tile_list_msg_tanh_gate_kernel(
                 row = 96 + 16 * a + 4 * q
                 nc.sync.dma_start(out=lifted[32 * q : 32 * q + 4, a, :].bitcast(I32), in_=picked[row : row + 4, :].bitcast(I32))
 
-        gates = [tile(f"gates{n}", [P, T], F32) for n in range(4)]
-        for n in range(4):
+        wgo_t = tile("wgo_t", [P, J], F32)
+        nc.sync.dma_start(out=wgo_t[:], in_=wgo)
+        for n in range(1, 4):
             nc.sync.dma_start(out=gates[n][:], in_=gT[n * P : (n + 1) * P, :])
         wdw = tile("wdw", [P, 2 * N], U8)
         nc.sync.dma_start(out=wdw[:].bitcast(I32), in_=wd_words[0].bitcast(I32))
@@ -137,7 +139,8 @@ def tile_list_msg_tanh_gate_kernel(
 
         def place(tiles, name, i, t):
             count = PIECES[i][1]
-            b, first = divmod(t * count, BANK)
+            b, first = divmod(t, 4 // len(BANKS[name][i]))
+            first = first * count
             if first == 0:
                 tiles[i, b] = psum.tile([P, BANK], F32, name=name, tag=f"bank{BANKS[name][i][b]}")
             return tiles[i, b][:, first : first + count]
@@ -167,8 +170,8 @@ def tile_list_msg_tanh_gate_kernel(
             count = PIECES[i][1]
             if ts[0] == 0:
                 hb[i] = tile(f"hb{i}", [P, 4, count], BF16)
-            th = tile(f"th{i}{ts[0]}", [P, BANK], F32)
-            nc.scalar.activation(th[:], sums[i, ts[0] * count // BANK][:], ACT.Tanh)
+            th = tile(f"th{i}{ts[0]}", [P, len(ts) * count], F32)
+            nc.scalar.activation(th[:], sums[i, ts[0] // len(ts)][:, 0 : len(ts) * count], ACT.Tanh)
             for t in ts:
                 first = (t - ts[0]) * count
                 nc.scalar.activation(hb[i][:, t, :], th[:, first : first + count], ACT.Copy, scale=sm_t[:, t : t + 1])
@@ -216,14 +219,16 @@ def tile_list_msg_tanh_gate_kernel(
         clear_window(1)
         gather_gates(0)
         gather_gates(1)
-        for i in range(2):
-            product1(i, (0, 1, 2, 3))
-            activate(i, (0, 1))
-            activate(i, (2, 3))
-            interleave(i)
-        product1(2, (0, 1))
+        product1(0, (0, 1, 2, 3))
+        for t in range(4):
+            activate(0, (t,))
+        interleave(0)
+        product1(1, (0, 1, 2, 3))
+        activate(1, (0, 1))
+        activate(1, (2, 3))
+        interleave(1)
+        product1(2, (0,))
         activate(2, (0,))
-        activate(2, (1,))
         quantise(0)
         clear_window(2)
         product2(0, (0, 1))
@@ -232,10 +237,9 @@ def tile_list_msg_tanh_gate_kernel(
         gather_gates(3)
         quantise(1)
         clear_window(3)
-        product1(2, (2,))
-        product1(2, (3,))
-        activate(2, (2,))
-        activate(2, (3,))
+        for t in range(1, 4):
+            product1(2, (t,))
+            activate(2, (t,))
         product2(1, (0, 1), True)
         interleave(2)
         product2(1, (2, 3), True)

@@ -23,15 +23,16 @@ PIECES = ((0, 256), (256, 256), (512, 512))
 BANKS = {"sums": ((0, 1, 2, 3), (6, 7), (0, 4, 5, 4)), "yt": ((4, 5), (5, 4), (2, 3, 6, 7))}
 ROW = 4 * T
 GATES_AT = 4096
-WINS_AT = GATES_AT + 4 * ROW + 2 * N
+SMALL = 2 * N + 64
+WINS_AT = GATES_AT + 4 * ROW + SMALL
 REST_AT = WINS_AT + 4 * ROW
 AT = {
     "raw": 0, "lifted": 0,
     "wt_raw": GATES_AT + ROW - 64,
-    "wgo_t": GATES_AT + ROW - 4 * J, "gates1": GATES_AT + ROW, "wdw": GATES_AT + 2 * ROW,
-    "gates2": GATES_AT + 2 * ROW + 2 * N, "gates3": GATES_AT + 3 * ROW + 2 * N,
+    "gates0": GATES_AT, "gates1": GATES_AT + ROW, "wdw": GATES_AT + 2 * ROW, "sm_t": GATES_AT + 2 * ROW + 2 * N,
+    "gates2": GATES_AT + 2 * ROW + SMALL, "gates3": GATES_AT + 3 * ROW + SMALL,
     "win0": WINS_AT, "win1": WINS_AT + ROW, "win2": WINS_AT + 2 * ROW, "win3": WINS_AT + 3 * ROW,
-    "gw01": WINS_AT + ROW, "gw11": WINS_AT + ROW,
+    "gw11": WINS_AT + ROW,
     "hi0": WINS_AT + 2 * ROW, "hi1": WINS_AT + 3 * ROW,
     "hq0": REST_AT, "hq1": REST_AT,
     "hb0": REST_AT + 8192, "th10": REST_AT + 8192,
@@ -61,11 +62,10 @@ def tile_list_msg_tanh_gate_kernel(
         raw = tile("raw", [P, 5, R], U8)
         planes = tile("planes", [P, 5 * R], U8)
         ws_raw = tile("ws_raw", [P, 4 * R], U8)
-        wt_raw = tile("wt_raw", [P, 2 * ROW + 2 * N + 128], U8)
+        wt_raw = tile("wt_raw", [P, 2 * ROW + SMALL + 128], U8)
         wsw = tile("wsw", [P, 4 * R], U8)
         wtw = tile("wtw", [P, 8 * R], U8)
-        gates = [tile(f"gates{n}", [P, T], F32) for n in range(4)]
-        sm_t = tile("sm_t", [P, 4], F32)
+        wgo_t = tile("wgo_t", [P, J], F32)
 
         win = {0: tile("win0", [P, T], F32)}
         nc.gpsimd.memset(tabs[0:96, :].bitcast(I32), 0)
@@ -80,8 +80,7 @@ def tile_list_msg_tanh_gate_kernel(
         nc.sync.dma_start(out=tabw[:], in_=tab_words[0].rearrange("p t b -> p (t b)").bitcast(I32))
         nc.sync.dma_start(out=ws_raw[:].bitcast(I32).rearrange("p (a n) -> p a n", a=2), in_=ws_words.rearrange("a p n -> p a n").bitcast(I32))
         nc.sync.dma_start(out=wt_raw[:, 0 : 8 * R].bitcast(I32).rearrange("p (a n) -> p a n", a=2), in_=wt_words.rearrange("a p n b -> p a (n b)").bitcast(I32))
-        nc.sync.dma_start(out=gates[0][:], in_=gT[0:P, :])
-        nc.sync.dma_start(out=sm_t[:], in_=sm.rearrange("(p t) -> p t", t=4))
+        nc.sync.dma_start(out=wgo_t[:], in_=wgo)
 
         nc.gpsimd.tensor_copy(
             planes[:, 0 : 4 * R].rearrange("p (a t m) -> p a t m", a=4, t=4), raw[:, 0:4, :].rearrange("p a (m t) -> p a t m", t=4)
@@ -110,23 +109,35 @@ def tile_list_msg_tanh_gate_kernel(
                 row = 96 + 16 * a + 4 * q
                 nc.sync.dma_start(out=lifted[32 * q : 32 * q + 4, a, :].bitcast(I32), in_=picked[row : row + 4, :].bitcast(I32))
 
-        wgo_t = tile("wgo_t", [P, J], F32)
-        nc.sync.dma_start(out=wgo_t[:], in_=wgo)
-        for n in range(1, 4):
+        gates = [tile(f"gates{n}", [P, T], F32) for n in range(4)]
+        for n in range(4):
             nc.sync.dma_start(out=gates[n][:], in_=gT[n * P : (n + 1) * P, :])
+            if n == 0:
+                sm_t = tile("sm_t", [P, 4], F32)
+                nc.sync.dma_start(out=sm_t[:], in_=sm.rearrange("(p t) -> p t", t=4))
         wdw = tile("wdw", [P, 2 * N], U8)
         nc.sync.dma_start(out=wdw[:].bitcast(I32), in_=wd_words[0].bitcast(I32))
 
-        vw = {}
-        for i, (j0, count) in enumerate(((0, HALF), (HALF, HALF))):
-            words = [tile(f"gw{i}{l}", [P, count], I32, f"gw{l}") for l in range(2)]
-            for l in range(2):
-                nc.vector.tensor_copy(words[l][:].bitcast(U32), tabw[:].bitcast(U32).indirect(entries(lists[l], j0, count)))
-            for l in range(2):
-                vw[i, l] = tile(f"vw{i}{l}", [P, 2, 2 * count], U8)
-                nc.vector.tensor_copy(vw[i, l][:].bitcast(U16), words[l][:].bitcast(U16).rearrange("p (j a) -> p a j", a=2))
+        words, vw = {}, {}
 
-        gg, sums, hb, hi, hq, yt, y = {}, {}, {}, {}, {}, {}, {}
+        def gather_words(h, l):
+            words[h, l] = tile(f"gw{h}{l}", [P, HALF], I32)
+            nc.vector.tensor_copy(words[h, l][:].bitcast(U32), tabw[:].bitcast(U32).indirect(entries(lists[l], h * HALF, HALF)))
+
+        def part_words(h, l):
+            vw[h, l] = tile(f"vw{h}{l}", [P, 2, 2 * HALF], U8)
+            nc.vector.tensor_copy(vw[h, l][:].bitcast(U16), words[h, l][:].bitcast(U16).rearrange("p (j a) -> p a j", a=2))
+
+        gather_words(0, 0)
+        gather_words(0, 1)
+        part_words(0, 0)
+        gather_words(1, 0)
+        gather_words(1, 1)
+        part_words(0, 1)
+        part_words(1, 0)
+        part_words(1, 1)
+
+        gg, sums, acc, hb, hi, hq, yt, y = {}, {}, {}, {}, {}, {}, {}, {}
         hs = tile("hs", [P, J], U8)
 
         def clear_window(n):
@@ -145,11 +156,12 @@ def tile_list_msg_tanh_gate_kernel(
                 tiles[i, b] = psum.tile([P, BANK], F32, name=name, tag=f"bank{BANKS[name][i][b]}")
             return tiles[i, b][:, first : first + count]
 
-        def product1(i, ts):
+        def product1(i, ts, ls=(0, 1)):
             j0, count = PIECES[i]
             for t in ts:
-                acc = place(sums, "sums", i, t)
-                for l in range(2):
+                if ls[0] == 0:
+                    acc[i, t] = place(sums, "sums", i, t)
+                for l in ls:
                     for a in range(2):
                         col = a * R + t * P
                         if l == 0:
@@ -157,7 +169,7 @@ def tile_list_msg_tanh_gate_kernel(
                         else:
                             w = wtw[:, 4 * col : 4 * (col + P)].bitcast(FP8X4)
                         nc.tensor.matmul_mx(
-                            out=acc,
+                            out=acc[i, t],
                             lhsT=w,
                             lhsT_scale=planes[:, 2 * l * R + col : 2 * l * R + col + P],
                             rhs=vw[j0 // HALF, l][:, a, 2 * (j0 % HALF) : 2 * (j0 % HALF + count)].bitcast(FP4X4),
@@ -219,7 +231,8 @@ def tile_list_msg_tanh_gate_kernel(
         clear_window(1)
         gather_gates(0)
         gather_gates(1)
-        product1(0, (0, 1, 2, 3))
+        for l in range(2):
+            product1(0, (0, 1, 2, 3), (l,))
         for t in range(4):
             activate(0, (t,))
         interleave(0)

from contextlib import ExitStack

import concourse.mybir as mybir

K, R, N, T, J = 1024, 512, 512, 2048, 1024
FLOPS = 2 * J * (2 * K * R + R * N)

F32 = mybir.dt.float32
BF16 = mybir.dt.bfloat16
I32 = mybir.dt.int32
U32 = mybir.dt.uint32
U16 = mybir.dt.uint16
U8 = mybir.dt.uint8
FP8X4 = mybir.dt.float8_e4m3fn_x4
FP4X4 = mybir.dt.float4_e2m1fn_x4
ACT = mybir.ActivationFunctionType
MULT = mybir.AluOpType.mult

P = 128
BANK = 512
HALF = J // 2
PIECES = ((0, 256), (256, 256), (512, 512))
BANKS = {"sums": ((0, 1, 2, 3), (6, 7), (0, 4, 5, 4)), "yt": ((4, 5), (5, 4), (2, 3, 6, 7))}
ROW = 4 * T
GATES_AT = 4096
SMALL = 2 * N + 64
WINS_AT = GATES_AT + 4 * ROW + SMALL
REST_AT = WINS_AT + 4 * ROW
AT = {
    "raw": 0, "lifted": 0,
    "wt_raw": GATES_AT + ROW - 64,
    "gates0": GATES_AT, "gates1": GATES_AT + ROW, "wdw": GATES_AT + 2 * ROW, "sm_t": GATES_AT + 2 * ROW + 2 * N,
    "gates2": GATES_AT + 2 * ROW + SMALL, "gates3": GATES_AT + 3 * ROW + SMALL,
    "win0": WINS_AT, "win1": WINS_AT + ROW, "win2": WINS_AT + 2 * ROW, "win3": WINS_AT + 3 * ROW,
    "gw11": WINS_AT + ROW,
    "hi0": WINS_AT + 2 * ROW, "hi1": WINS_AT + 3 * ROW,
    "hq0": REST_AT, "hq1": REST_AT,
    "hb0": REST_AT + 8192, "th10": REST_AT + 8192,
    "hb2": REST_AT + 2048, "y12": REST_AT + 2048,
}


def tile_list_msg_tanh_gate_kernel(
    tc, tab_words, tab_scales, ws_words, ws_scales, wt_words, wt_scales, sm, wd_words, wd_scales, gT, wgo, offs, offs2, out
):
    nc = tc.nc
    with ExitStack() as ctx:
        keep = ctx.enter_context(tc.tile_pool(name="keep", bufs=1))
        lay = ctx.enter_context(tc.tile_pool(name="lay", bufs=1))
        psum = ctx.enter_context(tc.psum_pool(name="psum", bufs=1))

        def tile(name, shape, dtype, tag=None):
            if name in AT:
                return lay.tile(shape, dtype, name=name, align_bytes=64, offset=AT[name])
            return keep.tile(shape, dtype, name=name, tag=tag or name, align_bytes=64)

        src_list = keep.tile([P, J // 16], U16, name="src_list")
        dst_list = keep.tile([P, J // 16], U16, name="dst_list")
        lists = (src_list, dst_list)
        tabw = tile("tabw", [P, T], I32)
        tabs = tile("tabs", [P, T], U8)
        raw = tile("raw", [P, 5, R], U8)
        planes = tile("planes", [P, 5 * R], U8)
        ws_raw = tile("ws_raw", [P, 4 * R], U8)
        wt_raw = tile("wt_raw", [P, 2 * ROW + SMALL + 128], U8)
        wsw = tile("wsw", [P, 4 * R], U8)
        wtw = tile("wtw", [P, 8 * R], U8)
        wgo_t = tile("wgo_t", [P, J], F32)

        win = {0: tile("win0", [P, T], F32)}
        nc.gpsimd.memset(tabs[0:96, :].bitcast(I32), 0)
        nc.gpsimd.memset(raw[0:112, :, :].rearrange("p a n -> p (a n)").bitcast(I32), 0)
        nc.gpsimd.memset(win[0][:].bitcast(I32), 0)

        nc.sync.dma_start(src_list[:], offs)
        nc.scalar.dma_start(out=tabs[96:128, :].bitcast(I32), in_=tab_scales.rearrange("a q t -> (a q) t").bitcast(I32))
        nc.sync.dma_start(dst_list[:], offs2)
        for first, rows, passes in ((0, ws_scales, 2), (2, wt_scales, 2), (4, wd_scales, 1)):
            nc.sync.dma_start(out=raw[112:128, first : first + passes, :].bitcast(I32), in_=rows.rearrange("a q n -> q a n").bitcast(I32))
        nc.sync.dma_start(out=tabw[:], in_=tab_words[0].rearrange("p t b -> p (t b)").bitcast(I32))
        nc.sync.dma_start(out=ws_raw[:].bitcast(I32).rearrange("p (a n) -> p a n", a=2), in_=ws_words.rearrange("a p n -> p a n").bitcast(I32))
        nc.sync.dma_start(out=wt_raw[:, 0 : 8 * R].bitcast(I32).rearrange("p (a n) -> p a n", a=2), in_=wt_words.rearrange("a p n b -> p a (n b)").bitcast(I32))
        nc.sync.dma_start(out=wgo_t[:], in_=wgo)

        nc.gpsimd.tensor_copy(
            planes[:, 0 : 4 * R].rearrange("p (a t m) -> p a t m", a=4, t=4), raw[:, 0:4, :].rearrange("p a (m t) -> p a t m", t=4)
        )
        nc.gpsimd.tensor_copy(planes[:, 4 * R : 5 * R].bitcast(I32), raw[:, 4, :].bitcast(I32))
        for q in range(4):
            nc.sync.dma_start(out=planes[32 * q : 32 * q + 4, :].bitcast(I32), in_=planes[112 + 4 * q : 116 + 4 * q, :].bitcast(I32))
        lifted = tile("lifted", [P, 2, 2 * J], U8)
        nc.gpsimd.memset(lifted[:].rearrange("p a n -> p (a n)").bitcast(I32), 0)

        nc.scalar.copy(
            wsw[:].bitcast(U16).rearrange("p (a t m) -> p a t m", a=2, t=4), ws_raw[:].bitcast(U16).rearrange("p (a m t) -> p a t m", a=2, t=4)
        )
        nc.scalar.copy(
            wtw[:].bitcast(U32).rearrange("p (a t m) -> p a t m", a=2, t=4), wt_raw[:, 0 : 8 * R].bitcast(U32).rearrange("p (a m t) -> p a t m", a=2, t=4)
        )

        def entries(lst, j0, count):
            return lst[:, j0 // 16 : (j0 + count) // 16]

        picked = tile("picked", [P, 2 * J], U8)
        for l in range(2):
            nc.vector.tensor_copy(picked[:, l * J : (l + 1) * J], tabs[:].indirect(lists[l][:]))
        for q in range(4):
            for a in range(2):
                row = 96 + 16 * a + 4 * q
                nc.sync.dma_start(out=lifted[32 * q : 32 * q + 4, a, :].bitcast(I32), in_=picked[row : row + 4, :].bitcast(I32))

        gates = [tile(f"gates{n}", [P, T], F32) for n in range(4)]
        for n in range(4):
            nc.sync.dma_start(out=gates[n][:], in_=gT[n * P : (n + 1) * P, :])
            if n == 0:
                sm_t = tile("sm_t", [P, 4], F32)
                nc.sync.dma_start(out=sm_t[:], in_=sm.rearrange("(p t) -> p t", t=4))
        wdw = tile("wdw", [P, 2 * N], U8)
        nc.sync.dma_start(out=wdw[:].bitcast(I32), in_=wd_words[0].bitcast(I32))

        words, vw = {}, {}

        def gather_words(h, l):
            words[h, l] = tile(f"gw{h}{l}", [P, HALF], I32)
            nc.vector.tensor_copy(words[h, l][:].bitcast(U32), tabw[:].bitcast(U32).indirect(entries(lists[l], h * HALF, HALF)))

        def part_words(h, l):
            vw[h, l] = tile(f"vw{h}{l}", [P, 2, 2 * HALF], U8)
            nc.vector.tensor_copy(vw[h, l][:].bitcast(U16), words[h, l][:].bitcast(U16).rearrange("p (j a) -> p a j", a=2))

        gather_words(0, 0)
        gather_words(0, 1)
        part_words(0, 0)
        gather_words(1, 0)
        gather_words(1, 1)
        part_words(0, 1)
        part_words(1, 0)
        part_words(1, 1)

        gg, sums, acc, hb, hi, hq, yt, y = {}, {}, {}, {}, {}, {}, {}, {}
        hs = tile("hs", [P, J], U8)

        def clear_window(n):
            win[n] = tile(f"win{n}", [P, T], F32)
            nc.gpsimd.memset(win[n][:].bitcast(I32), 0)

        def gather_gates(n):
            gg[n] = tile(f"gg{n}", [P, J], F32)
            nc.vector.tensor_tensor(gg[n][:], gates[n][:].indirect(src_list[:]), wgo_t[:], MULT)

        def place(tiles, name, i, t):
            count = PIECES[i][1]
            b, first = divmod(t, 4 // len(BANKS[name][i]))
            first = first * count
            if first == 0:
                tiles[i, b] = psum.tile([P, BANK], F32, name=name, tag=f"bank{BANKS[name][i][b]}")
            return tiles[i, b][:, first : first + count]

        def product1(i, ts, ls=(0, 1)):
            j0, count = PIECES[i]
            for t in ts:
                if ls[0] == 0:
                    acc[i, t] = place(sums, "sums", i, t)
                for l in ls:
                    for a in range(2):
                        col = a * R + t * P
                        if l == 0:
                            w = wsw[:, 2 * col : 2 * (col + P)].bitcast(FP4X4)
                        else:
                            w = wtw[:, 4 * col : 4 * (col + P)].bitcast(FP8X4)
                        nc.tensor.matmul_mx(
                            out=acc[i, t],
                            lhsT=w,
                            lhsT_scale=planes[:, 2 * l * R + col : 2 * l * R + col + P],
                            rhs=vw[j0 // HALF, l][:, a, 2 * (j0 % HALF) : 2 * (j0 % HALF + count)].bitcast(FP4X4),
                            rhs_scale=lifted[:, a, l * J + j0 : l * J + j0 + count],
                            start=(a == 0 and l == 0),
                            stop=(a == 1 and l == 1),
                        )

        def activate(i, ts):
            count = PIECES[i][1]
            if ts[0] == 0:
                hb[i] = tile(f"hb{i}", [P, 4, count], BF16)
            th = tile(f"th{i}{ts[0]}", [P, len(ts) * count], F32)
            nc.scalar.activation(th[:], sums[i, ts[0] // len(ts)][:, 0 : len(ts) * count], ACT.Tanh)
            for t in ts:
                first = (t - ts[0]) * count
                nc.scalar.activation(hb[i][:, t, :], th[:, first : first + count], ACT.Copy, scale=sm_t[:, t : t + 1])

        def interleave(i):
            count = PIECES[i][1]
            hi[i] = tile(f"hi{i}", [P, 4 * count], BF16)
            nc.scalar.copy(
                hi[i][:].rearrange("p (c i t) -> p c t i", i=4, t=4), hb[i][:].rearrange("p t (c i) -> p c t i", i=4)
            )

        def quantise(i):
            j0, count = PIECES[i]
            hq[i] = tile(f"hq{i}", [P, count], U32)
            nc.vector.quantize_mx(out=hq[i][:].bitcast(FP8X4), scales=hs[:, j0 : j0 + count], in_=hi[i][:])

        def product2(i, blocks, joint=False):
            j0, count = PIECES[i]
            made = {}
            for n in blocks:
                made[n] = place(yt, "yt", i, n)
                nc.tensor.matmul_mx(
                    out=made[n],
                    lhsT=wdw[:, 2 * n * P : 2 * (n + 1) * P].bitcast(FP4X4),
                    lhsT_scale=planes[:, 4 * R + n * P : 4 * R + (n + 1) * P],
                    rhs=hq[i][:].bitcast(FP8X4),
                    rhs_scale=hs[:, j0 : j0 + count],
                    start=True,
                    stop=True,
                )
            if joint:
                both = tile(f"y{i}{blocks[0]}", [P, BANK], F32)
                nc.scalar.copy(both[:], yt[i, blocks[0] * count // BANK][:])
            for b, n in enumerate(blocks):
                if joint:
                    y[i, n] = both[:, b * count : (b + 1) * count]
                else:
                    y[i, n] = tile(f"y{i}{n}", [P, count], F32)[:, :]
                    nc.scalar.copy(y[i, n], made[n])

        def scatter(i, n):
            j0, count = PIECES[i]
            nc.vector.tensor_tensor(win[n][:].indirect(entries(dst_list, j0, count)), y[i, n], gg[n][:, j0 : j0 + count], MULT)

        clear_window(1)
        gather_gates(0)
        gather_gates(1)
        for l in range(2):
            product1(0, (0, 1, 2, 3), (l,))
        for t in range(4):
            activate(0, (t,))
        interleave(0)
        product1(1, (0, 1, 2, 3))
        activate(1, (0, 1))
        activate(1, (2, 3))
        interleave(1)
        product1(2, (0,))
        activate(2, (0,))
        quantise(0)
        clear_window(2)
        product2(0, (0, 1))
        product2(0, (2, 3), True)
        gather_gates(2)
        gather_gates(3)
        quantise(1)
        clear_window(3)
        for t in range(1, 4):
            product1(2, (t,))
            activate(2, (t,))
        product2(1, (0, 1), True)
        interleave(2)
        product2(1, (2, 3), True)
        for n in range(4):
            scatter(0, n)
        scatter(1, 0)
        scatter(1, 1)
        quantise(2)
        for n in range(4):
            product2(2, (n,))
        scatter(1, 2)
        scatter(1, 3)
        for n in range(4):
            scatter(2, n)
            nc.sync.dma_start(out=out[n * P : (n + 1) * P, :], in_=win[n][:])
